import numpy as np
import ml_dtypes


def mxq(x, axis, fmt="e4m3"):
    dtype, down = {"e4m3": (ml_dtypes.float8_e4m3fn, 7), "e5m2": (ml_dtypes.float8_e5m2, 14)}[fmt]
    v = np.moveaxis(np.asarray(x, np.float32).astype(ml_dtypes.bfloat16).astype(np.float64), axis, -1)
    blocks = v.reshape(v.shape[:-1] + (-1, 32))
    amax = np.abs(blocks).max(-1, keepdims=True)
    byte = np.maximum(np.where(amax > 0, np.frexp(amax)[1] - 1 + 127, 0) - down, 1)
    scale = np.exp2(byte - 127.0)
    codes = (blocks / scale).astype(np.float32).astype(dtype).astype(np.float64)
    return np.moveaxis((codes * scale).reshape(v.shape), -1, axis)


WIDE = False


def mx_kscale(k):
    if not WIDE:
        return np.ones(k)
    levels = np.array([10, -10, 5, -5, 0])
    if k % 512:
        return np.exp2(np.random.permutation(np.resize(levels, k // 32))).repeat(32)
    a = np.empty((k // 512, 16))
    for p in range(k // 512):
        a[p, :8] = np.random.permutation(np.resize(levels, 8))
        for g in range(8):
            far = levels[np.abs(levels - a[p, g]) >= 10]
            a[p, g + 8] = far[np.random.randint(len(far))]
    return np.exp2(a.ravel()).repeat(32)


def f64(x):
    return np.asarray(x).astype(np.float64)


def striped(idx):
    return np.tile(idx.reshape(-1, 16).T, (8, 1)).astype(np.uint16)


def unstriped(offs):
    return offs[:16].T.reshape(-1).astype(np.int64)


E2M1 = np.array([0.0, 0.5, 1.0, 1.5, 2.0, 3.0, 4.0, 6.0, -0.0, -0.5, -1.0, -1.5, -2.0, -3.0, -4.0, -6.0])


def pack_weight(w, fmt):
    k, n = w.shape
    w = f64(np.asarray(w, np.float32).astype(ml_dtypes.bfloat16)).reshape(k // 32, 32, n)
    amax = np.abs(w).max(1)
    if fmt == "e4m3":
        byte = np.frexp(amax)[1] - 1 + 127 - 7
    else:
        mant, ex = np.frexp(amax / 6.0)
        byte = np.where(mant > 0.5, ex, ex - 1) + 127
    byte = np.clip(np.where(amax > 0, byte, 1), 1, 254)
    scaled = (w * np.exp2(127.0 - byte)[:, None, :]).reshape(k, n).astype(np.float32)
    by_word = np.ascontiguousarray(scaled.reshape(k // 512, 128, 4, n).transpose(0, 1, 3, 2))
    if fmt == "e4m3":
        words = by_word.astype(ml_dtypes.float8_e4m3fn).view(np.uint8)
    else:
        c = by_word.astype(ml_dtypes.float4_e2m1fn).view(np.uint8) & 0xF
        words = (c[..., 0::2] | (c[..., 1::2] << 4)).reshape(k // 512, 128, 2 * n)
    return np.ascontiguousarray(words), np.ascontiguousarray(byte.astype(np.uint8).reshape(k // 512, 16, n))


def unpack_weight(words, scales, fmt):
    g, _, n = scales.shape
    words = np.ascontiguousarray(words).reshape(g, 128, n, -1)
    if fmt == "e4m3":
        vals = words.view(ml_dtypes.float8_e4m3fn).astype(np.float64)
    else:
        nib = np.empty((g, 128, n, 4), np.uint8)
        nib[..., 0::2] = words & 0xF
        nib[..., 1::2] = words >> 4
        vals = E2M1[nib]
    vals = vals * np.repeat(np.exp2(scales.astype(np.float64) - 127.0), 8, axis=1)[..., None]
    return vals.transpose(0, 1, 3, 2).reshape(g * 512, n)


def gelu(v):
    return 0.5 * v * (1.0 + np.tanh(np.sqrt(2.0 / np.pi) * (v + 0.044715 * v**3)))


def bf(x):
    return np.asarray(x, np.float32).astype(ml_dtypes.bfloat16)

def planes(Y):
    n, m = Y.shape
    b = f64(bf(Y)).reshape(n // 32, 32, m)
    amax = np.abs(b).max(1)
    byte = np.clip(np.where(amax > 0, np.frexp(amax)[1] - 1 + 127 - 7, 1), 1, 254)
    codes = (b * np.exp2(127.0 - byte)[:, None, :]).reshape(n, m).astype(np.float32).astype(ml_dtypes.float8_e4m3fn).view(np.uint8)
    words = codes.reshape(n // 512, 128, 4, m).transpose(0, 1, 3, 2)
    return np.ascontiguousarray(words), np.ascontiguousarray(byte.astype(np.uint8).reshape(n // 512, 16, m))


K, H, N, T, S, T2 = 1024, 1024, 512, 2048, 1024, 2048

def setup_inputs():
    n = np.random.standard_normal
    s, u = mx_kscale(K)[:, None], mx_kscale(H)[:, None]
    tab_words, tab_scales = pack_weight(n((K, T)) * np.exp(0.4 * n(T)) * s, "e4m3")
    w1 = n((K, H)) / np.sqrt(K) / s
    gain = np.exp(0.3 * n(H)) * u[:, 0]
    wp_words, wp_scales = pack_weight(np.exp(0.8 * n((H, N))) / (1.4 * H) / u, "e2m1")
    wd = n((H, N)) * np.exp(0.8 * n(N)) / np.sqrt(H) / u
    return {"tab_words": tab_words, "tab_scales": tab_scales,
            "offs": striped(np.random.permutation(T)[:S]),
            "w1": w1.astype(np.float32), "gain": gain.astype(np.float32),
            "wp_words": wp_words, "wp_scales": wp_scales,
            "wd": wd.astype(np.float32),
            "wgo": np.exp(0.3 * n((128, S))).astype(np.float32),
            "offs2": striped(np.random.permutation(T2)[:S])}

def reference(tab_words, tab_scales, offs, w1, gain, wp_words, wp_scales, wd, wgo, offs2):
    v = unpack_weight(tab_words, tab_scales, "e4m3")[:, unstriped(offs)]
    lin = mxq(f64(w1), 0, "e4m3").T @ v
    e = np.square(lin) * f64(gain)[:, None]
    eq = mxq(e, 0, "e4m3")
    pool = unpack_weight(wp_words, wp_scales, "e2m1").T @ eq
    drive = mxq(f64(wd), 0, "e4m3").T @ eq
    y = drive / (1.0 + pool)
    page = np.zeros((N, T2))
    page[:, unstriped(offs2)] = np.tile(f64(wgo), (N // 128, 1)) * y
    y = page
    words, scales = planes(y)
    return y, words, scales

@@ -1,0 +1,339 @@
+from contextlib import ExitStack
+
+import concourse.mybir as mybir
+
+K, H, N, T, S, T2 = 1024, 1024, 512, 2048, 1024, 2048
+FLOPS = 2 * K * H * S + 2 * 2 * H * N * S
+
+F32 = mybir.dt.float32
+BF16 = mybir.dt.bfloat16
+I32 = mybir.dt.int32
+U32 = mybir.dt.uint32
+U16 = mybir.dt.uint16
+U8 = mybir.dt.uint8
+FP8X4 = mybir.dt.float8_e4m3fn_x4
+FP4X4 = mybir.dt.float4_e2m1fn_x4
+ACT = mybir.ActivationFunctionType
+ALU = mybir.AluOpType
+
+P = 128
+W = 512
+C = 512
+NC = T2 // C
+
+
+def tile_list_contrast_gain_control_kernel(
+    tc, tab_words, tab_scales, offs, w1, gain, wp_words, wp_scales, wd, wgo, offs2, out_0, out_1, out_2
+):
+    nc = tc.nc
+    with ExitStack() as ctx:
+        keep = ctx.enter_context(tc.tile_pool(name="keep", bufs=1))
+        ring = ctx.enter_context(tc.tile_pool(name="ring", bufs=2))
+        psum = ctx.enter_context(tc.psum_pool(name="psum", bufs=2))
+
+        idx = keep.tile([P, S // 16], U16, name="idx")
+        idx2 = keep.tile([P, S // 16], U16, name="idx2")
+        tabs = keep.tile([P, T], U8, name="tabs", align_bytes=64)
+        wps_raw = keep.tile([P, 2, N], U8, name="wps_raw", align_bytes=64)
+        wpw_raw = keep.tile([P, 2, 2 * N], U8, name="wpw_raw", tag="rawB", align_bytes=64)
+        g_sb = keep.tile([P, 2, 4], F32, name="g_sb", tag="page2")
+        half = keep.tile([P, 2, 4], F32, name="half", tag="page3")
+        sg = keep.tile([P, 2, 4], F32, name="sg")
+        warm = keep.tile([P, 2], F32, name="warm")
+        one = keep.tile([P, 1], F32, name="one", tag="tab0", align_bytes=64)
+        wpw = keep.tile([P, 2, 2 * N], U8, name="wpw", align_bytes=64)
+        wps = keep.tile([P, 2, N], U8, name="wps", align_bytes=64)
+        yscales = keep.tile([P, T2], U8, name="yscales", align_bytes=64)
+        pages = {}
+        tabw = {}
+        raws = {}
+        grouped = {}
+        wq = {}
+        gw = {}
+        gs = {}
+        est = {}
+        eil = {}
+        eq = {}
+        rec = {}
+        ys = {}
+        wg = {}
+        yil = {}
+        wgq = wgo.rearrange("(q t) j -> q t j", t=4)
+        out_rows = out_0.rearrange("(p t) m -> p t m", t=4)
+        words_out = out_1[0].rearrange("p m t -> p (m t)").bitcast(I32)
+
+        def copy_on(eng, o, i):
+            if eng == "v":
+                nc.vector.tensor_copy(out=o, in_=i)
+            else:
+                nc.scalar.copy(out=o, in_=i)
+
+        def clear_page(t, eng):
+            pages[t] = keep.tile([P, T2], F32, name=f"page{t}", tag=f"page{t}")
+            if eng == "v":
+                nc.vector.memset(pages[t][:].bitcast(I32), 0)
+            else:
+                for c in range(4):
+                    nc.gpsimd.memset(pages[t][:, c * W : (c + 1) * W].bitcast(I32), 0)
+
+        def load_w(key, src, a, h, tag):
+            raw = keep.tile([P, 4, W], F32, name="raw_" + key, tag=tag, align_bytes=64)
+            nc.sync.dma_start(
+                out=raw[:], in_=src[a * W : (a + 1) * W, h * W : (h + 1) * W].rearrange("(p i) c -> p i c", i=4)
+            )
+            raws[key] = raw
+
+        def load_tab(a, tag):
+            tabw[a] = keep.tile([P, T], I32, name=f"tabw{a}", tag=tag, align_bytes=64)
+            nc.sync.dma_start(out=tabw[a][:], in_=tab_words[a].rearrange("p n t -> p (n t)").bitcast(I32))
+
+        def load_tabs():
+            for q in range(4):
+                nc.sync.dma_start(
+                    out=tabs[32 * q : 32 * q + 8, :].bitcast(I32),
+                    in_=tab_scales[:, 4 * q : 4 * q + 4, :].bitcast(I32),
+                )
+
+        def load_wps():
+            for q in range(4):
+                nc.sync.dma_start(
+                    out=wps_raw[32 * q : 32 * q + 4, :, :].bitcast(I32),
+                    in_=wp_scales[:, 4 * q : 4 * q + 4, :].rearrange("a r c -> r a c").bitcast(I32),
+                )
+
+        def load_wg(t0, t1, tag):
+            tile = keep.tile([P, t1 - t0, S], F32, name=f"wg{t0}", tag=tag, align_bytes=64)
+            for q in range(4):
+                nc.sync.dma_start(out=tile[32 * q : 32 * q + 32, :, :], in_=wgq[:, t0:t1, :])
+            for t in range(t0, t1):
+                wg[t] = (tile, t - t0)
+
+        def cast_w(key, eng, tag):
+            g = keep.tile([P, 4 * W], BF16, name="grp_" + key, tag=tag, align_bytes=64)
+            copy_on(
+                eng,
+                g[:].rearrange("p (t m i) -> p m t i", t=4, i=4),
+                raws[key][:].rearrange("p i (m t) -> p m t i", t=4),
+            )
+            grouped[key] = g
+
+        def quant(name, src):
+            codes = keep.tile([P, W], U32, name=name + "_c", align_bytes=64)
+            scales = keep.tile([P, W], U8, name=name + "_s", align_bytes=64)
+            nc.vector.quantize_mx(out=codes[:].bitcast(FP8X4), scales=scales[:], in_=src)
+            return codes, scales
+
+        def quant_w(key):
+            wq[key] = quant("q_" + key, grouped[key][:])
+
+        def gather_w(a, j):
+            g = keep.tile([P, W], U32, name=f"gw{a}{j}", align_bytes=64)
+            nc.vector.tensor_copy(g[:], tabw[a][:].bitcast(U32).indirect(idx[:, 32 * j : 32 * j + 32]))
+            gw[(a, j)] = g
+
+        def gather_s(j):
+            g = keep.tile([P, W], U8, name=f"gs{j}", align_bytes=64)
+            nc.vector.tensor_copy(g[:], tabs[:].indirect(idx[:, 32 * j : 32 * j + 32]))
+            gs[j] = g
+
+        def lin(h, j, tag):
+            st = keep.tile([P, 4, W], BF16, name=f"est{h}{j}", tag=tag, align_bytes=64)
+            for t in range(4):
+                acc = psum.tile([P, W], F32, name="lin", tag="lin", bufs=4)
+                for a in range(2):
+                    c, s = wq[f"w{a}{h}"]
+                    nc.tensor.matmul_mx(
+                        out=acc[:],
+                        lhsT=c[:, t * P : (t + 1) * P].bitcast(FP8X4),
+                        lhsT_scale=s[:, t * P : (t + 1) * P],
+                        rhs=gw[(a, j)][:].bitcast(FP8X4),
+                        rhs_scale=gs[j][4 * a : P, :],
+                        start=(a == 0),
+                        stop=(a == 1),
+                    )
+                nc.scalar.activation(st[:, t, :], acc[:], ACT.Square, scale=sg[:, h, t : t + 1])
+            est[(h, j)] = st
+
+        def weave_e(h, j, eng, tag):
+            il = keep.tile([P, 4 * W], BF16, name=f"eil{h}{j}", tag=tag, align_bytes=64)
+            copy_on(
+                eng,
+                il[:].rearrange("p (c i t) -> p c t i", i=4, t=4),
+                est[(h, j)][:].rearrange("p t (c i) -> p c t i", i=4),
+            )
+            eil[(h, j)] = il
+
+        def quant_e(h, j):
+            eq[(h, j)] = quant(f"q_e{h}{j}", eil[(h, j)][:])
+
+        def deal_wpw():
+            for a in range(2):
+                nc.vector.tensor_copy(
+                    out=wpw[:, a, :].rearrange("p (t m b) -> p m t b", t=4, b=2),
+                    in_=wpw_raw[:, a, :].rearrange("p (m t b) -> p m t b", t=4, b=2),
+                )
+
+        def deal_wps():
+            nc.vector.tensor_copy(
+                out=wps[:].rearrange("p a (t m) -> p a m t", t=4),
+                in_=wps_raw[:].rearrange("p a (m t) -> p a m t", t=4),
+            )
+
+        def pool_part(t, j, tag):
+            acc = psum.tile([P, W], F32, name="pool", tag="pool", bufs=2)
+            for h in range(2):
+                c, s = eq[(h, j)]
+                nc.tensor.matmul_mx(
+                    out=acc[:],
+                    lhsT=wpw[:, h, 2 * t * P : 2 * (t + 1) * P].bitcast(FP4X4),
+                    lhsT_scale=wps[:, h, t * P : (t + 1) * P],
+                    rhs=c[:].bitcast(FP8X4),
+                    rhs_scale=s[:],
+                    start=(h == 0),
+                    stop=(h == 1),
+                )
+            r = keep.tile([P, W], F32, name=f"r{t}{j}", tag=tag, align_bytes=64)
+            nc.scalar.activation(r[:], acc[:], ACT.Abs_reciprocal_sqrt, bias=1.0)
+            r2 = ring.tile([P, W], F32, name=f"rr{t}{j}", tag="r2", bufs=6)
+            nc.scalar.activation(r2[:], r[:], ACT.Square)
+            rec[(t, j)] = r2
+
+        def drive_part(t, j):
+            acc = psum.tile([P, W], F32, name="drive", tag="drive", bufs=2)
+            for h in range(2):
+                c, s = eq[(h, j)]
+                wc, ws = wq[f"d{h}"]
+                nc.tensor.matmul_mx(
+                    out=acc[:],
+                    lhsT=wc[:, t * P : (t + 1) * P].bitcast(FP8X4),
+                    lhsT_scale=ws[:, t * P : (t + 1) * P],
+                    rhs=c[:].bitcast(FP8X4),
+                    rhs_scale=s[:],
+                    start=(h == 0),
+                    stop=(h == 1),
+                )
+            y = ring.tile([P, W], F32, name=f"y{t}{j}", tag="y", bufs=2)
+            nc.vector.tensor_tensor(y[:], acc[:], rec[(t, j)][:], ALU.mult)
+            ys[(t, j)] = y
+
+        def scatter(t, j):
+            tile, row = wg[t]
+            nc.vector.tensor_tensor(
+                pages[t][:].indirect(idx2[:, 32 * j : 32 * j + 32]),
+                ys[(t, j)][:],
+                tile[:, row, j * W : (j + 1) * W],
+                ALU.mult,
+            )
+
+        pairs = [keep.tile([P, 2, C, 2], BF16, name=f"pairs{c}") for c in range(NC)]
+
+        def round_page(t, c, eng):
+            copy_on(eng, pairs[c][:, t // 2, :, t % 2], pages[t][:, c * C : (c + 1) * C])
+
+        def finish_page(t):
+            nc.sync.dma_start(out=out_rows[:, t, :], in_=pages[t][:])
+            for c in range(NC):
+                round_page(t, c, "s")
+
+        def weave_y(c):
+            il = ring.tile([P, 4 * C], BF16, name=f"yil{c}", tag="yil", bufs=3, align_bytes=64)
+            nc.vector.tensor_copy(
+                out=il[:].bitcast(I32).rearrange("p (m u) -> p m u", u=2),
+                in_=pairs[c][:].rearrange("p u m b -> p u (m b)").bitcast(I32).rearrange("p u m -> p m u"),
+            )
+            yil[c] = il
+
+        def quant_y(c):
+            codes = keep.tile([P, C], U32, name=f"ycodes{c}", align_bytes=64)
+            nc.vector.quantize_mx(out=codes[:].bitcast(FP8X4), scales=yscales[:, c * C : (c + 1) * C], in_=yil[c][:])
+            nc.sync.dma_start(out=words_out[:, c * C : (c + 1) * C], in_=codes[:].bitcast(I32))
+
+        nc.vector.memset(tabs[:].bitcast(I32), 0)
+        nc.vector.memset(wps_raw[:].rearrange("p a c -> p (a c)").bitcast(I32), 0)
+        nc.gpsimd.memset(one[:], 1.0)
+        nc.gpsimd.memset(half[:], 0.5)
+        nc.scalar.activation(warm[:, 0:1], one[:], ACT.Abs_reciprocal_sqrt)
+        clear_page(0, "v")
+        clear_page(1, "v")
+        nc.sync.dma_start(idx[:], offs)
+        nc.sync.dma_start(out=g_sb[:], in_=gain.rearrange("(a p t) -> p a t", a=2, t=4))
+        nc.sync.dma_start(idx2[:], offs2)
+        nc.sync.dma_start(out=wpw_raw[:].bitcast(I32), in_=wp_words.rearrange("a p c -> p a c").bitcast(I32))
+        load_w("w00", w1, 0, 0, "rawA")
+        load_tabs()
+        load_tab(0, "tab0")
+        nc.gpsimd.tensor_tensor(sg[:], g_sb[:], half[:], ALU.pow)
+        clear_page(2, "g")
+        clear_page(3, "g")
+        deal_wpw()
+        load_w("w10", w1, 1, 0, "rawB")
+        load_wps()
+        cast_w("w00", "s", "rawC")
+        load_tab(1, "rawA")
+        gather_s(0)
+        gather_s(1)
+        gather_w(0, 0)
+        quant_w("w00")
+        load_w("w01", w1, 0, 1, "rawC")
+        gather_w(0, 1)
+        load_w("w11", w1, 1, 1, "tab0")
+        deal_wps()
+        cast_w("w10", "s", "grpA")
+        load_w("d0", wd, 0, 0, "rawB")
+        quant_w("w10")
+        gather_w(1, 0)
+        lin(0, 0, "estA")
+        gather_w(1, 1)
+        load_w("d1", wd, 1, 0, "rawA")
+        cast_w("w01", "v", "grpB")
+        load_wg(0, 1, "rawC")
+        quant_w("w01")
+        lin(0, 1, "estC")
+        cast_w("w11", "v", "grpA")
+        load_wg(1, 4, "tab0")
+        quant_w("w11")
+        lin(1, 0, "estB")
+        weave_e(0, 0, "v", "grpA")
+        quant_e(0, 0)
+        weave_e(1, 0, "v", "eilB")
+        quant_e(1, 0)
+        pool_part(0, 0, "rA")
+        cast_w("d0", "v", "estA")
+        cast_w("d1", "s", "grpB")
+        quant_w("d0")
+        quant_w("d1")
+
+        drive_part(0, 0)
+        pool_part(1, 0, "rA")
+        scatter(0, 0)
+        drive_part(1, 0)
+        pool_part(2, 0, "rB")
+        weave_e(0, 1, "s", "rA")
+        scatter(1, 0)
+        drive_part(2, 0)
+        lin(1, 1, "rB")
+        weave_e(1, 1, "s", "eilA")
+        scatter(2, 0)
+        quant_e(0, 1)
+        quant_e(1, 1)
+        pool_part(3, 0, "rC")
+        drive_part(3, 0)
+        scatter(3, 0)
+        for t in range(4):
+            pool_part(t, 1, "rC" if t % 2 else "rD")
+        drive_part(0, 1)
+        for t in range(4):
+            scatter(t, 1)
+            if t < 3:
+                drive_part(t + 1, 1)
+            finish_page(t)
+        weave_y(0)
+        for c in range(NC):
+            if c + 1 < NC:
+                weave_y(c + 1)
+            quant_y(c)
+        for q in range(4):
+            eng = nc.sync if q % 2 == 0 else nc.scalar
+            eng.dma_start(
+                out=out_2[0, 4 * q : 4 * q + 4, :].bitcast(I32), in_=yscales[32 * q : 32 * q + 4, :].bitcast(I32)
+            )

@@ -34,7 +34,7 @@ def tile_list_contrast_gain_control_kernel(
         idx = keep.tile([P, S // 16], U16, name="idx")
         idx2 = keep.tile([P, S // 16], U16, name="idx2")
         tabs = keep.tile([P, T], U8, name="tabs", align_bytes=64)
-        wps_raw = keep.tile([P, 2, N], U8, name="wps_raw", align_bytes=64)
+        wps_raw = keep.tile([P, 2, N], U8, name="wps_raw", tag="wg00", align_bytes=64)
         wpw_raw = keep.tile([P, 2, 2 * N], U8, name="wpw_raw", tag="rawB", align_bytes=64)
         g_sb = keep.tile([P, 2, 4], F32, name="g_sb", tag="page2")
         half = keep.tile([P, 2, 4], F32, name="half", tag="page3")
@@ -101,24 +101,28 @@ def tile_list_contrast_gain_control_kernel(
                     in_=wp_scales[:, 4 * q : 4 * q + 4, :].rearrange("a r c -> r a c").bitcast(I32),
                 )
 
-        def load_wg(t0, t1, tag):
-            tile = keep.tile([P, t1 - t0, S], F32, name=f"wg{t0}", tag=tag, align_bytes=64)
-            for q in range(4):
-                nc.sync.dma_start(out=tile[32 * q : 32 * q + 32, :, :], in_=wgq[:, t0:t1, :])
+        def load_wg(t0, t1, j, tag, step):
+            tile = keep.tile([P, t1 - t0, W], F32, name=f"wg{t0}{j}", tag=tag, align_bytes=64)
+            for t in range(t0, t1, step):
+                for q in (0, 2, 1, 3):
+                    nc.sync.dma_start(
+                        out=tile[32 * q : 32 * q + 32, t - t0 : t - t0 + step, :],
+                        in_=wgq[:, t : t + step, j * W : (j + 1) * W],
+                    )
             for t in range(t0, t1):
-                wg[t] = (tile, t - t0)
+                wg[(t, j)] = (tile, t - t0)
 
-        def cast_w(key, eng, tag):
+        def cast_w(key, engs, tag):
             g = keep.tile([P, 4 * W], BF16, name="grp_" + key, tag=tag, align_bytes=64)
-            copy_on(
-                eng,
-                g[:].rearrange("p (t m i) -> p m t i", t=4, i=4),
-                raws[key][:].rearrange("p i (m t) -> p m t i", t=4),
-            )
+            o = g[:].rearrange("p (t m i) -> p m t i", t=4, i=4)
+            i = raws[key][:].rearrange("p i (m t) -> p m t i", t=4)
+            step = P // len(engs)
+            for n, eng in enumerate(engs):
+                copy_on(eng, o[:, n * step : (n + 1) * step], i[:, n * step : (n + 1) * step])
             grouped[key] = g
 
-        def quant(name, src):
-            codes = keep.tile([P, W], U32, name=name + "_c", align_bytes=64)
+        def quant(name, src, tag=None):
+            codes = keep.tile([P, W], U32, name=name + "_c", tag=tag or name, align_bytes=64)
             scales = keep.tile([P, W], U8, name=name + "_s", align_bytes=64)
             nc.vector.quantize_mx(out=codes[:].bitcast(FP8X4), scales=scales[:], in_=src)
             return codes, scales
@@ -136,10 +140,12 @@ def tile_list_contrast_gain_control_kernel(
             nc.vector.tensor_copy(g[:], tabs[:].indirect(idx[:, 32 * j : 32 * j + 32]))
             gs[j] = g
 
-        def lin(h, j, tag):
-            st = keep.tile([P, 4, W], BF16, name=f"est{h}{j}", tag=tag, align_bytes=64)
-            for t in range(4):
-                acc = psum.tile([P, W], F32, name="lin", tag="lin", bufs=4)
+        def lin(h, j, tag, ts=range(4), bank="lin"):
+            if (h, j) not in est:
+                est[(h, j)] = keep.tile([P, 4, W], BF16, name=f"est{h}{j}", tag=tag, align_bytes=64)
+            st = est[(h, j)]
+            for t in ts:
+                acc = psum.tile([P, W], F32, name="lin", tag=bank, bufs=4 if bank == "lin" else 2)
                 for a in range(2):
                     c, s = wq[f"w{a}{h}"]
                     nc.tensor.matmul_mx(
@@ -152,7 +158,6 @@ def tile_list_contrast_gain_control_kernel(
                         stop=(a == 1),
                     )
                 nc.scalar.activation(st[:, t, :], acc[:], ACT.Square, scale=sg[:, h, t : t + 1])
-            est[(h, j)] = st
 
         def weave_e(h, j, eng, tag):
             il = keep.tile([P, 4 * W], BF16, name=f"eil{h}{j}", tag=tag, align_bytes=64)
@@ -163,8 +168,8 @@ def tile_list_contrast_gain_control_kernel(
             )
             eil[(h, j)] = il
 
-        def quant_e(h, j):
-            eq[(h, j)] = quant(f"q_e{h}{j}", eil[(h, j)][:])
+        def quant_e(h, j, tag=None):
+            eq[(h, j)] = quant(f"q_e{h}{j}", eil[(h, j)][:], tag)
 
         def deal_wpw():
             for a in range(2):
@@ -179,9 +184,9 @@ def tile_list_contrast_gain_control_kernel(
                 in_=wps_raw[:].rearrange("p a (m t) -> p a m t", t=4),
             )
 
-        def pool_part(t, j, tag):
+        def pool_part(t, j, tag, tag2):
             acc = psum.tile([P, W], F32, name="pool", tag="pool", bufs=2)
-            for h in range(2):
+            for h in (j, 1 - j):
                 c, s = eq[(h, j)]
                 nc.tensor.matmul_mx(
                     out=acc[:],
@@ -189,18 +194,18 @@ def tile_list_contrast_gain_control_kernel(
                     lhsT_scale=wps[:, h, t * P : (t + 1) * P],
                     rhs=c[:].bitcast(FP8X4),
                     rhs_scale=s[:],
-                    start=(h == 0),
-                    stop=(h == 1),
+                    start=(h == j),
+                    stop=(h != j),
                 )
             r = keep.tile([P, W], F32, name=f"r{t}{j}", tag=tag, align_bytes=64)
             nc.scalar.activation(r[:], acc[:], ACT.Abs_reciprocal_sqrt, bias=1.0)
-            r2 = ring.tile([P, W], F32, name=f"rr{t}{j}", tag="r2", bufs=6)
+            r2 = keep.tile([P, W], F32, name=f"rr{t}{j}", tag=tag2, align_bytes=64)
             nc.scalar.activation(r2[:], r[:], ACT.Square)
             rec[(t, j)] = r2
 
-        def drive_part(t, j):
+        def drive_part(t, j, tag):
             acc = psum.tile([P, W], F32, name="drive", tag="drive", bufs=2)
-            for h in range(2):
+            for h in (j, 1 - j):
                 c, s = eq[(h, j)]
                 wc, ws = wq[f"d{h}"]
                 nc.tensor.matmul_mx(
@@ -209,19 +214,19 @@ def tile_list_contrast_gain_control_kernel(
                     lhsT_scale=ws[:, t * P : (t + 1) * P],
                     rhs=c[:].bitcast(FP8X4),
                     rhs_scale=s[:],
-                    start=(h == 0),
-                    stop=(h == 1),
+                    start=(h == j),
+                    stop=(h != j),
                 )
-            y = ring.tile([P, W], F32, name=f"y{t}{j}", tag="y", bufs=2)
+            y = keep.tile([P, W], F32, name=f"y{t}{j}", tag=tag, align_bytes=64)
             nc.vector.tensor_tensor(y[:], acc[:], rec[(t, j)][:], ALU.mult)
             ys[(t, j)] = y
 
         def scatter(t, j):
-            tile, row = wg[t]
+            tile, row = wg[(t, j)]
             nc.vector.tensor_tensor(
                 pages[t][:].indirect(idx2[:, 32 * j : 32 * j + 32]),
                 ys[(t, j)][:],
-                tile[:, row, j * W : (j + 1) * W],
+                tile[:, row, :],
                 ALU.mult,
             )
 
@@ -235,11 +240,13 @@ def tile_list_contrast_gain_control_kernel(
             for c in range(NC):
                 round_page(t, c, "s")
 
-        def weave_y(c):
-            il = ring.tile([P, 4 * C], BF16, name=f"yil{c}", tag="yil", bufs=3, align_bytes=64)
-            nc.vector.tensor_copy(
-                out=il[:].bitcast(I32).rearrange("p (m u) -> p m u", u=2),
-                in_=pairs[c][:].rearrange("p u m b -> p u (m b)").bitcast(I32).rearrange("p u m -> p m u"),
+        def weave_y(c, eng):
+            il = ring.tile([P, 4 * C], BF16, name=f"yil{c}", tag="yil", bufs=4, align_bytes=64)
+            word = I32 if eng == "v" else U32
+            copy_on(
+                eng,
+                il[:].bitcast(word).rearrange("p (m u) -> p m u", u=2),
+                pairs[c][:].rearrange("p u m b -> p u (m b)").bitcast(word).rearrange("p u m -> p m u"),
             )
             yil[c] = il
 
@@ -278,6 +285,7 @@ def tile_list_contrast_gain_control_kernel(
         gather_w(0, 1)
         load_w("w11", w1, 1, 1, "tab0")
         deal_wps()
+        load_wg(0, 1, 0, "wg00", 1)
         cast_w("w10", "s", "grpA")
         load_w("d0", wd, 0, 0, "rawB")
         quant_w("w10")
@@ -286,52 +294,62 @@ def tile_list_contrast_gain_control_kernel(
         gather_w(1, 1)
         load_w("d1", wd, 1, 0, "rawA")
         cast_w("w01", "v", "grpB")
-        load_wg(0, 1, "rawC")
+        load_wg(1, 4, 0, "rawC", 1)
         quant_w("w01")
         lin(0, 1, "estC")
         cast_w("w11", "v", "grpA")
-        load_wg(1, 4, "tab0")
+        load_wg(0, 4, 1, "tab0", 4)
         quant_w("w11")
         lin(1, 0, "estB")
         weave_e(0, 0, "v", "grpA")
         quant_e(0, 0)
         weave_e(1, 0, "v", "eilB")
         quant_e(1, 0)
-        pool_part(0, 0, "rA")
+        pool_part(0, 0, "rA", "q0")
         cast_w("d0", "v", "estA")
         cast_w("d1", "s", "grpB")
         quant_w("d0")
         quant_w("d1")
-
-        drive_part(0, 0)
-        pool_part(1, 0, "rA")
+        drive_part(0, 0, "yA")
+        pool_part(1, 0, "rA", "q1")
+        drive_part(1, 0, "yB")
         scatter(0, 0)
-        drive_part(1, 0)
-        pool_part(2, 0, "rB")
+        pool_part(2, 0, "rB", "q2")
         weave_e(0, 1, "s", "rA")
+        drive_part(2, 0, "yC")
         scatter(1, 0)
-        drive_part(2, 0)
+        quant_e(0, 1, "yB")
         lin(1, 1, "rB")
         weave_e(1, 1, "s", "eilA")
+        pool_part(3, 0, "rC", "q3")
         scatter(2, 0)
-        quant_e(0, 1)
-        quant_e(1, 1)
-        pool_part(3, 0, "rC")
-        drive_part(3, 0)
+        quant_e(1, 1, "yC")
+        drive_part(3, 0, "eilA")
+        pool_part(0, 1, "rD", "q0")
+        pool_part(1, 1, "rC", "q1")
+        pool_part(2, 1, "rD", "q2")
+        pool_part(3, 1, "rC", "q3")
         scatter(3, 0)
-        for t in range(4):
-            pool_part(t, 1, "rC" if t % 2 else "rD")
-        drive_part(0, 1)
-        for t in range(4):
-            scatter(t, 1)
-            if t < 3:
-                drive_part(t + 1, 1)
-            finish_page(t)
-        weave_y(0)
-        for c in range(NC):
-            if c + 1 < NC:
-                weave_y(c + 1)
-            quant_y(c)
+        drive_part(0, 1, "eilA")
+        drive_part(1, 1, "q0")
+        scatter(0, 1)
+        finish_page(0)
+        drive_part(2, 1, "eilA")
+        scatter(1, 1)
+        finish_page(1)
+        drive_part(3, 1, "q0")
+        scatter(2, 1)
+        finish_page(2)
+        scatter(3, 1)
+        finish_page(3)
+        weave_y(0, "v")
+        weave_y(1, "v")
+        quant_y(0)
+        weave_y(2, "v")
+        quant_y(1)
+        weave_y(3, "s")
+        quant_y(2)
+        quant_y(3)
         for q in range(4):
             eng = nc.sync if q % 2 == 0 else nc.scalar
             eng.dma_start(

@@ -36,11 +36,9 @@ def tile_list_contrast_gain_control_kernel(
         tabs = keep.tile([P, T], U8, name="tabs", align_bytes=64)
         wps_raw = keep.tile([P, 2, N], U8, name="wps_raw", tag="wg00", align_bytes=64)
         wpw_raw = keep.tile([P, 2, 2 * N], U8, name="wpw_raw", tag="rawB", align_bytes=64)
-        g_sb = keep.tile([P, 2, 4], F32, name="g_sb", tag="page2")
-        half = keep.tile([P, 2, 4], F32, name="half", tag="page3")
+        g_sb = keep.tile([P, 2, 4], F32, name="g_sb")
         sg = keep.tile([P, 2, 4], F32, name="sg")
-        warm = keep.tile([P, 2], F32, name="warm")
-        one = keep.tile([P, 1], F32, name="one", tag="tab0", align_bytes=64)
+        tiny = keep.tile([P, 1], F32, name="tiny", tag="tab0", align_bytes=64)
         wpw = keep.tile([P, 2, 2 * N], U8, name="wpw", align_bytes=64)
         wps = keep.tile([P, 2, N], U8, name="wps", align_bytes=64)
         yscales = keep.tile([P, T2], U8, name="yscales", align_bytes=64)
@@ -68,13 +66,22 @@ def tile_list_contrast_gain_control_kernel(
             else:
                 nc.scalar.copy(out=o, in_=i)
 
-        def clear_page(t, eng):
-            pages[t] = keep.tile([P, T2], F32, name=f"page{t}", tag=f"page{t}")
-            if eng == "v":
+        def clear_page(t, tag):
+            pages[t] = keep.tile([P, T2], F32, name=f"page{t}", tag=tag, align_bytes=64)
+            if t < 2:
                 nc.vector.memset(pages[t][:].bitcast(I32), 0)
             else:
                 for c in range(4):
                     nc.gpsimd.memset(pages[t][:, c * W : (c + 1) * W].bitcast(I32), 0)
+
+        def root_gain():
+            r, s0, sq, rest, fix = [keep.tile([P, 2, 4], F32, name=f"root{n}") for n in range(5)]
+            nc.scalar.activation(r[:], g_sb[:], ACT.Abs_reciprocal_sqrt, bias=tiny[:])
+            nc.vector.tensor_tensor(s0[:], g_sb[:], r[:], ALU.mult)
+            nc.vector.tensor_tensor(sq[:], s0[:], s0[:], ALU.mult)
+            nc.vector.tensor_tensor(rest[:], g_sb[:], sq[:], ALU.subtract)
+            nc.vector.scalar_tensor_tensor(fix[:], rest[:], 0.5, r[:], ALU.mult, ALU.mult)
+            nc.vector.tensor_tensor(sg[:], s0[:], fix[:], ALU.add)
 
         def load_w(key, src, a, h, tag):
             raw = keep.tile([P, 4, W], F32, name="raw_" + key, tag=tag, align_bytes=64)
@@ -257,21 +264,17 @@ def tile_list_contrast_gain_control_kernel(
 
         nc.vector.memset(tabs[:].bitcast(I32), 0)
         nc.vector.memset(wps_raw[:].rearrange("p a c -> p (a c)").bitcast(I32), 0)
-        nc.gpsimd.memset(one[:], 1.0)
-        nc.gpsimd.memset(half[:], 0.5)
-        nc.scalar.activation(warm[:, 0:1], one[:], ACT.Abs_reciprocal_sqrt)
-        clear_page(0, "v")
-        clear_page(1, "v")
+        nc.gpsimd.memset(tiny[:], 2.0**-100)
+        clear_page(0, "page0")
+        clear_page(1, "page1")
         nc.sync.dma_start(idx[:], offs)
         nc.sync.dma_start(out=g_sb[:], in_=gain.rearrange("(a p t) -> p a t", a=2, t=4))
         nc.sync.dma_start(idx2[:], offs2)
         nc.sync.dma_start(out=wpw_raw[:].bitcast(I32), in_=wp_words.rearrange("a p c -> p a c").bitcast(I32))
         load_w("w00", w1, 0, 0, "rawA")
         load_tabs()
+        root_gain()
         load_tab(0, "tab0")
-        nc.gpsimd.tensor_tensor(sg[:], g_sb[:], half[:], ALU.pow)
-        clear_page(2, "g")
-        clear_page(3, "g")
         deal_wpw()
         load_w("w10", w1, 1, 0, "rawB")
         load_wps()
@@ -311,6 +314,8 @@ def tile_list_contrast_gain_control_kernel(
         quant_w("d0")
         quant_w("d1")
         drive_part(0, 0, "yA")
+        clear_page(2, "grpB")
+        clear_page(3, "q0")
         pool_part(1, 0, "rA", "q1")
         drive_part(1, 0, "yB")
         scatter(0, 0)
@@ -325,19 +330,19 @@ def tile_list_contrast_gain_control_kernel(
         scatter(2, 0)
         quant_e(1, 1, "yC")
         drive_part(3, 0, "eilA")
-        pool_part(0, 1, "rD", "q0")
+        pool_part(0, 1, "rD", "q4")
         pool_part(1, 1, "rC", "q1")
         pool_part(2, 1, "rD", "q2")
         pool_part(3, 1, "rC", "q3")
         scatter(3, 0)
         drive_part(0, 1, "eilA")
-        drive_part(1, 1, "q0")
+        drive_part(1, 1, "q4")
         scatter(0, 1)
         finish_page(0)
         drive_part(2, 1, "eilA")
         scatter(1, 1)
         finish_page(1)
-        drive_part(3, 1, "q0")
+        drive_part(3, 1, "q4")
         scatter(2, 1)
         finish_page(2)
         scatter(3, 1)

@@ -18,8 +18,8 @@ ALU = mybir.AluOpType
 
 P = 128
 W = 512
-C = 512
-NC = T2 // C
+CUTS = (0, 256, 512, 1024, 1536, 2048)
+NC = len(CUTS) - 1
 
 
 def tile_list_contrast_gain_control_kernel(
@@ -28,13 +28,12 @@ def tile_list_contrast_gain_control_kernel(
     nc = tc.nc
     with ExitStack() as ctx:
         keep = ctx.enter_context(tc.tile_pool(name="keep", bufs=1))
-        ring = ctx.enter_context(tc.tile_pool(name="ring", bufs=2))
         psum = ctx.enter_context(tc.psum_pool(name="psum", bufs=2))
 
         idx = keep.tile([P, S // 16], U16, name="idx")
         idx2 = keep.tile([P, S // 16], U16, name="idx2")
         tabs = keep.tile([P, T], U8, name="tabs", align_bytes=64)
-        wps_raw = keep.tile([P, 2, N], U8, name="wps_raw", tag="wg00", align_bytes=64)
+        wps_raw = keep.tile([P, 2, N], U8, name="wps_raw", align_bytes=64)
         wpw_raw = keep.tile([P, 2, 2 * N], U8, name="wpw_raw", tag="rawB", align_bytes=64)
         g_sb = keep.tile([P, 2, 4], F32, name="g_sb")
         sg = keep.tile([P, 2, 4], F32, name="sg")
@@ -134,8 +133,8 @@ def tile_list_contrast_gain_control_kernel(
             nc.vector.quantize_mx(out=codes[:].bitcast(FP8X4), scales=scales[:], in_=src)
             return codes, scales
 
-        def quant_w(key):
-            wq[key] = quant("q_" + key, grouped[key][:])
+        def quant_w(key, tag=None):
+            wq[key] = quant("q_" + key, grouped[key][:], tag)
 
         def gather_w(a, j):
             g = keep.tile([P, W], U32, name=f"gw{a}{j}", align_bytes=64)
@@ -147,36 +146,40 @@ def tile_list_contrast_gain_control_kernel(
             nc.vector.tensor_copy(g[:], tabs[:].indirect(idx[:, 32 * j : 32 * j + 32]))
             gs[j] = g
 
-        def lin(h, j, tag, ts=range(4), bank="lin"):
-            if (h, j) not in est:
-                est[(h, j)] = keep.tile([P, 4, W], BF16, name=f"est{h}{j}", tag=tag, align_bytes=64)
-            st = est[(h, j)]
-            for t in ts:
-                acc = psum.tile([P, W], F32, name="lin", tag=bank, bufs=4 if bank == "lin" else 2)
+        def lin(h, j, c0, c1, tag):
+            st = keep.tile([P, 4, c1 - c0], BF16, name=f"est{h}{j}{c0}", tag=tag, align_bytes=64)
+            for t in range(4):
+                acc = psum.tile([P, c1 - c0], F32, name="lin", tag="lin", bufs=4)
                 for a in range(2):
                     c, s = wq[f"w{a}{h}"]
                     nc.tensor.matmul_mx(
                         out=acc[:],
                         lhsT=c[:, t * P : (t + 1) * P].bitcast(FP8X4),
                         lhsT_scale=s[:, t * P : (t + 1) * P],
-                        rhs=gw[(a, j)][:].bitcast(FP8X4),
-                        rhs_scale=gs[j][4 * a : P, :],
+                        rhs=gw[(a, j)][:, c0:c1].bitcast(FP8X4),
+                        rhs_scale=gs[j][4 * a : P, c0:c1],
                         start=(a == 0),
                         stop=(a == 1),
                     )
                 nc.scalar.activation(st[:, t, :], acc[:], ACT.Square, scale=sg[:, h, t : t + 1])
+            est[(h, j, c0)] = st
 
-        def weave_e(h, j, eng, tag):
-            il = keep.tile([P, 4 * W], BF16, name=f"eil{h}{j}", tag=tag, align_bytes=64)
+        def weave_e(h, j, c0, c1, eng, tag):
+            il = keep.tile([P, 4 * (c1 - c0)], BF16, name=f"eil{h}{j}{c0}", tag=tag, align_bytes=64)
             copy_on(
                 eng,
                 il[:].rearrange("p (c i t) -> p c t i", i=4, t=4),
-                est[(h, j)][:].rearrange("p t (c i) -> p c t i", i=4),
+                est[(h, j, c0)][:].rearrange("p t (c i) -> p c t i", i=4),
             )
-            eil[(h, j)] = il
+            eil[(h, j, c0)] = il
 
-        def quant_e(h, j, tag=None):
-            eq[(h, j)] = quant(f"q_e{h}{j}", eil[(h, j)][:], tag)
+        def quant_e(h, j, c0, c1, tag=None):
+            if (h, j) not in eq:
+                codes = keep.tile([P, W], U32, name=f"q_e{h}{j}_c", tag=tag or f"q_e{h}{j}", align_bytes=64)
+                scales = keep.tile([P, W], U8, name=f"q_e{h}{j}_s", align_bytes=64)
+                eq[(h, j)] = (codes, scales)
+            codes, scales = eq[(h, j)]
+            nc.vector.quantize_mx(out=codes[:, c0:c1].bitcast(FP8X4), scales=scales[:, c0:c1], in_=eil[(h, j, c0)][:])
 
         def deal_wpw():
             for a in range(2):
@@ -191,7 +194,7 @@ def tile_list_contrast_gain_control_kernel(
                 in_=wps_raw[:].rearrange("p a (m t) -> p a m t", t=4),
             )
 
-        def pool_part(t, j, tag, tag2):
+        def pool_part(t, j, tag, tag2, parts=1):
             acc = psum.tile([P, W], F32, name="pool", tag="pool", bufs=2)
             for h in (j, 1 - j):
                 c, s = eq[(h, j)]
@@ -205,12 +208,14 @@ def tile_list_contrast_gain_control_kernel(
                     stop=(h != j),
                 )
             r = keep.tile([P, W], F32, name=f"r{t}{j}", tag=tag, align_bytes=64)
-            nc.scalar.activation(r[:], acc[:], ACT.Abs_reciprocal_sqrt, bias=1.0)
             r2 = keep.tile([P, W], F32, name=f"rr{t}{j}", tag=tag2, align_bytes=64)
-            nc.scalar.activation(r2[:], r[:], ACT.Square)
+            for c0 in range(0, W, W // parts):
+                cols = slice(c0, c0 + W // parts)
+                nc.scalar.activation(r[:, cols], acc[:, cols], ACT.Abs_reciprocal_sqrt, bias=1.0)
+                nc.scalar.activation(r2[:, cols], r[:, cols], ACT.Square)
             rec[(t, j)] = r2
 
-        def drive_part(t, j, tag):
+        def drive_part(t, j, tag, parts=1):
             acc = psum.tile([P, W], F32, name="drive", tag="drive", bufs=2)
             for h in (j, 1 - j):
                 c, s = eq[(h, j)]
@@ -225,22 +230,24 @@ def tile_list_contrast_gain_control_kernel(
                     stop=(h != j),
                 )
             y = keep.tile([P, W], F32, name=f"y{t}{j}", tag=tag, align_bytes=64)
-            nc.vector.tensor_tensor(y[:], acc[:], rec[(t, j)][:], ALU.mult)
             ys[(t, j)] = y
+            for c0 in range(0, W, W // parts):
+                cols = slice(c0, c0 + W // parts)
+                nc.vector.tensor_tensor(y[:, cols], acc[:, cols], rec[(t, j)][:, cols], ALU.mult)
 
-        def scatter(t, j):
+        def scatter(t, j, c0=0, c1=W):
             tile, row = wg[(t, j)]
             nc.vector.tensor_tensor(
-                pages[t][:].indirect(idx2[:, 32 * j : 32 * j + 32]),
-                ys[(t, j)][:],
-                tile[:, row, :],
+                pages[t][:].indirect(idx2[:, (j * W + c0) // 16 : (j * W + c1) // 16]),
+                ys[(t, j)][:, c0:c1],
+                tile[:, row, c0:c1],
                 ALU.mult,
             )
 
-        pairs = [keep.tile([P, 2, C, 2], BF16, name=f"pairs{c}") for c in range(NC)]
+        pairs = [keep.tile([P, 2, CUTS[c + 1] - CUTS[c], 2], BF16, name=f"pairs{c}") for c in range(NC)]
 
         def round_page(t, c, eng):
-            copy_on(eng, pairs[c][:, t // 2, :, t % 2], pages[t][:, c * C : (c + 1) * C])
+            copy_on(eng, pairs[c][:, t // 2, :, t % 2], pages[t][:, CUTS[c] : CUTS[c + 1]])
 
         def finish_page(t):
             nc.sync.dma_start(out=out_rows[:, t, :], in_=pages[t][:])
@@ -248,7 +255,7 @@ def tile_list_contrast_gain_control_kernel(
                 round_page(t, c, "s")
 
         def weave_y(c, eng):
-            il = ring.tile([P, 4 * C], BF16, name=f"yil{c}", tag="yil", bufs=4, align_bytes=64)
+            il = keep.tile([P, 4 * (CUTS[c + 1] - CUTS[c])], BF16, name=f"yil{c}", align_bytes=64)
             word = I32 if eng == "v" else U32
             copy_on(
                 eng,
@@ -258,9 +265,9 @@ def tile_list_contrast_gain_control_kernel(
             yil[c] = il
 
         def quant_y(c):
-            codes = keep.tile([P, C], U32, name=f"ycodes{c}", align_bytes=64)
-            nc.vector.quantize_mx(out=codes[:].bitcast(FP8X4), scales=yscales[:, c * C : (c + 1) * C], in_=yil[c][:])
-            nc.sync.dma_start(out=words_out[:, c * C : (c + 1) * C], in_=codes[:].bitcast(I32))
+            codes = keep.tile([P, CUTS[c + 1] - CUTS[c]], U32, name=f"ycodes{c}", align_bytes=64)
+            nc.vector.quantize_mx(out=codes[:].bitcast(FP8X4), scales=yscales[:, CUTS[c] : CUTS[c + 1]], in_=yil[c][:])
+            nc.sync.dma_start(out=words_out[:, CUTS[c] : CUTS[c + 1]], in_=codes[:].bitcast(I32))
 
         nc.vector.memset(tabs[:].bitcast(I32), 0)
         nc.vector.memset(wps_raw[:].rearrange("p a c -> p (a c)").bitcast(I32), 0)
@@ -288,62 +295,65 @@ def tile_list_contrast_gain_control_kernel(
         gather_w(0, 1)
         load_w("w11", w1, 1, 1, "tab0")
         deal_wps()
-        load_wg(0, 1, 0, "wg00", 1)
         cast_w("w10", "s", "grpA")
         load_w("d0", wd, 0, 0, "rawB")
         quant_w("w10")
         gather_w(1, 0)
-        lin(0, 0, "estA")
+        lin(0, 0, 0, 512, "estA")
         gather_w(1, 1)
         load_w("d1", wd, 1, 0, "rawA")
         cast_w("w01", "v", "grpB")
-        load_wg(1, 4, 0, "rawC", 1)
+        load_wg(0, 4, 0, "rawC", 1)
         quant_w("w01")
-        lin(0, 1, "estC")
+        lin(0, 1, 0, 512, "estC")
         cast_w("w11", "v", "grpA")
         load_wg(0, 4, 1, "tab0", 4)
         quant_w("w11")
-        lin(1, 0, "estB")
-        weave_e(0, 0, "v", "grpA")
-        quant_e(0, 0)
-        weave_e(1, 0, "v", "eilB")
-        quant_e(1, 0)
-        pool_part(0, 0, "rA", "q0")
+        lin(1, 0, 0, 256, "estB")
+        lin(1, 0, 256, 512, "estD")
+        weave_e(0, 0, 0, 512, "v", "grpA")
+        quant_e(0, 0, 0, 512)
         cast_w("d0", "v", "estA")
+        weave_e(1, 0, 0, 256, "v", "eilB")
+        weave_e(1, 0, 256, 512, "v", "eilC")
+        quant_e(1, 0, 0, 256)
+        quant_e(1, 0, 256, 512)
+        pool_part(0, 0, "rA", "q0", 2)
         cast_w("d1", "s", "grpB")
         quant_w("d0")
         quant_w("d1")
-        drive_part(0, 0, "yA")
+        drive_part(0, 0, "yA", 2)
         clear_page(2, "grpB")
         clear_page(3, "q0")
         pool_part(1, 0, "rA", "q1")
+        scatter(0, 0, 0, 256)
         drive_part(1, 0, "yB")
-        scatter(0, 0)
+        scatter(0, 0, 256, 512)
         pool_part(2, 0, "rB", "q2")
-        weave_e(0, 1, "s", "rA")
+        pool_part(3, 0, "rA", "q3")
+        weave_e(0, 1, 0, 512, "s", "rA")
         drive_part(2, 0, "yC")
         scatter(1, 0)
-        quant_e(0, 1, "yB")
-        lin(1, 1, "rB")
-        weave_e(1, 1, "s", "eilA")
-        pool_part(3, 0, "rC", "q3")
+        quant_e(0, 1, 0, 512, "yB")
+        lin(1, 1, 0, 512, "rB")
+        weave_e(1, 1, 0, 512, "s", "eilA")
         scatter(2, 0)
-        quant_e(1, 1, "yC")
+        quant_e(1, 1, 0, 512, "yC")
         drive_part(3, 0, "eilA")
         pool_part(0, 1, "rD", "q4")
         pool_part(1, 1, "rC", "q1")
-        pool_part(2, 1, "rD", "q2")
+        pool_part(2, 1, "rE", "q2")
         pool_part(3, 1, "rC", "q3")
         scatter(3, 0)
         drive_part(0, 1, "eilA")
-        drive_part(1, 1, "q4")
         scatter(0, 1)
         finish_page(0)
-        drive_part(2, 1, "eilA")
+        drive_part(1, 1, "rE")
+        drive_part(2, 1, "yD")
         scatter(1, 1)
         finish_page(1)
-        drive_part(3, 1, "q4")
         scatter(2, 1)
+        drive_part(3, 1, "yD")
         finish_page(2)
         scatter(3, 1)
         finish_page(3)
@@ -352,9 +362,11 @@ def tile_list_contrast_gain_control_kernel(
         quant_y(0)
         weave_y(2, "v")
         quant_y(1)
-        weave_y(3, "s")
+        weave_y(3, "v")
         quant_y(2)
+        weave_y(4, "s")
         quant_y(3)
+        quant_y(4)
         for q in range(4):
             eng = nc.sync if q % 2 == 0 else nc.scalar
             eng.dma_start(

@@ -18,8 +18,11 @@ ALU = mybir.AluOpType
 
 P = 128
 W = 512
-CUTS = (0, 256, 512, 1024, 1536, 2048)
+CUTS = (0, 256, 512, 1024, 1536, 1792, 2048)
 NC = len(CUTS) - 1
+FIRST = [(t, 0) for t in range(4)]
+SECOND = [(t, 1) for t in range(4)]
+BOTH = [(t, a) for t in range(4) for a in range(2)]
 
 
 def tile_list_contrast_gain_control_kernel(
@@ -28,20 +31,22 @@ def tile_list_contrast_gain_control_kernel(
     nc = tc.nc
     with ExitStack() as ctx:
         keep = ctx.enter_context(tc.tile_pool(name="keep", bufs=1))
-        psum = ctx.enter_context(tc.psum_pool(name="psum", bufs=2))
+        psum = ctx.enter_context(tc.psum_pool(name="psum", bufs=1))
 
         idx = keep.tile([P, S // 16], U16, name="idx")
         idx2 = keep.tile([P, S // 16], U16, name="idx2")
-        tabs = keep.tile([P, T], U8, name="tabs", align_bytes=64)
-        wps_raw = keep.tile([P, 2, N], U8, name="wps_raw", align_bytes=64)
-        wpw_raw = keep.tile([P, 2, 2 * N], U8, name="wpw_raw", tag="rawB", align_bytes=64)
+        tabs = keep.tile([P, T], U8, name="tabs", tag="q_w00", align_bytes=64)
+        wps_raw = keep.tile([P, 2, N], U8, name="wps_raw", tag="q_w10", align_bytes=64)
+        wpw_raw = keep.tile([P, 2, 2 * N], U8, name="wpw_raw", tag="page2", align_bytes=64)
         g_sb = keep.tile([P, 2, 4], F32, name="g_sb")
         sg = keep.tile([P, 2, 4], F32, name="sg")
-        tiny = keep.tile([P, 1], F32, name="tiny", tag="tab0", align_bytes=64)
+        tiny = keep.tile([P, 1], F32, name="tiny")
         wpw = keep.tile([P, 2, 2 * N], U8, name="wpw", align_bytes=64)
         wps = keep.tile([P, 2, N], U8, name="wps", align_bytes=64)
-        yscales = keep.tile([P, T2], U8, name="yscales", align_bytes=64)
+        yscales = keep.tile([P, W], U8, name="yscales", align_bytes=64)
         pages = {}
+        accs = {}
+        drives = {}
         tabw = {}
         raws = {}
         grouped = {}
@@ -74,7 +79,8 @@ def tile_list_contrast_gain_control_kernel(
                     nc.gpsimd.memset(pages[t][:, c * W : (c + 1) * W].bitcast(I32), 0)
 
         def root_gain():
-            r, s0, sq, rest, fix = [keep.tile([P, 2, 4], F32, name=f"root{n}") for n in range(5)]
+            r, s0, sq, rest = [keep.tile([P, 2, 4], F32, name=f"root{n}") for n in range(4)]
+            fix = keep.tile([P, 2, 4], F32, name="fix", tag="page3", align_bytes=64)
             nc.scalar.activation(r[:], g_sb[:], ACT.Abs_reciprocal_sqrt, bias=tiny[:])
             nc.vector.tensor_tensor(s0[:], g_sb[:], r[:], ALU.mult)
             nc.vector.tensor_tensor(sq[:], s0[:], s0[:], ALU.mult)
@@ -82,12 +88,16 @@ def tile_list_contrast_gain_control_kernel(
             nc.vector.scalar_tensor_tensor(fix[:], rest[:], 0.5, r[:], ALU.mult, ALU.mult)
             nc.vector.tensor_tensor(sg[:], s0[:], fix[:], ALU.add)
 
-        def load_w(key, src, a, h, tag):
-            raw = keep.tile([P, 4, W], F32, name="raw_" + key, tag=tag, align_bytes=64)
-            nc.sync.dma_start(
-                out=raw[:], in_=src[a * W : (a + 1) * W, h * W : (h + 1) * W].rearrange("(p i) c -> p i c", i=4)
-            )
-            raws[key] = raw
+        def load_w(key, src, a, h, tags):
+            n = W // len(tags)
+            raws[key] = []
+            for u, tag in enumerate(tags):
+                raw = keep.tile([P, 4, n], F32, name=f"raw_{key}{u}", tag=tag, align_bytes=64)
+                c0 = h * W + u * n
+                nc.sync.dma_start(
+                    out=raw[:], in_=src[a * W : (a + 1) * W, c0 : c0 + n].rearrange("(p i) c -> p i c", i=4)
+                )
+                raws[key].append(raw)
 
         def load_tab(a, tag):
             tabw[a] = keep.tile([P, T], I32, name=f"tabw{a}", tag=tag, align_bytes=64)
@@ -118,50 +128,59 @@ def tile_list_contrast_gain_control_kernel(
             for t in range(t0, t1):
                 wg[(t, j)] = (tile, t - t0)
 
-        def cast_w(key, engs, tag):
+        def cast_w(key, shares, tag):
             g = keep.tile([P, 4 * W], BF16, name="grp_" + key, tag=tag, align_bytes=64)
             o = g[:].rearrange("p (t m i) -> p m t i", t=4, i=4)
-            i = raws[key][:].rearrange("p i (m t) -> p m t i", t=4)
-            step = P // len(engs)
-            for n, eng in enumerate(engs):
-                copy_on(eng, o[:, n * step : (n + 1) * step], i[:, n * step : (n + 1) * step])
+            per = P // len(raws[key])
+            for eng, m0, m1 in shares:
+                i = raws[key][m0 // per][:].rearrange("p i (m t) -> p m t i", t=4)
+                copy_on(eng, o[:, m0:m1], i[:, m0 % per : m0 % per + m1 - m0])
             grouped[key] = g
 
-        def quant(name, src, tag=None):
-            codes = keep.tile([P, W], U32, name=name + "_c", tag=tag or name, align_bytes=64)
-            scales = keep.tile([P, W], U8, name=name + "_s", align_bytes=64)
-            nc.vector.quantize_mx(out=codes[:].bitcast(FP8X4), scales=scales[:], in_=src)
-            return codes, scales
+        def quant_w(key, t0=0, t1=4, tag=None):
+            if key not in wq:
+                codes = keep.tile([P, W], U32, name=f"q_{key}_c", tag=tag or "q_" + key, align_bytes=64)
+                scales = keep.tile([P, W], U8, name=f"q_{key}_s", align_bytes=64)
+                wq[key] = (codes, scales)
+            codes, scales = wq[key]
+            nc.vector.quantize_mx(
+                out=codes[:, t0 * P : t1 * P].bitcast(FP8X4),
+                scales=scales[:, t0 * P : t1 * P],
+                in_=grouped[key][:, t0 * W : t1 * W],
+            )
 
-        def quant_w(key, tag=None):
-            wq[key] = quant("q_" + key, grouped[key][:], tag)
-
-        def gather_w(a, j):
-            g = keep.tile([P, W], U32, name=f"gw{a}{j}", align_bytes=64)
-            nc.vector.tensor_copy(g[:], tabw[a][:].bitcast(U32).indirect(idx[:, 32 * j : 32 * j + 32]))
-            gw[(a, j)] = g
+        def gather_w(a, j, c0, n, tag=None):
+            g = keep.tile([P, n], U32, name=f"gw{a}{j}{c0}", tag=tag or f"gw{a}{j}{c0}", align_bytes=64)
+            first = (j * W + c0) // 16
+            nc.vector.tensor_copy(g[:], tabw[a][:].bitcast(U32).indirect(idx[:, first : first + n // 16]))
+            for c in range(c0, c0 + n, 256):
+                gw[(a, j, c)] = (g, c - c0)
 
         def gather_s(j):
             g = keep.tile([P, W], U8, name=f"gs{j}", align_bytes=64)
             nc.vector.tensor_copy(g[:], tabs[:].indirect(idx[:, 32 * j : 32 * j + 32]))
             gs[j] = g
 
-        def lin(h, j, c0, c1, tag):
+        def lin(h, j, c0, n, passes, bank):
+            for t, a in passes:
+                c, s = wq[f"w{a}{h}"]
+                g, g0 = gw[(a, j, c0)]
+                if a == 0:
+                    accs[(h, j, c0, t)] = psum.tile([P, n], F32, name=f"lin{h}{j}{c0}{t}", tag=f"{bank}{t}")
+                nc.tensor.matmul_mx(
+                    out=accs[(h, j, c0, t)][:],
+                    lhsT=c[:, t * P : (t + 1) * P].bitcast(FP8X4),
+                    lhsT_scale=s[:, t * P : (t + 1) * P],
+                    rhs=g[:, g0 : g0 + n].bitcast(FP8X4),
+                    rhs_scale=gs[j][4 * a : P, c0 : c0 + n],
+                    start=(a == 0),
+                    stop=(a == 1),
+                )
+
+        def square(h, j, c0, c1, tag):
             st = keep.tile([P, 4, c1 - c0], BF16, name=f"est{h}{j}{c0}", tag=tag, align_bytes=64)
             for t in range(4):
-                acc = psum.tile([P, c1 - c0], F32, name="lin", tag="lin", bufs=4)
-                for a in range(2):
-                    c, s = wq[f"w{a}{h}"]
-                    nc.tensor.matmul_mx(
-                        out=acc[:],
-                        lhsT=c[:, t * P : (t + 1) * P].bitcast(FP8X4),
-                        lhsT_scale=s[:, t * P : (t + 1) * P],
-                        rhs=gw[(a, j)][:, c0:c1].bitcast(FP8X4),
-                        rhs_scale=gs[j][4 * a : P, c0:c1],
-                        start=(a == 0),
-                        stop=(a == 1),
-                    )
-                nc.scalar.activation(st[:, t, :], acc[:], ACT.Square, scale=sg[:, h, t : t + 1])
+                nc.scalar.activation(st[:, t, :], accs[(h, j, c0, t)][:], ACT.Square, scale=sg[:, h, t : t + 1])
             est[(h, j, c0)] = st
 
         def weave_e(h, j, c0, c1, eng, tag):
@@ -194,9 +213,10 @@ def tile_list_contrast_gain_control_kernel(
                 in_=wps_raw[:].rearrange("p a (m t) -> p a m t", t=4),
             )
 
-        def pool_part(t, j, tag, tag2, parts=1):
-            acc = psum.tile([P, W], F32, name="pool", tag="pool", bufs=2)
-            for h in (j, 1 - j):
+        def pool_part(t, j, bank, tag, tag2, parts=1):
+            acc = psum.tile([P, W], F32, name=f"pool{t}{j}", tag=bank)
+            order = (0, 1) if (t, j) == (0, 0) else (1, 0)
+            for h in order:
                 c, s = eq[(h, j)]
                 nc.tensor.matmul_mx(
                     out=acc[:],
@@ -204,20 +224,20 @@ def tile_list_contrast_gain_control_kernel(
                     lhsT_scale=wps[:, h, t * P : (t + 1) * P],
                     rhs=c[:].bitcast(FP8X4),
                     rhs_scale=s[:],
-                    start=(h == j),
-                    stop=(h != j),
+                    start=(h == order[0]),
+                    stop=(h == order[1]),
                 )
             r = keep.tile([P, W], F32, name=f"r{t}{j}", tag=tag, align_bytes=64)
             r2 = keep.tile([P, W], F32, name=f"rr{t}{j}", tag=tag2, align_bytes=64)
-            for c0 in range(0, W, W // parts):
-                cols = slice(c0, c0 + W // parts)
-                nc.scalar.activation(r[:, cols], acc[:, cols], ACT.Abs_reciprocal_sqrt, bias=1.0)
-                nc.scalar.activation(r2[:, cols], r[:, cols], ACT.Square)
+            n = W // parts
+            for c0 in range(0, W, n):
+                nc.scalar.activation(r[:, c0 : c0 + n], acc[:, c0 : c0 + n], ACT.Abs_reciprocal_sqrt, bias=1.0)
+                nc.scalar.activation(r2[:, c0 : c0 + n], r[:, c0 : c0 + n], ACT.Square)
             rec[(t, j)] = r2
 
-        def drive_part(t, j, tag, parts=1):
-            acc = psum.tile([P, W], F32, name="drive", tag="drive", bufs=2)
-            for h in (j, 1 - j):
+        def drive_part(t, j, bank):
+            acc = psum.tile([P, W], F32, name=f"drive{t}{j}", tag=bank)
+            for h in (1, 0):
                 c, s = eq[(h, j)]
                 wc, ws = wq[f"d{h}"]
                 nc.tensor.matmul_mx(
@@ -226,21 +246,22 @@ def tile_list_contrast_gain_control_kernel(
                     lhsT_scale=ws[:, t * P : (t + 1) * P],
                     rhs=c[:].bitcast(FP8X4),
                     rhs_scale=s[:],
-                    start=(h == j),
-                    stop=(h != j),
+                    start=(h == 1),
+                    stop=(h == 0),
                 )
-            y = keep.tile([P, W], F32, name=f"y{t}{j}", tag=tag, align_bytes=64)
-            ys[(t, j)] = y
-            for c0 in range(0, W, W // parts):
-                cols = slice(c0, c0 + W // parts)
-                nc.vector.tensor_tensor(y[:, cols], acc[:, cols], rec[(t, j)][:, cols], ALU.mult)
+            drives[(t, j)] = acc
 
-        def scatter(t, j, c0=0, c1=W):
+        def divide(t, j, tag, c0=0, n=W):
+            if c0 == 0:
+                ys[(t, j)] = keep.tile([P, W], F32, name=f"y{t}{j}", tag=tag, align_bytes=64)
+            nc.vector.tensor_tensor(ys[(t, j)][:, c0 : c0 + n], drives[(t, j)][:, c0 : c0 + n], rec[(t, j)][:, c0 : c0 + n], ALU.mult)
+
+        def scatter(t, j, c0=0, n=W):
             tile, row = wg[(t, j)]
             nc.vector.tensor_tensor(
-                pages[t][:].indirect(idx2[:, (j * W + c0) // 16 : (j * W + c1) // 16]),
-                ys[(t, j)][:, c0:c1],
-                tile[:, row, c0:c1],
+                pages[t][:].indirect(idx2[:, (j * W + c0) // 16 : (j * W + c0 + n) // 16]),
+                ys[(t, j)][:, c0 : c0 + n],
+                tile[:, row, c0 : c0 + n],
                 ALU.mult,
             )
 
@@ -266,94 +287,121 @@ def tile_list_contrast_gain_control_kernel(
 
         def quant_y(c):
             codes = keep.tile([P, CUTS[c + 1] - CUTS[c]], U32, name=f"ycodes{c}", align_bytes=64)
-            nc.vector.quantize_mx(out=codes[:].bitcast(FP8X4), scales=yscales[:, CUTS[c] : CUTS[c + 1]], in_=yil[c][:])
+            g, c0 = divmod(CUTS[c], W)
+            plane = yscales[4 * g : P, c0 : c0 + CUTS[c + 1] - CUTS[c]]
+            nc.vector.quantize_mx(out=codes[:].bitcast(FP8X4), scales=plane, in_=yil[c][:])
             nc.sync.dma_start(out=words_out[:, CUTS[c] : CUTS[c + 1]], in_=codes[:].bitcast(I32))
 
         nc.vector.memset(tabs[:].bitcast(I32), 0)
         nc.vector.memset(wps_raw[:].rearrange("p a c -> p (a c)").bitcast(I32), 0)
-        nc.gpsimd.memset(tiny[:], 2.0**-100)
+        nc.vector.memset(tiny[:], 2.0**-100)
+        nc.sync.dma_start(out=g_sb[:], in_=gain.rearrange("(a p t) -> p a t", a=2, t=4))
+        nc.sync.dma_start(out=wpw_raw[:].bitcast(I32), in_=wp_words.rearrange("a p c -> p a c").bitcast(I32))
+        load_w("w00", w1, 0, 0, ["R0"])
+        load_tabs()
+        nc.sync.dma_start(idx[:], offs)
+        load_w("w10", w1, 1, 0, ["R1"])
+        load_wps()
+        load_tab(0, "T0")
+        load_w("w01", w1, 0, 1, ["R2"])
+        root_gain()
         clear_page(0, "page0")
         clear_page(1, "page1")
-        nc.sync.dma_start(idx[:], offs)
-        nc.sync.dma_start(out=g_sb[:], in_=gain.rearrange("(a p t) -> p a t", a=2, t=4))
-        nc.sync.dma_start(idx2[:], offs2)
-        nc.sync.dma_start(out=wpw_raw[:].bitcast(I32), in_=wp_words.rearrange("a p c -> p a c").bitcast(I32))
-        load_w("w00", w1, 0, 0, "rawA")
-        load_tabs()
-        root_gain()
-        load_tab(0, "tab0")
         deal_wpw()
-        load_w("w10", w1, 1, 0, "rawB")
-        load_wps()
-        cast_w("w00", "s", "rawC")
-        load_tab(1, "rawA")
+        clear_page(2, "page2")
+        clear_page(3, "page3")
+        cast_w("w00", [("s", 0, 128)], "G0")
+        load_w("w11", w1, 1, 1, ["R0"])
+        load_tab(1, "T1")
         gather_s(0)
         gather_s(1)
-        gather_w(0, 0)
         quant_w("w00")
-        load_w("w01", w1, 0, 1, "rawC")
-        gather_w(0, 1)
-        load_w("w11", w1, 1, 1, "tab0")
         deal_wps()
-        cast_w("w10", "s", "grpA")
-        load_w("d0", wd, 0, 0, "rawB")
+        cast_w("w10", [("s", 0, 128)], "G1")
+        load_w("d0", wd, 0, 0, ["R1"])
+        gather_w(0, 0, 0, 512)
         quant_w("w10")
-        gather_w(1, 0)
-        lin(0, 0, 0, 512, "estA")
-        gather_w(1, 1)
-        load_w("d1", wd, 1, 0, "rawA")
-        cast_w("w01", "v", "grpB")
-        load_wg(0, 4, 0, "rawC", 1)
+        gather_w(0, 1, 0, 512)
+        load_w("d1", wd, 1, 0, ["T0"])
+        nc.sync.dma_start(idx2[:], offs2)
+        lin(0, 0, 0, 256, FIRST, "A")
+        cast_w("w01", [("s", 0, 64), ("v", 64, 128)], "G0")
         quant_w("w01")
-        lin(0, 1, 0, 512, "estC")
-        cast_w("w11", "v", "grpA")
-        load_wg(0, 4, 1, "tab0", 4)
+        load_wg(0, 1, 0, "R2", 1)
+        lin(1, 0, 0, 256, FIRST, "B")
+        cast_w("w11", [("s", 0, 64), ("v", 64, 128)], "G1")
         quant_w("w11")
-        lin(1, 0, 0, 256, "estB")
-        lin(1, 0, 256, 512, "estD")
-        weave_e(0, 0, 0, 512, "v", "grpA")
-        quant_e(0, 0, 0, 512)
-        cast_w("d0", "v", "estA")
-        weave_e(1, 0, 0, 256, "v", "eilB")
-        weave_e(1, 0, 256, 512, "v", "eilC")
+        gather_w(1, 0, 0, 256)
+        lin(0, 0, 0, 256, SECOND, "A")
+        lin(1, 0, 0, 256, SECOND, "B")
+        gather_w(1, 0, 256, 256)
+        gather_w(1, 1, 0, 512)
+        square(0, 0, 0, 256, "E0")
+        square(1, 0, 0, 256, "E1")
+        lin(0, 0, 256, 256, BOTH, "A")
+        lin(1, 0, 256, 256, BOTH, "B")
+        square(0, 0, 256, 512, "E2")
+        square(1, 0, 256, 512, "E3")
+        cast_w("d0", [("v", 0, 128)], "G0")
+        weave_e(0, 0, 0, 256, "v", "R1")
+        weave_e(1, 0, 0, 256, "v", "L1")
+        quant_e(0, 0, 0, 256)
         quant_e(1, 0, 0, 256)
+        weave_e(0, 0, 256, 512, "v", "L2")
+        weave_e(1, 0, 256, 512, "v", "L3")
+        quant_e(0, 0, 256, 512)
         quant_e(1, 0, 256, 512)
-        pool_part(0, 0, "rA", "q0", 2)
-        cast_w("d1", "s", "grpB")
-        quant_w("d0")
-        quant_w("d1")
-        drive_part(0, 0, "yA", 2)
-        clear_page(2, "grpB")
-        clear_page(3, "q0")
-        pool_part(1, 0, "rA", "q1")
-        scatter(0, 0, 0, 256)
-        drive_part(1, 0, "yB")
-        scatter(0, 0, 256, 512)
-        pool_part(2, 0, "rB", "q2")
-        pool_part(3, 0, "rA", "q3")
-        weave_e(0, 1, 0, 512, "s", "rA")
-        drive_part(2, 0, "yC")
+        cast_w("d1", [("s", 0, 96), ("v", 96, 128)], "G1")
+        quant_w("d0", 0, 1, "L3")
+        quant_w("d1", 0, 1)
+        pool_part(0, 0, "A0", "rA", "q0", 2)
+        drive_part(0, 0, "A1")
+        quant_w("d0", 1, 2)
+        quant_w("d1", 1, 2)
+        quant_w("d0", 2, 4)
+        quant_w("d1", 2, 4)
+        divide(0, 0, "yA", 0, 256)
+        divide(0, 0, "yA", 256, 256)
+        load_wg(1, 4, 0, "q0", 1)
+        pool_part(1, 0, "A2", "rB", "q1")
+        drive_part(1, 0, "A3")
+        scatter(0, 0)
+        divide(1, 0, "yB")
+        lin(0, 1, 0, 512, BOTH, "B")
+        pool_part(2, 0, "A0", "rC", "q2")
+        drive_part(2, 0, "A1")
+        divide(2, 0, "yA")
+        square(0, 1, 0, 512, "rA")
+        lin(1, 1, 0, 512, BOTH, "B")
+        square(1, 1, 0, 512, "E2")
+        pool_part(3, 0, "A2", "rD", "q3")
+        weave_e(0, 1, 0, 512, "s", "L0")
+        load_wg(0, 4, 1, "R0", 4)
+        weave_e(1, 1, 0, 512, "s", "L1")
         scatter(1, 0)
-        quant_e(0, 1, 0, 512, "yB")
-        lin(1, 1, 0, 512, "rB")
-        weave_e(1, 1, 0, 512, "s", "eilA")
         scatter(2, 0)
-        quant_e(1, 1, 0, 512, "yC")
-        drive_part(3, 0, "eilA")
-        pool_part(0, 1, "rD", "q4")
-        pool_part(1, 1, "rC", "q1")
-        pool_part(2, 1, "rE", "q2")
-        pool_part(3, 1, "rC", "q3")
+        quant_e(0, 1, 0, 512, "yA")
+        quant_e(1, 1, 0, 512)
+        drive_part(3, 0, "B3")
+        divide(3, 0, "L1")
+        pool_part(0, 1, "B0", "rB", "q4")
         scatter(3, 0)
-        drive_part(0, 1, "eilA")
+        pool_part(1, 1, "B1", "rC", "q1")
+        pool_part(2, 1, "B2", "rB", "q2")
+        pool_part(3, 1, "A0", "rC", "q3")
+        drive_part(0, 1, "A1")
+        drive_part(1, 1, "A2")
+        drive_part(2, 1, "A3")
+        drive_part(3, 1, "B3")
+        divide(0, 1, "yC")
+        divide(1, 1, "yB")
         scatter(0, 1)
         finish_page(0)
-        drive_part(1, 1, "rE")
-        drive_part(2, 1, "yD")
+        divide(2, 1, "yC")
         scatter(1, 1)
         finish_page(1)
+        divide(3, 1, "yB")
         scatter(2, 1)
-        drive_part(3, 1, "yD")
         finish_page(2)
         scatter(3, 1)
         finish_page(3)
@@ -365,10 +413,11 @@ def tile_list_contrast_gain_control_kernel(
         weave_y(3, "v")
         quant_y(2)
         weave_y(4, "s")
+        weave_y(5, "s")
         quant_y(3)
         quant_y(4)
+        quant_y(5)
+        scales_out = out_2[0].bitcast(I32).rearrange("r (g m) -> g r m", g=4)
         for q in range(4):
             eng = nc.sync if q % 2 == 0 else nc.scalar
-            eng.dma_start(
-                out=out_2[0, 4 * q : 4 * q + 4, :].bitcast(I32), in_=yscales[32 * q : 32 * q + 4, :].bitcast(I32)
-            )
+            eng.dma_start(out=scales_out[:, 4 * q : 4 * q + 4, :], in_=yscales[32 * q : 32 * q + 16, :].bitcast(I32))

@@ -23,6 +23,7 @@ NC = len(CUTS) - 1
 FIRST = [(t, 0) for t in range(4)]
 SECOND = [(t, 1) for t in range(4)]
 BOTH = [(t, a) for t in range(4) for a in range(2)]
+LATE = [(t, a) for t in range(4) for a in (1, 0)]
 
 
 def tile_list_contrast_gain_control_kernel(
@@ -37,7 +38,7 @@ def tile_list_contrast_gain_control_kernel(
         idx2 = keep.tile([P, S // 16], U16, name="idx2")
         tabs = keep.tile([P, T], U8, name="tabs", tag="q_w00", align_bytes=64)
         wps_raw = keep.tile([P, 2, N], U8, name="wps_raw", tag="q_w10", align_bytes=64)
-        wpw_raw = keep.tile([P, 2, 2 * N], U8, name="wpw_raw", tag="page2", align_bytes=64)
+        wpw_raw = keep.tile([P, 2, 2 * N], U8, name="wpw_raw", align_bytes=64)
         g_sb = keep.tile([P, 2, 4], F32, name="g_sb")
         sg = keep.tile([P, 2, 4], F32, name="sg")
         tiny = keep.tile([P, 1], F32, name="tiny")
@@ -46,6 +47,7 @@ def tile_list_contrast_gain_control_kernel(
         yscales = keep.tile([P, W], U8, name="yscales", align_bytes=64)
         pages = {}
         accs = {}
+        sliced = {}
         drives = {}
         tabw = {}
         raws = {}
@@ -72,15 +74,12 @@ def tile_list_contrast_gain_control_kernel(
 
         def clear_page(t, tag):
             pages[t] = keep.tile([P, T2], F32, name=f"page{t}", tag=tag, align_bytes=64)
-            if t < 2:
-                nc.vector.memset(pages[t][:].bitcast(I32), 0)
-            else:
-                for c in range(4):
-                    nc.gpsimd.memset(pages[t][:, c * W : (c + 1) * W].bitcast(I32), 0)
+            for c in range(4):
+                nc.gpsimd.memset(pages[t][:, c * W : (c + 1) * W].bitcast(I32), 0)
 
         def root_gain():
             r, s0, sq, rest = [keep.tile([P, 2, 4], F32, name=f"root{n}") for n in range(4)]
-            fix = keep.tile([P, 2, 4], F32, name="fix", tag="page3", align_bytes=64)
+            fix = keep.tile([P, 2, 4], F32, name="fix")
             nc.scalar.activation(r[:], g_sb[:], ACT.Abs_reciprocal_sqrt, bias=tiny[:])
             nc.vector.tensor_tensor(s0[:], g_sb[:], r[:], ALU.mult)
             nc.vector.tensor_tensor(sq[:], s0[:], s0[:], ALU.mult)
@@ -117,16 +116,12 @@ def tile_list_contrast_gain_control_kernel(
                     in_=wp_scales[:, 4 * q : 4 * q + 4, :].rearrange("a r c -> r a c").bitcast(I32),
                 )
 
-        def load_wg(t0, t1, j, tag, step):
-            tile = keep.tile([P, t1 - t0, W], F32, name=f"wg{t0}{j}", tag=tag, align_bytes=64)
-            for t in range(t0, t1, step):
+        def load_wg(units, tag):
+            tile = keep.tile([P, len(units), W], F32, name=f"wg{units[0][0]}{units[0][1]}", tag=tag, align_bytes=64)
+            for row, (t, j) in enumerate(units):
                 for q in (0, 2, 1, 3):
-                    nc.sync.dma_start(
-                        out=tile[32 * q : 32 * q + 32, t - t0 : t - t0 + step, :],
-                        in_=wgq[:, t : t + step, j * W : (j + 1) * W],
-                    )
-            for t in range(t0, t1):
-                wg[(t, j)] = (tile, t - t0)
+                    nc.sync.dma_start(out=tile[32 * q : 32 * q + 32, row, :], in_=wgq[:, t, j * W : (j + 1) * W])
+                wg[(t, j)] = (tile, row)
 
         def cast_w(key, shares, tag):
             g = keep.tile([P, 4 * W], BF16, name="grp_" + key, tag=tag, align_bytes=64)
@@ -137,16 +132,25 @@ def tile_list_contrast_gain_control_kernel(
                 copy_on(eng, o[:, m0:m1], i[:, m0 % per : m0 % per + m1 - m0])
             grouped[key] = g
 
+        def cast_slices(key, t0, t1, eng, tag):
+            g = keep.tile([P, (t1 - t0) * W], BF16, name=f"grp_{key}{t0}", tag=tag, align_bytes=64)
+            o = g[:].rearrange("p (t m i) -> p m t i", t=t1 - t0, i=4)
+            i = raws[key][0][:].rearrange("p i (m t) -> p m t i", t=4)[:, :, t0:t1, :]
+            copy_on(eng, o, i)
+            for t in range(t0, t1):
+                sliced[(key, t)] = (g, t0)
+
         def quant_w(key, t0=0, t1=4, tag=None):
             if key not in wq:
                 codes = keep.tile([P, W], U32, name=f"q_{key}_c", tag=tag or "q_" + key, align_bytes=64)
                 scales = keep.tile([P, W], U8, name=f"q_{key}_s", align_bytes=64)
                 wq[key] = (codes, scales)
             codes, scales = wq[key]
+            g, first = sliced[(key, t0)] if (key, t0) in sliced else (grouped[key], 0)
             nc.vector.quantize_mx(
                 out=codes[:, t0 * P : t1 * P].bitcast(FP8X4),
                 scales=scales[:, t0 * P : t1 * P],
-                in_=grouped[key][:, t0 * W : t1 * W],
+                in_=g[:, (t0 - first) * W : (t1 - first) * W],
             )
 
         def gather_w(a, j, c0, n, tag=None):
@@ -161,11 +165,11 @@ def tile_list_contrast_gain_control_kernel(
             nc.vector.tensor_copy(g[:], tabs[:].indirect(idx[:, 32 * j : 32 * j + 32]))
             gs[j] = g
 
-        def lin(h, j, c0, n, passes, bank):
+        def lin(h, j, c0, n, passes, bank, opens=0):
             for t, a in passes:
                 c, s = wq[f"w{a}{h}"]
                 g, g0 = gw[(a, j, c0)]
-                if a == 0:
+                if a == opens:
                     accs[(h, j, c0, t)] = psum.tile([P, n], F32, name=f"lin{h}{j}{c0}{t}", tag=f"{bank}{t}")
                 nc.tensor.matmul_mx(
                     out=accs[(h, j, c0, t)][:],
@@ -173,8 +177,8 @@ def tile_list_contrast_gain_control_kernel(
                     lhsT_scale=s[:, t * P : (t + 1) * P],
                     rhs=g[:, g0 : g0 + n].bitcast(FP8X4),
                     rhs_scale=gs[j][4 * a : P, c0 : c0 + n],
-                    start=(a == 0),
-                    stop=(a == 1),
+                    start=(a == opens),
+                    stop=(a != opens),
                 )
 
         def square(h, j, c0, c1, tag):
@@ -183,14 +187,16 @@ def tile_list_contrast_gain_control_kernel(
                 nc.scalar.activation(st[:, t, :], accs[(h, j, c0, t)][:], ACT.Square, scale=sg[:, h, t : t + 1])
             est[(h, j, c0)] = st
 
-        def weave_e(h, j, c0, c1, eng, tag):
-            il = keep.tile([P, 4 * (c1 - c0)], BF16, name=f"eil{h}{j}{c0}", tag=tag, align_bytes=64)
+        def weave_e(h, j, c0, c1, eng, tag, base=None):
+            if base is None:
+                eil[(h, j, c0)] = keep.tile([P, 4 * W], BF16, name=f"eil{h}{j}{c0}", tag=tag, align_bytes=64)
+                base = c0
+            il = eil[(h, j, base)][:, 4 * (c0 - base) : 4 * (c1 - base)]
             copy_on(
                 eng,
-                il[:].rearrange("p (c i t) -> p c t i", i=4, t=4),
+                il.rearrange("p (c i t) -> p c t i", i=4, t=4),
                 est[(h, j, c0)][:].rearrange("p t (c i) -> p c t i", i=4),
             )
-            eil[(h, j, c0)] = il
 
         def quant_e(h, j, c0, c1, tag=None):
             if (h, j) not in eq:
@@ -198,7 +204,7 @@ def tile_list_contrast_gain_control_kernel(
                 scales = keep.tile([P, W], U8, name=f"q_e{h}{j}_s", align_bytes=64)
                 eq[(h, j)] = (codes, scales)
             codes, scales = eq[(h, j)]
-            nc.vector.quantize_mx(out=codes[:, c0:c1].bitcast(FP8X4), scales=scales[:, c0:c1], in_=eil[(h, j, c0)][:])
+            nc.vector.quantize_mx(out=codes[:, c0:c1].bitcast(FP8X4), scales=scales[:, c0:c1], in_=eil[(h, j, c0)][:, : 4 * (c1 - c0)])
 
         def deal_wpw():
             for a in range(2):
@@ -215,7 +221,7 @@ def tile_list_contrast_gain_control_kernel(
 
         def pool_part(t, j, bank, tag, tag2, parts=1):
             acc = psum.tile([P, W], F32, name=f"pool{t}{j}", tag=bank)
-            order = (0, 1) if (t, j) == (0, 0) else (1, 0)
+            order = (0, 1) if t < 2 else (1, 0)
             for h in order:
                 c, s = eq[(h, j)]
                 nc.tensor.matmul_mx(
@@ -237,7 +243,8 @@ def tile_list_contrast_gain_control_kernel(
 
         def drive_part(t, j, bank):
             acc = psum.tile([P, W], F32, name=f"drive{t}{j}", tag=bank)
-            for h in (1, 0):
+            order = (0, 1) if (t, j) == (0, 0) else (1, 0)
+            for h in order:
                 c, s = eq[(h, j)]
                 wc, ws = wq[f"d{h}"]
                 nc.tensor.matmul_mx(
@@ -246,8 +253,8 @@ def tile_list_contrast_gain_control_kernel(
                     lhsT_scale=ws[:, t * P : (t + 1) * P],
                     rhs=c[:].bitcast(FP8X4),
                     rhs_scale=s[:],
-                    start=(h == 1),
-                    stop=(h == 0),
+                    start=(h == order[0]),
+                    stop=(h == order[1]),
                 )
             drives[(t, j)] = acc
 
@@ -300,10 +307,10 @@ def tile_list_contrast_gain_control_kernel(
         load_w("w00", w1, 0, 0, ["R0"])
         load_tabs()
         nc.sync.dma_start(idx[:], offs)
-        load_w("w10", w1, 1, 0, ["R1"])
-        load_wps()
         load_tab(0, "T0")
-        load_w("w01", w1, 0, 1, ["R2"])
+        load_wps()
+        load_w("w10", w1, 1, 0, ["R1"])
+        load_tab(1, "T1")
         root_gain()
         clear_page(0, "page0")
         clear_page(1, "page1")
@@ -311,93 +318,96 @@ def tile_list_contrast_gain_control_kernel(
         clear_page(2, "page2")
         clear_page(3, "page3")
         cast_w("w00", [("s", 0, 128)], "G0")
-        load_w("w11", w1, 1, 1, ["R0"])
-        load_tab(1, "T1")
+        load_w("w01", w1, 0, 1, ["R0"])
+        load_w("w11", w1, 1, 1, ["R2"])
         gather_s(0)
         gather_s(1)
         quant_w("w00")
-        deal_wps()
-        cast_w("w10", [("s", 0, 128)], "G1")
-        load_w("d0", wd, 0, 0, ["R1"])
         gather_w(0, 0, 0, 512)
-        quant_w("w10")
         gather_w(0, 1, 0, 512)
+        deal_wps()
+        cast_w("w10", [("s", 0, 96), ("v", 96, 128)], "G1")
+        load_w("d0", wd, 0, 0, ["R1"])
         load_w("d1", wd, 1, 0, ["T0"])
         nc.sync.dma_start(idx2[:], offs2)
         lin(0, 0, 0, 256, FIRST, "A")
-        cast_w("w01", [("s", 0, 64), ("v", 64, 128)], "G0")
+        lin(0, 0, 256, 256, FIRST, "B")
+        quant_w("w10")
+        gather_w(1, 0, 0, 256)
+        lin(0, 0, 0, 256, SECOND, "A")
+        gather_w(1, 0, 256, 256)
+        lin(0, 0, 256, 256, SECOND, "B")
+        gather_w(1, 1, 0, 512)
+        load_wg([(0, 0)], "T1")
+        square(0, 0, 0, 256, "E0")
+        square(0, 0, 256, 512, "E2")
+        cast_w("w01", [("v", 0, 128)], "G0")
         quant_w("w01")
-        load_wg(0, 1, 0, "R2", 1)
         lin(1, 0, 0, 256, FIRST, "B")
         cast_w("w11", [("s", 0, 64), ("v", 64, 128)], "G1")
         quant_w("w11")
-        gather_w(1, 0, 0, 256)
-        lin(0, 0, 0, 256, SECOND, "A")
         lin(1, 0, 0, 256, SECOND, "B")
-        gather_w(1, 0, 256, 256)
-        gather_w(1, 1, 0, 512)
-        square(0, 0, 0, 256, "E0")
+        lin(1, 0, 256, 256, LATE, "A", 1)
+        weave_e(0, 0, 0, 256, "s", "R2")
         square(1, 0, 0, 256, "E1")
-        lin(0, 0, 256, 256, BOTH, "A")
-        lin(1, 0, 256, 256, BOTH, "B")
-        square(0, 0, 256, 512, "E2")
         square(1, 0, 256, 512, "E3")
+        weave_e(0, 0, 256, 512, "v", "G1")
         cast_w("d0", [("v", 0, 128)], "G0")
-        weave_e(0, 0, 0, 256, "v", "R1")
         weave_e(1, 0, 0, 256, "v", "L1")
-        quant_e(0, 0, 0, 256)
-        quant_e(1, 0, 0, 256)
-        weave_e(0, 0, 256, 512, "v", "L2")
-        weave_e(1, 0, 256, 512, "v", "L3")
+        quant_e(0, 0, 0, 256, "R1")
         quant_e(0, 0, 256, 512)
+        weave_e(1, 0, 256, 512, "v", "L3")
+        quant_e(1, 0, 0, 256, "E3")
         quant_e(1, 0, 256, 512)
-        cast_w("d1", [("s", 0, 96), ("v", 96, 128)], "G1")
-        quant_w("d0", 0, 1, "L3")
+        cast_slices("d1", 0, 3, "s", "G2")
+        quant_w("d0", 0, 1, "L1")
         quant_w("d1", 0, 1)
-        pool_part(0, 0, "A0", "rA", "q0", 2)
-        drive_part(0, 0, "A1")
+        pool_part(0, 0, "B0", "rA", "q0", 2)
+        drive_part(0, 0, "B1")
         quant_w("d0", 1, 2)
         quant_w("d1", 1, 2)
         quant_w("d0", 2, 4)
-        quant_w("d1", 2, 4)
+        cast_slices("d1", 3, 4, "v", "L3")
+        quant_w("d1", 2, 3)
+        quant_w("d1", 3, 4)
         divide(0, 0, "yA", 0, 256)
         divide(0, 0, "yA", 256, 256)
-        load_wg(1, 4, 0, "q0", 1)
-        pool_part(1, 0, "A2", "rB", "q1")
-        drive_part(1, 0, "A3")
+        load_wg([(1, 0), (2, 0)], "q0")
+        pool_part(1, 0, "B2", "rB", "q1")
+        drive_part(1, 0, "B3")
         scatter(0, 0)
         divide(1, 0, "yB")
-        lin(0, 1, 0, 512, BOTH, "B")
-        pool_part(2, 0, "A0", "rC", "q2")
-        drive_part(2, 0, "A1")
+        lin(0, 1, 0, 512, BOTH, "A")
+        pool_part(2, 0, "B0", "rC", "q2")
+        drive_part(2, 0, "B1")
         divide(2, 0, "yA")
         square(0, 1, 0, 512, "rA")
-        lin(1, 1, 0, 512, BOTH, "B")
+        lin(1, 1, 0, 512, BOTH, "A")
         square(1, 1, 0, 512, "E2")
-        pool_part(3, 0, "A2", "rD", "q3")
+        pool_part(3, 0, "B2", "rD", "q3")
         weave_e(0, 1, 0, 512, "s", "L0")
-        load_wg(0, 4, 1, "R0", 4)
-        weave_e(1, 1, 0, 512, "s", "L1")
+        load_wg([(3, 0), (0, 1), (1, 1), (2, 1), (3, 1)], "rA")
+        weave_e(1, 1, 0, 512, "s", "L4")
         scatter(1, 0)
         scatter(2, 0)
-        quant_e(0, 1, 0, 512, "yA")
+        quant_e(0, 1, 0, 512)
+        drive_part(3, 0, "A3")
+        divide(3, 0, "yB")
         quant_e(1, 1, 0, 512)
-        drive_part(3, 0, "B3")
-        divide(3, 0, "L1")
-        pool_part(0, 1, "B0", "rB", "q4")
+        pool_part(0, 1, "A0", "rB", "q4")
         scatter(3, 0)
-        pool_part(1, 1, "B1", "rC", "q1")
-        pool_part(2, 1, "B2", "rB", "q2")
-        pool_part(3, 1, "A0", "rC", "q3")
-        drive_part(0, 1, "A1")
-        drive_part(1, 1, "A2")
-        drive_part(2, 1, "A3")
-        drive_part(3, 1, "B3")
+        pool_part(1, 1, "A1", "rC", "q1")
+        pool_part(2, 1, "A2", "rB", "q2")
+        pool_part(3, 1, "B0", "rC", "q3")
+        drive_part(0, 1, "B1")
+        drive_part(1, 1, "B2")
+        drive_part(2, 1, "B3")
+        drive_part(3, 1, "A3")
         divide(0, 1, "yC")
-        divide(1, 1, "yB")
+        divide(1, 1, "yD")
         scatter(0, 1)
         finish_page(0)
-        divide(2, 1, "yC")
+        divide(2, 1, "yA")
         scatter(1, 1)
         finish_page(1)
         divide(3, 1, "yB")
@@ -419,5 +429,4 @@ def tile_list_contrast_gain_control_kernel(
         quant_y(5)
         scales_out = out_2[0].bitcast(I32).rearrange("r (g m) -> g r m", g=4)
         for q in range(4):
-            eng = nc.sync if q % 2 == 0 else nc.scalar
-            eng.dma_start(out=scales_out[:, 4 * q : 4 * q + 4, :], in_=yscales[32 * q : 32 * q + 16, :].bitcast(I32))
+            nc.sync.dma_start(out=scales_out[:, 4 * q : 4 * q + 4, :], in_=yscales[32 * q : 32 * q + 16, :].bitcast(I32))

@@ -74,8 +74,8 @@ def tile_list_contrast_gain_control_kernel(
 
         def clear_page(t, tag):
             pages[t] = keep.tile([P, T2], F32, name=f"page{t}", tag=tag, align_bytes=64)
-            for c in range(4):
-                nc.gpsimd.memset(pages[t][:, c * W : (c + 1) * W].bitcast(I32), 0)
+            eng = nc.vector if t == 0 else nc.gpsimd
+            eng.memset(pages[t][:].bitcast(I32), 0)
 
         def root_gain():
             r, s0, sq, rest = [keep.tile([P, 2, 4], F32, name=f"root{n}") for n in range(4)]
@@ -313,10 +313,7 @@ def tile_list_contrast_gain_control_kernel(
         load_tab(1, "T1")
         root_gain()
         clear_page(0, "page0")
-        clear_page(1, "page1")
         deal_wpw()
-        clear_page(2, "page2")
-        clear_page(3, "page3")
         cast_w("w00", [("s", 0, 128)], "G0")
         load_w("w01", w1, 0, 1, ["R0"])
         load_w("w11", w1, 1, 1, ["R2"])
@@ -370,6 +367,7 @@ def tile_list_contrast_gain_control_kernel(
         cast_slices("d1", 3, 4, "v", "L3")
         quant_w("d1", 2, 3)
         quant_w("d1", 3, 4)
+        clear_page(1, "L3")
         divide(0, 0, "yA", 0, 256)
         divide(0, 0, "yA", 256, 256)
         load_wg([(1, 0), (2, 0)], "q0")
@@ -377,10 +375,12 @@ def tile_list_contrast_gain_control_kernel(
         drive_part(1, 0, "B3")
         scatter(0, 0)
         divide(1, 0, "yB")
+        clear_page(2, "q1")
         lin(0, 1, 0, 512, BOTH, "A")
         pool_part(2, 0, "B0", "rC", "q2")
         drive_part(2, 0, "B1")
         divide(2, 0, "yA")
+        clear_page(3, "q2")
         square(0, 1, 0, 512, "rA")
         lin(1, 1, 0, 512, BOTH, "A")
         square(1, 1, 0, 512, "E2")
@@ -396,8 +396,8 @@ def tile_list_contrast_gain_control_kernel(
         quant_e(1, 1, 0, 512)
         pool_part(0, 1, "A0", "rB", "q4")
         scatter(3, 0)
-        pool_part(1, 1, "A1", "rC", "q1")
-        pool_part(2, 1, "A2", "rB", "q2")
+        pool_part(1, 1, "A1", "rC", "q5")
+        pool_part(2, 1, "A2", "rB", "q6")
         pool_part(3, 1, "B0", "rC", "q3")
         drive_part(0, 1, "B1")
         drive_part(1, 1, "B2")
@@ -410,7 +410,7 @@ def tile_list_contrast_gain_control_kernel(
         divide(2, 1, "yA")
         scatter(1, 1)
         finish_page(1)
-        divide(3, 1, "yB")
+        divide(3, 1, "yD")
         scatter(2, 1)
         finish_page(2)
         scatter(3, 1)

@@ -78,14 +78,15 @@ def tile_list_contrast_gain_control_kernel(
             eng.memset(pages[t][:].bitcast(I32), 0)
 
         def root_gain():
-            r, s0, sq, rest = [keep.tile([P, 2, 4], F32, name=f"root{n}") for n in range(4)]
+            r, s0, sq, rest, half = [keep.tile([P, 2, 4], F32, name=f"root{n}") for n in range(5)]
             fix = keep.tile([P, 2, 4], F32, name="fix")
             nc.scalar.activation(r[:], g_sb[:], ACT.Abs_reciprocal_sqrt, bias=tiny[:])
-            nc.vector.tensor_tensor(s0[:], g_sb[:], r[:], ALU.mult)
-            nc.vector.tensor_tensor(sq[:], s0[:], s0[:], ALU.mult)
-            nc.vector.tensor_tensor(rest[:], g_sb[:], sq[:], ALU.subtract)
-            nc.vector.scalar_tensor_tensor(fix[:], rest[:], 0.5, r[:], ALU.mult, ALU.mult)
-            nc.vector.tensor_tensor(sg[:], s0[:], fix[:], ALU.add)
+            nc.gpsimd.tensor_tensor(s0[:], g_sb[:], r[:], ALU.mult)
+            nc.gpsimd.tensor_tensor(sq[:], s0[:], s0[:], ALU.mult)
+            nc.gpsimd.tensor_tensor(rest[:], g_sb[:], sq[:], ALU.subtract)
+            nc.gpsimd.tensor_scalar(half[:], r[:], 0.5, 0.0, ALU.mult, ALU.add)
+            nc.gpsimd.tensor_tensor(fix[:], rest[:], half[:], ALU.mult)
+            nc.gpsimd.tensor_tensor(sg[:], s0[:], fix[:], ALU.add)
 
         def load_w(key, src, a, h, tags):
             n = W // len(tags)
@@ -209,14 +210,14 @@ def tile_list_contrast_gain_control_kernel(
         def deal_wpw():
             for a in range(2):
                 nc.vector.tensor_copy(
-                    out=wpw[:, a, :].rearrange("p (t m b) -> p m t b", t=4, b=2),
-                    in_=wpw_raw[:, a, :].rearrange("p (m t b) -> p m t b", t=4, b=2),
+                    out=wpw[:, a, :].rearrange("p (t m b) -> p t m b", t=4, b=2),
+                    in_=wpw_raw[:, a, :].rearrange("p (m t b) -> p t m b", t=4, b=2),
                 )
 
         def deal_wps():
             nc.vector.tensor_copy(
-                out=wps[:].rearrange("p a (t m) -> p a m t", t=4),
-                in_=wps_raw[:].rearrange("p a (m t) -> p a m t", t=4),
+                out=wps[:].rearrange("p a (t m) -> p a t m", t=4),
+                in_=wps_raw[:].rearrange("p a (m t) -> p a t m", t=4),
             )
 
         def pool_part(t, j, bank, tag, tag2, parts=1):
@@ -304,9 +305,9 @@ def tile_list_contrast_gain_control_kernel(
         nc.vector.memset(tiny[:], 2.0**-100)
         nc.sync.dma_start(out=g_sb[:], in_=gain.rearrange("(a p t) -> p a t", a=2, t=4))
         nc.sync.dma_start(out=wpw_raw[:].bitcast(I32), in_=wp_words.rearrange("a p c -> p a c").bitcast(I32))
-        load_w("w00", w1, 0, 0, ["R0"])
         load_tabs()
         nc.sync.dma_start(idx[:], offs)
+        load_w("w00", w1, 0, 0, ["R0"])
         load_tab(0, "T0")
         load_wps()
         load_w("w10", w1, 1, 0, ["R1"])
@@ -314,7 +315,7 @@ def tile_list_contrast_gain_control_kernel(
         root_gain()
         clear_page(0, "page0")
         deal_wpw()
-        cast_w("w00", [("s", 0, 128)], "G0")
+        cast_w("w00", [("s", 0, 64), ("v", 64, 128)], "G0")
         load_w("w01", w1, 0, 1, ["R0"])
         load_w("w11", w1, 1, 1, ["R2"])
         gather_s(0)
@@ -323,7 +324,7 @@ def tile_list_contrast_gain_control_kernel(
         gather_w(0, 0, 0, 512)
         gather_w(0, 1, 0, 512)
         deal_wps()
-        cast_w("w10", [("s", 0, 96), ("v", 96, 128)], "G1")
+        cast_w("w10", [("s", 0, 64), ("v", 64, 128)], "G1")
         load_w("d0", wd, 0, 0, ["R1"])
         load_w("d1", wd, 1, 0, ["T0"])
         nc.sync.dma_start(idx2[:], offs2)
@@ -341,7 +342,7 @@ def tile_list_contrast_gain_control_kernel(
         cast_w("w01", [("v", 0, 128)], "G0")
         quant_w("w01")
         lin(1, 0, 0, 256, FIRST, "B")
-        cast_w("w11", [("s", 0, 64), ("v", 64, 128)], "G1")
+        cast_w("w11", [("s", 0, 44), ("v", 44, 128)], "G1")
         quant_w("w11")
         lin(1, 0, 0, 256, SECOND, "B")
         lin(1, 0, 256, 256, LATE, "A", 1)

@@ -126,17 +126,17 @@ def tile_list_contrast_gain_control_kernel(
 
         def cast_w(key, shares, tag):
             g = keep.tile([P, 4 * W], BF16, name="grp_" + key, tag=tag, align_bytes=64)
-            o = g[:].rearrange("p (t m i) -> p m t i", t=4, i=4)
+            o = g[:].rearrange("p (t m i) -> p m i t", t=4, i=4)
             per = P // len(raws[key])
             for eng, m0, m1 in shares:
-                i = raws[key][m0 // per][:].rearrange("p i (m t) -> p m t i", t=4)
+                i = raws[key][m0 // per][:].rearrange("p i (m t) -> p m i t", t=4)
                 copy_on(eng, o[:, m0:m1], i[:, m0 % per : m0 % per + m1 - m0])
             grouped[key] = g
 
         def cast_slices(key, t0, t1, eng, tag):
             g = keep.tile([P, (t1 - t0) * W], BF16, name=f"grp_{key}{t0}", tag=tag, align_bytes=64)
-            o = g[:].rearrange("p (t m i) -> p m t i", t=t1 - t0, i=4)
-            i = raws[key][0][:].rearrange("p i (m t) -> p m t i", t=4)[:, :, t0:t1, :]
+            o = g[:].rearrange("p (t m i) -> p m i t", t=t1 - t0, i=4)
+            i = raws[key][0][:].rearrange("p i (m t) -> p m i t", t=4)[:, :, :, t0:t1]
             copy_on(eng, o, i)
             for t in range(t0, t1):
                 sliced[(key, t)] = (g, t0)
@@ -398,10 +398,10 @@ def tile_list_contrast_gain_control_kernel(
         pool_part(0, 1, "A0", "rB", "q4")
         scatter(3, 0)
         pool_part(1, 1, "A1", "rC", "q5")
-        pool_part(2, 1, "A2", "rB", "q6")
-        pool_part(3, 1, "B0", "rC", "q3")
         drive_part(0, 1, "B1")
         drive_part(1, 1, "B2")
+        pool_part(2, 1, "A2", "rB", "q6")
+        pool_part(3, 1, "B0", "rC", "q3")
         drive_part(2, 1, "B3")
         drive_part(3, 1, "A3")
         divide(0, 1, "yC")

@@ -18,8 +18,12 @@ ALU = mybir.AluOpType
 
 P = 128
 W = 512
-CUTS = (0, 256, 512, 1024, 1536, 1792, 2048)
+CUTS = (0, 512, 1024, 1536, 1792, 2048)
+OWN = 384
 NC = len(CUTS) - 1
+BANKS_A = ["A0", "A1", "A2", "A3"]
+BANKS_B = ["B0", "B1", "B2", "B3"]
+LATER = ["B3", "B2", "B1", "A2"]
 FIRST = [(t, 0) for t in range(4)]
 SECOND = [(t, 1) for t in range(4)]
 BOTH = [(t, a) for t in range(4) for a in range(2)]
@@ -32,12 +36,18 @@ def tile_list_contrast_gain_control_kernel(
     nc = tc.nc
     with ExitStack() as ctx:
         keep = ctx.enter_context(tc.tile_pool(name="keep", bufs=1))
+        shared = ctx.enter_context(tc.tile_pool(name="shared", bufs=1))
         psum = ctx.enter_context(tc.psum_pool(name="psum", bufs=1))
+
+        def place(shape, dtype, name, tag):
+            if isinstance(tag, int):
+                return shared.tile(shape, dtype, name=name, align_bytes=64, offset=tag)
+            return keep.tile(shape, dtype, name=name, tag=tag, align_bytes=64)
 
         idx = keep.tile([P, S // 16], U16, name="idx")
         idx2 = keep.tile([P, S // 16], U16, name="idx2")
-        tabs = keep.tile([P, T], U8, name="tabs", tag="q_w00", align_bytes=64)
-        wps_raw = keep.tile([P, 2, N], U8, name="wps_raw", tag="q_w10", align_bytes=64)
+        tabs = keep.tile([P, T], U8, name="tabs", tag="q_w00_0", align_bytes=64)
+        wps_raw = keep.tile([P, 2, N], U8, name="wps_raw", tag="q_w10_0", align_bytes=64)
         wpw_raw = keep.tile([P, 2, 2 * N], U8, name="wpw_raw", align_bytes=64)
         g_sb = keep.tile([P, 2, 4], F32, name="g_sb")
         sg = keep.tile([P, 2, 4], F32, name="sg")
@@ -45,6 +55,7 @@ def tile_list_contrast_gain_control_kernel(
         wpw = keep.tile([P, 2, 2 * N], U8, name="wpw", align_bytes=64)
         wps = keep.tile([P, 2, N], U8, name="wps", align_bytes=64)
         yscales = keep.tile([P, W], U8, name="yscales", align_bytes=64)
+        ycodes = keep.tile([P, T2], U32, name="ycodes", align_bytes=64)
         pages = {}
         accs = {}
         sliced = {}
@@ -92,7 +103,7 @@ def tile_list_contrast_gain_control_kernel(
             n = W // len(tags)
             raws[key] = []
             for u, tag in enumerate(tags):
-                raw = keep.tile([P, 4, n], F32, name=f"raw_{key}{u}", tag=tag, align_bytes=64)
+                raw = place([P, 4, n], F32, f"raw_{key}{u}", tag)
                 c0 = h * W + u * n
                 nc.sync.dma_start(
                     out=raw[:], in_=src[a * W : (a + 1) * W, c0 : c0 + n].rearrange("(p i) c -> p i c", i=4)
@@ -118,11 +129,16 @@ def tile_list_contrast_gain_control_kernel(
                 )
 
         def load_wg(units, tag):
-            tile = keep.tile([P, len(units), W], F32, name=f"wg{units[0][0]}{units[0][1]}", tag=tag, align_bytes=64)
+            tile = place([P, len(units), W], F32, f"wg{units[0][0]}{units[0][1]}", tag)
             for row, (t, j) in enumerate(units):
-                for q in (0, 2, 1, 3):
-                    nc.sync.dma_start(out=tile[32 * q : 32 * q + 32, row, :], in_=wgq[:, t, j * W : (j + 1) * W])
                 wg[(t, j)] = (tile, row)
+                if j == 1 and t % 2 == 1:
+                    continue
+                n = 1 + j
+                for q in (0, 2, 1, 3):
+                    nc.sync.dma_start(
+                        out=tile[32 * q : 32 * q + 32, row : row + n, :], in_=wgq[:, t : t + n, j * W : (j + 1) * W]
+                    )
 
         def cast_w(key, shares, tag):
             g = keep.tile([P, 4 * W], BF16, name="grp_" + key, tag=tag, align_bytes=64)
@@ -142,17 +158,13 @@ def tile_list_contrast_gain_control_kernel(
                 sliced[(key, t)] = (g, t0)
 
         def quant_w(key, t0=0, t1=4, tag=None):
-            if key not in wq:
-                codes = keep.tile([P, W], U32, name=f"q_{key}_c", tag=tag or "q_" + key, align_bytes=64)
-                scales = keep.tile([P, W], U8, name=f"q_{key}_s", align_bytes=64)
-                wq[key] = (codes, scales)
-            codes, scales = wq[key]
+            codes = place([P, (t1 - t0) * P], U32, f"q_{key}{t0}_c", f"q_{key}_{t0}" if tag is None else tag)
+            scales = keep.tile([P, (t1 - t0) * P], U8, name=f"q_{key}{t0}_s", align_bytes=64)
             g, first = sliced[(key, t0)] if (key, t0) in sliced else (grouped[key], 0)
-            nc.vector.quantize_mx(
-                out=codes[:, t0 * P : t1 * P].bitcast(FP8X4),
-                scales=scales[:, t0 * P : t1 * P],
-                in_=g[:, (t0 - first) * W : (t1 - first) * W],
-            )
+            nc.vector.quantize_mx(out=codes[:].bitcast(FP8X4), scales=scales[:], in_=g[:, (t0 - first) * W : (t1 - first) * W])
+            for t in range(t0, t1):
+                cols = slice((t - t0) * P, (t - t0 + 1) * P)
+                wq[(key, t)] = (codes[:, cols].bitcast(FP8X4), scales[:, cols])
 
         def gather_w(a, j, c0, n, tag=None):
             g = keep.tile([P, n], U32, name=f"gw{a}{j}{c0}", tag=tag or f"gw{a}{j}{c0}", align_bytes=64)
@@ -168,29 +180,29 @@ def tile_list_contrast_gain_control_kernel(
 
         def lin(h, j, c0, n, passes, bank, opens=0):
             for t, a in passes:
-                c, s = wq[f"w{a}{h}"]
+                c, s = wq[(f"w{a}{h}", t)]
                 g, g0 = gw[(a, j, c0)]
                 if a == opens:
-                    accs[(h, j, c0, t)] = psum.tile([P, n], F32, name=f"lin{h}{j}{c0}{t}", tag=f"{bank}{t}")
+                    accs[(h, j, c0, t)] = psum.tile([P, n], F32, name=f"lin{h}{j}{c0}{t}", tag=bank[t])
                 nc.tensor.matmul_mx(
                     out=accs[(h, j, c0, t)][:],
-                    lhsT=c[:, t * P : (t + 1) * P].bitcast(FP8X4),
-                    lhsT_scale=s[:, t * P : (t + 1) * P],
+                    lhsT=c,
+                    lhsT_scale=s,
                     rhs=g[:, g0 : g0 + n].bitcast(FP8X4),
                     rhs_scale=gs[j][4 * a : P, c0 : c0 + n],
                     start=(a == opens),
                     stop=(a != opens),
                 )
 
-        def square(h, j, c0, c1, tag):
-            st = keep.tile([P, 4, c1 - c0], BF16, name=f"est{h}{j}{c0}", tag=tag, align_bytes=64)
-            for t in range(4):
-                nc.scalar.activation(st[:, t, :], accs[(h, j, c0, t)][:], ACT.Square, scale=sg[:, h, t : t + 1])
-            est[(h, j, c0)] = st
+        def square(h, j, c0, c1, tag, t0=0, t1=4):
+            if t0 == 0:
+                est[(h, j, c0)] = place([P, 4, c1 - c0], BF16, f"est{h}{j}{c0}", tag)
+            for t in range(t0, t1):
+                nc.scalar.activation(est[(h, j, c0)][:, t, :], accs[(h, j, c0, t)][:], ACT.Square, scale=sg[:, h, t : t + 1])
 
         def weave_e(h, j, c0, c1, eng, tag, base=None):
             if base is None:
-                eil[(h, j, c0)] = keep.tile([P, 4 * W], BF16, name=f"eil{h}{j}{c0}", tag=tag, align_bytes=64)
+                eil[(h, j, c0)] = place([P, 4 * W], BF16, f"eil{h}{j}{c0}", tag)
                 base = c0
             il = eil[(h, j, base)][:, 4 * (c0 - base) : 4 * (c1 - base)]
             copy_on(
@@ -201,7 +213,7 @@ def tile_list_contrast_gain_control_kernel(
 
         def quant_e(h, j, c0, c1, tag=None):
             if (h, j) not in eq:
-                codes = keep.tile([P, W], U32, name=f"q_e{h}{j}_c", tag=tag or f"q_e{h}{j}", align_bytes=64)
+                codes = place([P, W], U32, f"q_e{h}{j}_c", f"q_e{h}{j}" if tag is None else tag)
                 scales = keep.tile([P, W], U8, name=f"q_e{h}{j}_s", align_bytes=64)
                 eq[(h, j)] = (codes, scales)
             codes, scales = eq[(h, j)]
@@ -222,7 +234,7 @@ def tile_list_contrast_gain_control_kernel(
 
         def pool_part(t, j, bank, tag, tag2, parts=1):
             acc = psum.tile([P, W], F32, name=f"pool{t}{j}", tag=bank)
-            order = (0, 1) if t < 2 else (1, 0)
+            order = (0, 1) if t == 0 else (1, 0)
             for h in order:
                 c, s = eq[(h, j)]
                 nc.tensor.matmul_mx(
@@ -242,16 +254,56 @@ def tile_list_contrast_gain_control_kernel(
                 nc.scalar.activation(r2[:, c0 : c0 + n], r[:, c0 : c0 + n], ACT.Square)
             rec[(t, j)] = r2
 
+        def first_quarter(c0, banks):
+            n = W // 2
+            acc = psum.tile([P, n], F32, name=f"pool_q{c0}", tag=banks[0])
+            for m0 in range(0, n, P):
+                for h in range(2):
+                    c, s = eq[(h, 0)]
+                    nc.tensor.matmul_mx(
+                        out=acc[:, m0 : m0 + P],
+                        lhsT=wpw[:, h, : 2 * P].bitcast(FP4X4),
+                        lhsT_scale=wps[:, h, :P],
+                        rhs=c[:, c0 + m0 : c0 + m0 + P].bitcast(FP8X4),
+                        rhs_scale=s[:, c0 + m0 : c0 + m0 + P],
+                        start=(h == 0),
+                        stop=(h == 1),
+                    )
+            r = keep.tile([P, n], F32, name=f"r_q{c0}", tag="rA" if c0 == 0 else "rE", align_bytes=64)
+            rec[c0] = keep.tile([P, n], F32, name=f"rr_q{c0}", tag="q0" if c0 == 0 else "qE", align_bytes=64)
+            nc.scalar.activation(r[:], acc[:], ACT.Abs_reciprocal_sqrt, bias=1.0)
+            nc.scalar.activation(rec[c0][:], r[:], ACT.Square)
+            acc = psum.tile([P, n], F32, name=f"drive_q{c0}", tag=banks[1])
+            for h in range(2):
+                c, s = eq[(h, 0)]
+                wc, ws = wq[(f"d{h}", 0)]
+                nc.tensor.matmul_mx(
+                    out=acc[:],
+                    lhsT=wc,
+                    lhsT_scale=ws,
+                    rhs=c[:, c0 : c0 + n].bitcast(FP8X4),
+                    rhs_scale=s[:, c0 : c0 + n],
+                    start=(h == 0),
+                    stop=(h == 1),
+                )
+            drives[c0] = acc
+
+        def first_divide(c0):
+            n = W // 2
+            if c0 == 0:
+                ys[(0, 0)] = keep.tile([P, W], F32, name="y00", tag="yC", align_bytes=64)
+            nc.vector.tensor_tensor(ys[(0, 0)][:, c0 : c0 + n], drives[c0][:], rec[c0][:], ALU.mult)
+
         def drive_part(t, j, bank):
             acc = psum.tile([P, W], F32, name=f"drive{t}{j}", tag=bank)
             order = (0, 1) if (t, j) == (0, 0) else (1, 0)
             for h in order:
                 c, s = eq[(h, j)]
-                wc, ws = wq[f"d{h}"]
+                wc, ws = wq[(f"d{h}", t)]
                 nc.tensor.matmul_mx(
                     out=acc[:],
-                    lhsT=wc[:, t * P : (t + 1) * P].bitcast(FP8X4),
-                    lhsT_scale=ws[:, t * P : (t + 1) * P],
+                    lhsT=wc,
+                    lhsT_scale=ws,
                     rhs=c[:].bitcast(FP8X4),
                     rhs_scale=s[:],
                     start=(h == order[0]),
@@ -261,7 +313,7 @@ def tile_list_contrast_gain_control_kernel(
 
         def divide(t, j, tag, c0=0, n=W):
             if c0 == 0:
-                ys[(t, j)] = keep.tile([P, W], F32, name=f"y{t}{j}", tag=tag, align_bytes=64)
+                ys[(t, j)] = place([P, W], F32, f"y{t}{j}", tag)
             nc.vector.tensor_tensor(ys[(t, j)][:, c0 : c0 + n], drives[(t, j)][:, c0 : c0 + n], rec[(t, j)][:, c0 : c0 + n], ALU.mult)
 
         def scatter(t, j, c0=0, n=W):
@@ -275,13 +327,14 @@ def tile_list_contrast_gain_control_kernel(
 
         pairs = [keep.tile([P, 2, CUTS[c + 1] - CUTS[c], 2], BF16, name=f"pairs{c}") for c in range(NC)]
 
-        def round_page(t, c, eng):
-            copy_on(eng, pairs[c][:, t // 2, :, t % 2], pages[t][:, CUTS[c] : CUTS[c + 1]])
+        def round_page(t, c, eng, m0=0, m1=None):
+            m1 = m1 or CUTS[c + 1] - CUTS[c]
+            copy_on(eng, pairs[c][:, t // 2, m0:m1, t % 2], pages[t][:, CUTS[c] + m0 : CUTS[c] + m1])
 
         def finish_page(t):
             nc.sync.dma_start(out=out_rows[:, t, :], in_=pages[t][:])
             for c in range(NC):
-                round_page(t, c, "s")
+                round_page(t, c, "s", OWN if t >= 2 and c == 0 else 0)
 
         def weave_y(c, eng):
             il = keep.tile([P, 4 * (CUTS[c + 1] - CUTS[c])], BF16, name=f"yil{c}", align_bytes=64)
@@ -294,11 +347,18 @@ def tile_list_contrast_gain_control_kernel(
             yil[c] = il
 
         def quant_y(c):
-            codes = keep.tile([P, CUTS[c + 1] - CUTS[c]], U32, name=f"ycodes{c}", align_bytes=64)
-            g, c0 = divmod(CUTS[c], W)
-            plane = yscales[4 * g : P, c0 : c0 + CUTS[c + 1] - CUTS[c]]
-            nc.vector.quantize_mx(out=codes[:].bitcast(FP8X4), scales=plane, in_=yil[c][:])
-            nc.sync.dma_start(out=words_out[:, CUTS[c] : CUTS[c + 1]], in_=codes[:].bitcast(I32))
+            codes = ycodes[:, CUTS[c] : CUTS[c + 1]]
+            step = W if c == 0 else W // 2
+            for m0 in range(0, CUTS[c + 1] - CUTS[c], step):
+                g, c0 = divmod(CUTS[c] + m0, W)
+                nc.vector.quantize_mx(
+                    out=codes[:, m0 : m0 + step].bitcast(FP8X4),
+                    scales=yscales[4 * g : P, c0 : c0 + step],
+                    in_=yil[c][:, 4 * m0 : 4 * (m0 + step)],
+                )
+            if c != NC - 2:
+                first = CUTS[min(c, NC - 2)]
+                nc.sync.dma_start(out=words_out[:, first : CUTS[c + 1]], in_=ycodes[:, first : CUTS[c + 1]].bitcast(I32))
 
         nc.vector.memset(tabs[:].bitcast(I32), 0)
         nc.vector.memset(wps_raw[:].rearrange("p a c -> p (a c)").bitcast(I32), 0)
@@ -310,7 +370,7 @@ def tile_list_contrast_gain_control_kernel(
         load_w("w00", w1, 0, 0, ["R0"])
         load_tab(0, "T0")
         load_wps()
-        load_w("w10", w1, 1, 0, ["R1"])
+        load_w("w10", w1, 1, 0, [0])
         load_tab(1, "T1")
         root_gain()
         clear_page(0, "page0")
@@ -325,109 +385,112 @@ def tile_list_contrast_gain_control_kernel(
         gather_w(0, 1, 0, 512)
         deal_wps()
         cast_w("w10", [("s", 0, 64), ("v", 64, 128)], "G1")
-        load_w("d0", wd, 0, 0, ["R1"])
+        load_w("d0", wd, 0, 0, [0])
         load_w("d1", wd, 1, 0, ["T0"])
         nc.sync.dma_start(idx2[:], offs2)
-        lin(0, 0, 0, 256, FIRST, "A")
-        lin(0, 0, 256, 256, FIRST, "B")
+        lin(0, 0, 0, 256, FIRST, BANKS_A)
+        lin(0, 0, 256, 256, FIRST, BANKS_B)
         quant_w("w10")
         gather_w(1, 0, 0, 256)
-        lin(0, 0, 0, 256, SECOND, "A")
+        lin(0, 0, 0, 256, SECOND, BANKS_A)
         gather_w(1, 0, 256, 256)
-        lin(0, 0, 256, 256, SECOND, "B")
+        lin(0, 0, 256, 256, SECOND, BANKS_B)
         gather_w(1, 1, 0, 512)
         load_wg([(0, 0)], "T1")
-        square(0, 0, 0, 256, "E0")
-        square(0, 0, 256, 512, "E2")
+        square(0, 0, 0, 256, "E0", 0, 3)
+        square(0, 0, 256, 512, "E2", 0, 2)
+        square(0, 0, 0, 256, "E0", 3, 4)
+        square(0, 0, 256, 512, "E2", 2, 4)
+        lin(0, 1, 0, 512, BOTH[:2], BANKS_A)
+        square(0, 1, 0, 512, "E5", 0, 1)
         cast_w("w01", [("v", 0, 128)], "G0")
+        weave_e(0, 0, 0, 256, "v", "L5")
         quant_w("w01")
-        lin(1, 0, 0, 256, FIRST, "B")
+        lin(1, 0, 0, 256, FIRST, BANKS_B)
         cast_w("w11", [("s", 0, 44), ("v", 44, 128)], "G1")
         quant_w("w11")
-        lin(1, 0, 0, 256, SECOND, "B")
-        lin(1, 0, 256, 256, LATE, "A", 1)
-        weave_e(0, 0, 0, 256, "s", "R2")
+        lin(1, 0, 0, 256, SECOND, BANKS_B)
+        lin(1, 0, 256, 256, LATE, BANKS_A, 1)
+        weave_e(0, 0, 256, 512, "s", "R2")
         square(1, 0, 0, 256, "E1")
         square(1, 0, 256, 512, "E3")
-        weave_e(0, 0, 256, 512, "v", "G1")
         cast_w("d0", [("v", 0, 128)], "G0")
-        weave_e(1, 0, 0, 256, "v", "L1")
-        quant_e(0, 0, 0, 256, "R1")
+        quant_e(0, 0, 0, 256, 0)
         quant_e(0, 0, 256, 512)
+        weave_e(1, 0, 0, 256, "v", 2048)
+        quant_w("d0", 0, 2)
+        quant_e(1, 0, 0, 256)
         weave_e(1, 0, 256, 512, "v", "L3")
-        quant_e(1, 0, 0, 256, "E3")
+        quant_w("d0", 2, 4, 2048)
         quant_e(1, 0, 256, 512)
-        cast_slices("d1", 0, 3, "s", "G2")
-        quant_w("d0", 0, 1, "L1")
-        quant_w("d1", 0, 1)
-        pool_part(0, 0, "B0", "rA", "q0", 2)
-        drive_part(0, 0, "B1")
-        quant_w("d0", 1, 2)
-        quant_w("d1", 1, 2)
-        quant_w("d0", 2, 4)
-        cast_slices("d1", 3, 4, "v", "L3")
-        quant_w("d1", 2, 3)
-        quant_w("d1", 3, 4)
+        cast_slices("d1", 0, 2, "s", "G2")
+        quant_w("d1", 0, 2)
+        first_quarter(0, ["B0", "B1"])
+        first_quarter(256, ["B2", "B3"])
+        cast_slices("d1", 2, 4, "v", "L3")
+        first_divide(0)
+        quant_w("d1", 2, 4)
+        scatter(0, 0, 0, 256)
+        first_divide(256)
         clear_page(1, "L3")
-        divide(0, 0, "yA", 0, 256)
-        divide(0, 0, "yA", 256, 256)
+        pool_part(1, 0, "A0", "rB", "q1")
+        drive_part(1, 0, "A1")
         load_wg([(1, 0), (2, 0)], "q0")
-        pool_part(1, 0, "B2", "rB", "q1")
-        drive_part(1, 0, "B3")
-        scatter(0, 0)
         divide(1, 0, "yB")
+        scatter(0, 0, 256, 256)
         clear_page(2, "q1")
-        lin(0, 1, 0, 512, BOTH, "A")
-        pool_part(2, 0, "B0", "rC", "q2")
-        drive_part(2, 0, "B1")
+        lin(0, 1, 0, 512, BOTH[2:], ["A0", "A3", "B2", "B1"])
+        pool_part(2, 0, "A2", "rC", "q2")
+        drive_part(2, 0, "A3")
         divide(2, 0, "yA")
         clear_page(3, "q2")
-        square(0, 1, 0, 512, "rA")
-        lin(1, 1, 0, 512, BOTH, "A")
+        square(0, 1, 0, 512, None, 1, 4)
+        pool_part(3, 0, "A0", "rD", "q3")
+        lin(1, 1, 0, 512, BOTH, LATER)
         square(1, 1, 0, 512, "E2")
-        pool_part(3, 0, "B2", "rD", "q3")
-        weave_e(0, 1, 0, 512, "s", "L0")
-        load_wg([(3, 0), (0, 1), (1, 1), (2, 1), (3, 1)], "rA")
+        weave_e(0, 1, 0, 512, "s", "rD")
+        load_wg([(3, 0)], "E5")
         weave_e(1, 1, 0, 512, "s", "L4")
         scatter(1, 0)
         scatter(2, 0)
+        drive_part(3, 0, "B0")
+        divide(3, 0, "yF")
         quant_e(0, 1, 0, 512)
-        drive_part(3, 0, "A3")
-        divide(3, 0, "yB")
         quant_e(1, 1, 0, 512)
-        pool_part(0, 1, "A0", "rB", "q4")
+        load_wg([(0, 1), (1, 1), (2, 1), (3, 1)], "E2")
+        pool_part(0, 1, "B3", "rB", "q4")
         scatter(3, 0)
-        pool_part(1, 1, "A1", "rC", "q5")
-        drive_part(0, 1, "B1")
-        drive_part(1, 1, "B2")
-        pool_part(2, 1, "A2", "rB", "q6")
-        pool_part(3, 1, "B0", "rC", "q3")
-        drive_part(2, 1, "B3")
-        drive_part(3, 1, "A3")
-        divide(0, 1, "yC")
+        pool_part(1, 1, "B0", "rC", "q5")
+        drive_part(0, 1, "A1")
+        drive_part(1, 1, "A3")
+        pool_part(2, 1, "B2", "rB", "q6")
+        pool_part(3, 1, "A2", "rC", "q3")
+        drive_part(2, 1, "A0")
+        drive_part(3, 1, "B1")
+        divide(0, 1, "yE")
         divide(1, 1, "yD")
         scatter(0, 1)
         finish_page(0)
-        divide(2, 1, "yA")
         scatter(1, 1)
         finish_page(1)
+        divide(2, 1, "yE")
         divide(3, 1, "yD")
         scatter(2, 1)
         finish_page(2)
         scatter(3, 1)
+        round_page(2, 0, "v", 0, OWN)
+        round_page(3, 0, "v", 0, OWN)
         finish_page(3)
         weave_y(0, "v")
         weave_y(1, "v")
         quant_y(0)
         weave_y(2, "v")
         quant_y(1)
-        weave_y(3, "v")
-        quant_y(2)
+        weave_y(3, "s")
         weave_y(4, "s")
-        weave_y(5, "s")
+        quant_y(2)
         quant_y(3)
         quant_y(4)
-        quant_y(5)
         scales_out = out_2[0].bitcast(I32).rearrange("r (g m) -> g r m", g=4)
         for q in range(4):
             nc.sync.dma_start(out=scales_out[:, 4 * q : 4 * q + 4, :], in_=yscales[32 * q : 32 * q + 16, :].bitcast(I32))

@@ -316,6 +316,18 @@ def tile_list_contrast_gain_control_kernel(
                 ys[(t, j)] = place([P, W], F32, f"y{t}{j}", tag)
             nc.vector.tensor_tensor(ys[(t, j)][:, c0 : c0 + n], drives[(t, j)][:, c0 : c0 + n], rec[(t, j)][:, c0 : c0 + n], ALU.mult)
 
+        def products(t, j, tag):
+            tile, row = wg[(t, j)]
+            d = keep.tile([P, W], F32, name=f"d{t}{j}", tag=f"d{t}", align_bytes=64)
+            u = keep.tile([P, W], F32, name=f"u{t}{j}", tag="yE", align_bytes=64)
+            ys[(t, j)] = keep.tile([P, W], F32, name=f"z{t}{j}", tag=tag, align_bytes=64)
+            nc.scalar.copy(out=d[:], in_=drives[(t, j)][:])
+            nc.gpsimd.tensor_tensor(u[:], rec[(t, j)][:], tile[:, row, :], ALU.mult)
+            nc.gpsimd.tensor_tensor(ys[(t, j)][:], d[:], u[:], ALU.mult)
+
+        def put(t, j):
+            nc.vector.tensor_copy(pages[t][:].indirect(idx2[:, j * W // 16 : (j + 1) * W // 16]), ys[(t, j)][:])
+
         def scatter(t, j, c0=0, n=W):
             tile, row = wg[(t, j)]
             nc.vector.tensor_tensor(
@@ -468,16 +480,19 @@ def tile_list_contrast_gain_control_kernel(
         drive_part(2, 1, "A0")
         drive_part(3, 1, "B1")
         divide(0, 1, "yE")
-        divide(1, 1, "yD")
-        scatter(0, 1)
+        y = ys[(0, 1)]
+        ys[(0, 1)] = keep.tile([P, W], F32, name="z01", tag="yA", align_bytes=64)
+        nc.vector.tensor_tensor(ys[(0, 1)][:], y[:], wg[(0, 1)][0][:, 0, :], ALU.mult)
+        products(1, 1, "yD")
+        products(2, 1, "yB")
+        products(3, 1, "yC")
+        put(0, 1)
         finish_page(0)
-        scatter(1, 1)
+        put(1, 1)
         finish_page(1)
-        divide(2, 1, "yE")
-        divide(3, 1, "yD")
-        scatter(2, 1)
+        put(2, 1)
         finish_page(2)
-        scatter(3, 1)
+        put(3, 1)
         round_page(2, 0, "v", 0, OWN)
         round_page(3, 0, "v", 0, OWN)
         finish_page(3)

@@ -80,6 +80,8 @@ def tile_list_contrast_gain_control_kernel(
         def copy_on(eng, o, i):
             if eng == "v":
                 nc.vector.tensor_copy(out=o, in_=i)
+            elif eng == "g":
+                nc.gpsimd.tensor_copy(out=o, in_=i)
             else:
                 nc.scalar.copy(out=o, in_=i)
 
@@ -337,7 +339,7 @@ def tile_list_contrast_gain_control_kernel(
                 ALU.mult,
             )
 
-        pairs = [keep.tile([P, 2, CUTS[c + 1] - CUTS[c], 2], BF16, name=f"pairs{c}") for c in range(NC)]
+        pairs = [keep.tile([P, 2, CUTS[c + 1] - CUTS[c], 2], BF16, name=f"pairs{c}") for c in range(NC - 2)]
 
         def round_page(t, c, eng, m0=0, m1=None):
             m1 = m1 or CUTS[c + 1] - CUTS[c]
@@ -345,8 +347,8 @@ def tile_list_contrast_gain_control_kernel(
 
         def finish_page(t):
             nc.sync.dma_start(out=out_rows[:, t, :], in_=pages[t][:])
-            for c in range(NC):
-                round_page(t, c, "s", OWN if t >= 2 and c == 0 else 0)
+            for c in range(NC - 2 if t == 2 else NC):
+                round_page(t, c, "g" if t < 2 and c >= NC - 2 else "s", OWN if t >= 2 and c == 0 else 0)
 
         def weave_y(c, eng):
             il = keep.tile([P, 4 * (CUTS[c + 1] - CUTS[c])], BF16, name=f"yil{c}", align_bytes=64)
@@ -461,7 +463,7 @@ def tile_list_contrast_gain_control_kernel(
         lin(1, 1, 0, 512, BOTH, LATER)
         square(1, 1, 0, 512, "E2")
         weave_e(0, 1, 0, 512, "s", "rD")
-        load_wg([(3, 0)], "E5")
+        load_wg([(3, 0), (0, 1), (1, 1), (2, 1), (3, 1)], "E5")
         weave_e(1, 1, 0, 512, "s", "L4")
         scatter(1, 0)
         scatter(2, 0)
@@ -469,7 +471,6 @@ def tile_list_contrast_gain_control_kernel(
         divide(3, 0, "yF")
         quant_e(0, 1, 0, 512)
         quant_e(1, 1, 0, 512)
-        load_wg([(0, 1), (1, 1), (2, 1), (3, 1)], "E2")
         pool_part(0, 1, "B3", "rB", "q4")
         scatter(3, 0)
         pool_part(1, 1, "B0", "rC", "q5")
@@ -479,21 +480,27 @@ def tile_list_contrast_gain_control_kernel(
         pool_part(3, 1, "A2", "rC", "q3")
         drive_part(2, 1, "A0")
         drive_part(3, 1, "B1")
-        divide(0, 1, "yE")
-        y = ys[(0, 1)]
+        u = keep.tile([P, W], F32, name="u01", tag="yE", align_bytes=64)
         ys[(0, 1)] = keep.tile([P, W], F32, name="z01", tag="yA", align_bytes=64)
-        nc.vector.tensor_tensor(ys[(0, 1)][:], y[:], wg[(0, 1)][0][:, 0, :], ALU.mult)
+        for c0 in (0, 256):
+            nc.vector.tensor_tensor(u[:, c0 : c0 + 256], rec[(0, 1)][:, c0 : c0 + 256], wg[(0, 1)][0][:, 1, c0 : c0 + 256], ALU.mult)
+        for c0 in (0, 256):
+            nc.vector.tensor_tensor(ys[(0, 1)][:, c0 : c0 + 256], drives[(0, 1)][:, c0 : c0 + 256], u[:, c0 : c0 + 256], ALU.mult)
         products(1, 1, "yD")
         products(2, 1, "yB")
         products(3, 1, "yC")
+        pairs.append(keep.tile([P, 2, 256, 2], BF16, name="pairs3", tag="d3", align_bytes=64))
+        pairs.append(keep.tile([P, 2, 256, 2], BF16, name="pairs4", tag="yE", align_bytes=64))
         put(0, 1)
         finish_page(0)
         put(1, 1)
         finish_page(1)
         put(2, 1)
+        nc.scalar.copy(out=pairs[0][:, 1, 0:OWN, :], in_=pages[2][:, 0:OWN].unsqueeze(2).to_broadcast([P, OWN, 2]))
+        for c in (3, 4):
+            nc.gpsimd.tensor_copy(out=pairs[c][:, 1, :, :], in_=pages[2][:, CUTS[c] : CUTS[c + 1]].unsqueeze(2).to_broadcast([P, 256, 2]))
         finish_page(2)
         put(3, 1)
-        round_page(2, 0, "v", 0, OWN)
         round_page(3, 0, "v", 0, OWN)
         finish_page(3)
         weave_y(0, "v")

@@ -236,7 +236,7 @@ def tile_list_contrast_gain_control_kernel(
 
         def pool_part(t, j, bank, tag, tag2, parts=1):
             acc = psum.tile([P, W], F32, name=f"pool{t}{j}", tag=bank)
-            order = (0, 1) if t == 0 else (1, 0)
+            order = (0, 1) if t + j == 1 else (1, 0)
             for h in order:
                 c, s = eq[(h, j)]
                 nc.tensor.matmul_mx(
@@ -292,9 +292,8 @@ def tile_list_contrast_gain_control_kernel(
 
         def first_divide(c0):
             n = W // 2
-            if c0 == 0:
-                ys[(0, 0)] = keep.tile([P, W], F32, name="y00", tag="yC", align_bytes=64)
-            nc.vector.tensor_tensor(ys[(0, 0)][:, c0 : c0 + n], drives[c0][:], rec[c0][:], ALU.mult)
+            ys[c0] = keep.tile([P, n], F32, name=f"y_q{c0}", tag="yC" if c0 == 0 else "rB", align_bytes=64)
+            nc.vector.tensor_tensor(ys[c0][:], drives[c0][:], rec[c0][:], ALU.mult)
 
         def drive_part(t, j, bank):
             acc = psum.tile([P, W], F32, name=f"drive{t}{j}", tag=bank)
@@ -318,10 +317,10 @@ def tile_list_contrast_gain_control_kernel(
                 ys[(t, j)] = place([P, W], F32, f"y{t}{j}", tag)
             nc.vector.tensor_tensor(ys[(t, j)][:, c0 : c0 + n], drives[(t, j)][:, c0 : c0 + n], rec[(t, j)][:, c0 : c0 + n], ALU.mult)
 
-        def products(t, j, tag):
+        def products(t, j, tag, utag="yE", dtag=None):
             tile, row = wg[(t, j)]
-            d = keep.tile([P, W], F32, name=f"d{t}{j}", tag=f"d{t}", align_bytes=64)
-            u = keep.tile([P, W], F32, name=f"u{t}{j}", tag="yE", align_bytes=64)
+            d = keep.tile([P, W], F32, name=f"d{t}{j}", tag=dtag or f"d{t}", align_bytes=64)
+            u = keep.tile([P, W], F32, name=f"u{t}{j}", tag=utag, align_bytes=64)
             ys[(t, j)] = keep.tile([P, W], F32, name=f"z{t}{j}", tag=tag, align_bytes=64)
             nc.scalar.copy(out=d[:], in_=drives[(t, j)][:])
             nc.gpsimd.tensor_tensor(u[:], rec[(t, j)][:], tile[:, row, :], ALU.mult)
@@ -334,7 +333,7 @@ def tile_list_contrast_gain_control_kernel(
             tile, row = wg[(t, j)]
             nc.vector.tensor_tensor(
                 pages[t][:].indirect(idx2[:, (j * W + c0) // 16 : (j * W + c0 + n) // 16]),
-                ys[(t, j)][:, c0 : c0 + n],
+                ys[(t, j)][:] if n == W else ys[c0][:],
                 tile[:, row, c0 : c0 + n],
                 ALU.mult,
             )
@@ -415,50 +414,54 @@ def tile_list_contrast_gain_control_kernel(
         square(0, 0, 256, 512, "E2", 0, 2)
         square(0, 0, 0, 256, "E0", 3, 4)
         square(0, 0, 256, 512, "E2", 2, 4)
-        lin(0, 1, 0, 512, BOTH[:2], BANKS_A)
+        lin(0, 1, 0, 512, BOTH[:6], BANKS_A)
         square(0, 1, 0, 512, "E5", 0, 1)
+        weave_e(0, 0, 256, 512, "s", "L6")
+        square(0, 1, 0, 512, None, 1, 3)
         cast_w("w01", [("v", 0, 128)], "G0")
         weave_e(0, 0, 0, 256, "v", "L5")
         quant_w("w01")
         lin(1, 0, 0, 256, FIRST, BANKS_B)
-        cast_w("w11", [("s", 0, 44), ("v", 44, 128)], "G1")
-        quant_w("w11")
+        cast_slices("w11", 0, 2, "v", "G1")
+        cast_slices("w11", 2, 4, "v", "G4")
+        quant_w("w11", 0, 2)
+        quant_w("w11", 2, 4)
         lin(1, 0, 0, 256, SECOND, BANKS_B)
         lin(1, 0, 256, 256, LATE, BANKS_A, 1)
-        weave_e(0, 0, 256, 512, "s", "R2")
         square(1, 0, 0, 256, "E1")
         square(1, 0, 256, 512, "E3")
-        cast_w("d0", [("v", 0, 128)], "G0")
+        cast_slices("d0", 0, 2, "v", "G0")
+        cast_slices("d0", 2, 4, "v", "G3")
+        quant_w("d0", 0, 2)
         quant_e(0, 0, 0, 256, 0)
         quant_e(0, 0, 256, 512)
         weave_e(1, 0, 0, 256, "v", 2048)
-        quant_w("d0", 0, 2)
+        quant_w("d0", 2, 4)
         quant_e(1, 0, 0, 256)
         weave_e(1, 0, 256, 512, "v", "L3")
-        quant_w("d0", 2, 4, 2048)
-        quant_e(1, 0, 256, 512)
         cast_slices("d1", 0, 2, "s", "G2")
         quant_w("d1", 0, 2)
+        quant_e(1, 0, 256, 512)
         first_quarter(0, ["B0", "B1"])
         first_quarter(256, ["B2", "B3"])
-        cast_slices("d1", 2, 4, "v", "L3")
+        cast_slices("d1", 2, 4, "v", "G5")
         first_divide(0)
-        quant_w("d1", 2, 4)
+        quant_w("d1", 2, 4, "rA")
         scatter(0, 0, 0, 256)
-        first_divide(256)
-        clear_page(1, "L3")
+        clear_page(1, "G5")
         pool_part(1, 0, "A0", "rB", "q1")
         drive_part(1, 0, "A1")
+        first_divide(256)
         load_wg([(1, 0), (2, 0)], "q0")
         divide(1, 0, "yB")
         scatter(0, 0, 256, 256)
         clear_page(2, "q1")
-        lin(0, 1, 0, 512, BOTH[2:], ["A0", "A3", "B2", "B1"])
+        lin(0, 1, 0, 512, BOTH[6:], ["A0", "A1", "A2", "B2"])
         pool_part(2, 0, "A2", "rC", "q2")
         drive_part(2, 0, "A3")
         divide(2, 0, "yA")
         clear_page(3, "q2")
-        square(0, 1, 0, 512, None, 1, 4)
+        square(0, 1, 0, 512, None, 3, 4)
         pool_part(3, 0, "A0", "rD", "q3")
         lin(1, 1, 0, 512, BOTH, LATER)
         square(1, 1, 0, 512, "E2")
@@ -473,10 +476,10 @@ def tile_list_contrast_gain_control_kernel(
         quant_e(1, 1, 0, 512)
         pool_part(0, 1, "B3", "rB", "q4")
         scatter(3, 0)
-        pool_part(1, 1, "B0", "rC", "q5")
+        pool_part(1, 1, "B0", "rB", "q5")
         drive_part(0, 1, "A1")
         drive_part(1, 1, "A3")
-        pool_part(2, 1, "B2", "rB", "q6")
+        pool_part(2, 1, "B2", "rE", "q6")
         pool_part(3, 1, "A2", "rC", "q3")
         drive_part(2, 1, "A0")
         drive_part(3, 1, "B1")

@@ -18,16 +18,13 @@ ALU = mybir.AluOpType
 
 P = 128
 W = 512
+Q = 256
 CUTS = (0, 512, 1024, 1536, 1792, 2048)
+PARTS = len(CUTS) - 1
+WIDE = 3
 OWN = 384
-NC = len(CUTS) - 1
-BANKS_A = ["A0", "A1", "A2", "A3"]
-BANKS_B = ["B0", "B1", "B2", "B3"]
-LATER = ["B3", "B2", "B1", "A2"]
-FIRST = [(t, 0) for t in range(4)]
-SECOND = [(t, 1) for t in range(4)]
-BOTH = [(t, a) for t in range(4) for a in range(2)]
-LATE = [(t, a) for t in range(4) for a in (1, 0)]
+BANKS_A = ("A0", "A1", "A2", "A3")
+BANKS_B = ("B0", "B1", "B2", "B3")
 
 
 def tile_list_contrast_gain_control_kernel(
@@ -39,483 +36,410 @@ def tile_list_contrast_gain_control_kernel(
         shared = ctx.enter_context(tc.tile_pool(name="shared", bufs=1))
         psum = ctx.enter_context(tc.psum_pool(name="psum", bufs=1))
 
-        def place(shape, dtype, name, tag):
-            if isinstance(tag, int):
-                return shared.tile(shape, dtype, name=name, align_bytes=64, offset=tag)
-            return keep.tile(shape, dtype, name=name, tag=tag, align_bytes=64)
+        def place(shape, dtype, name, where=None):
+            if isinstance(where, int):
+                return shared.tile(shape, dtype, name=name, align_bytes=64, offset=where)
+            return keep.tile(shape, dtype, name=name, tag=where or name, align_bytes=64)
 
         idx = keep.tile([P, S // 16], U16, name="idx")
         idx2 = keep.tile([P, S // 16], U16, name="idx2")
-        tabs = keep.tile([P, T], U8, name="tabs", tag="q_w00_0", align_bytes=64)
-        wps_raw = keep.tile([P, 2, N], U8, name="wps_raw", tag="q_w10_0", align_bytes=64)
-        wpw_raw = keep.tile([P, 2, 2 * N], U8, name="wpw_raw", align_bytes=64)
-        g_sb = keep.tile([P, 2, 4], F32, name="g_sb")
-        sg = keep.tile([P, 2, 4], F32, name="sg")
+        tab_planes = place([P, T], U8, "tab_planes")
+        wp_planes_raw = place([P, 2, N], U8, "wp_planes_raw")
+        wp_codes_raw = place([P, 2, 2 * N], U8, "wp_codes_raw")
+        gains = keep.tile([P, 2, 4], F32, name="gains")
+        roots = keep.tile([P, 2, 4], F32, name="roots")
         tiny = keep.tile([P, 1], F32, name="tiny")
-        wpw = keep.tile([P, 2, 2 * N], U8, name="wpw", align_bytes=64)
-        wps = keep.tile([P, 2, N], U8, name="wps", align_bytes=64)
-        yscales = keep.tile([P, W], U8, name="yscales", align_bytes=64)
-        ycodes = keep.tile([P, T2], U32, name="ycodes", align_bytes=64)
+        wp_codes = place([P, 2, 2 * N], U8, "wp_codes")
+        wp_planes = place([P, 2, N], U8, "wp_planes")
+        y_planes = place([P, W], U8, "y_planes")
+        y_codes = place([P, T2], U32, "y_codes")
         pages = {}
-        accs = {}
-        sliced = {}
-        drives = {}
-        tabw = {}
+        tables = {}
         raws = {}
-        grouped = {}
-        wq = {}
-        gw = {}
-        gs = {}
-        est = {}
-        eil = {}
-        eq = {}
-        rec = {}
-        ys = {}
-        wg = {}
-        yil = {}
-        wgq = wgo.rearrange("(q t) j -> q t j", t=4)
+        rounded = {}
+        weights = {}
+        picked = {}
+        picked_planes = {}
+        lins = {}
+        squares = {}
+        woven = {}
+        e_mx = {}
+        recips = {}
+        drives = {}
+        values = {}
+        readout = {}
+        pairs = {}
+        y_woven = {}
+        wgo_rows = wgo.rearrange("(q t) j -> q t j", t=4)
         out_rows = out_0.rearrange("(p t) m -> p t m", t=4)
         words_out = out_1[0].rearrange("p m t -> p (m t)").bitcast(I32)
 
-        def copy_on(eng, o, i):
-            if eng == "v":
-                nc.vector.tensor_copy(out=o, in_=i)
-            elif eng == "g":
-                nc.gpsimd.tensor_copy(out=o, in_=i)
+        def copy_on(eng, out, in_):
+            if eng == "vector":
+                nc.vector.tensor_copy(out=out, in_=in_)
+            elif eng == "gpsimd":
+                nc.gpsimd.tensor_copy(out=out, in_=in_)
             else:
-                nc.scalar.copy(out=o, in_=i)
+                nc.scalar.copy(out=out, in_=in_)
 
-        def clear_page(t, tag):
-            pages[t] = keep.tile([P, T2], F32, name=f"page{t}", tag=tag, align_bytes=64)
-            eng = nc.vector if t == 0 else nc.gpsimd
+        def clear_page(t, eng, where=None):
+            pages[t] = place([P, T2], F32, f"page{t}", where)
             eng.memset(pages[t][:].bitcast(I32), 0)
 
-        def root_gain():
-            r, s0, sq, rest, half = [keep.tile([P, 2, 4], F32, name=f"root{n}") for n in range(5)]
-            fix = keep.tile([P, 2, 4], F32, name="fix")
-            nc.scalar.activation(r[:], g_sb[:], ACT.Abs_reciprocal_sqrt, bias=tiny[:])
-            nc.gpsimd.tensor_tensor(s0[:], g_sb[:], r[:], ALU.mult)
-            nc.gpsimd.tensor_tensor(sq[:], s0[:], s0[:], ALU.mult)
-            nc.gpsimd.tensor_tensor(rest[:], g_sb[:], sq[:], ALU.subtract)
+        def root_of_gain():
+            r, s, s2, rest, half, fix = [keep.tile([P, 2, 4], F32, name=f"newton{n}") for n in range(6)]
+            nc.scalar.activation(r[:], gains[:], ACT.Abs_reciprocal_sqrt, bias=tiny[:])
+            nc.gpsimd.tensor_tensor(s[:], gains[:], r[:], ALU.mult)
+            nc.gpsimd.tensor_tensor(s2[:], s[:], s[:], ALU.mult)
+            nc.gpsimd.tensor_tensor(rest[:], gains[:], s2[:], ALU.subtract)
             nc.gpsimd.tensor_scalar(half[:], r[:], 0.5, 0.0, ALU.mult, ALU.add)
             nc.gpsimd.tensor_tensor(fix[:], rest[:], half[:], ALU.mult)
-            nc.gpsimd.tensor_tensor(sg[:], s0[:], fix[:], ALU.add)
+            nc.gpsimd.tensor_tensor(roots[:], s[:], fix[:], ALU.add)
 
-        def load_w(key, src, a, h, tags):
-            n = W // len(tags)
-            raws[key] = []
-            for u, tag in enumerate(tags):
-                raw = place([P, 4, n], F32, f"raw_{key}{u}", tag)
-                c0 = h * W + u * n
-                nc.sync.dma_start(
-                    out=raw[:], in_=src[a * W : (a + 1) * W, c0 : c0 + n].rearrange("(p i) c -> p i c", i=4)
-                )
-                raws[key].append(raw)
+        def load_weight(key, src, a, h, where):
+            raws[key] = place([P, 4, W], F32, "raw_" + key, where)
+            rows = src[a * W : (a + 1) * W, h * W : (h + 1) * W]
+            nc.sync.dma_start(out=raws[key][:], in_=rows.rearrange("(p i) c -> p i c", i=4))
 
-        def load_tab(a, tag):
-            tabw[a] = keep.tile([P, T], I32, name=f"tabw{a}", tag=tag, align_bytes=64)
-            nc.sync.dma_start(out=tabw[a][:], in_=tab_words[a].rearrange("p n t -> p (n t)").bitcast(I32))
+        def load_table(a):
+            tables[a] = place([P, T], I32, f"table{a}")
+            nc.sync.dma_start(out=tables[a][:], in_=tab_words[a].rearrange("p n t -> p (n t)").bitcast(I32))
 
-        def load_tabs():
-            for q in range(4):
-                nc.sync.dma_start(
-                    out=tabs[32 * q : 32 * q + 8, :].bitcast(I32),
-                    in_=tab_scales[:, 4 * q : 4 * q + 4, :].bitcast(I32),
-                )
-
-        def load_wps():
-            for q in range(4):
-                nc.sync.dma_start(
-                    out=wps_raw[32 * q : 32 * q + 4, :, :].bitcast(I32),
-                    in_=wp_scales[:, 4 * q : 4 * q + 4, :].rearrange("a r c -> r a c").bitcast(I32),
-                )
-
-        def load_wg(units, tag):
-            tile = place([P, len(units), W], F32, f"wg{units[0][0]}{units[0][1]}", tag)
-            for row, (t, j) in enumerate(units):
-                wg[(t, j)] = (tile, row)
-                if j == 1 and t % 2 == 1:
-                    continue
-                n = 1 + j
+        def load_readout(runs, where):
+            tile = place([P, sum(pages_in for t0, pages_in, j in runs), W], F32, "readout_" + where, where)
+            row = 0
+            for t0, pages_in, j in runs:
                 for q in (0, 2, 1, 3):
                     nc.sync.dma_start(
-                        out=tile[32 * q : 32 * q + 32, row : row + n, :], in_=wgq[:, t : t + n, j * W : (j + 1) * W]
+                        out=tile[32 * q : 32 * q + 32, row : row + pages_in, :],
+                        in_=wgo_rows[:, t0 : t0 + pages_in, j * W : (j + 1) * W],
                     )
+                for u in range(pages_in):
+                    readout[(t0 + u, j)] = tile[:, row + u, :]
+                row = row + pages_in
 
-        def cast_w(key, shares, tag):
-            g = keep.tile([P, 4 * W], BF16, name="grp_" + key, tag=tag, align_bytes=64)
-            o = g[:].rearrange("p (t m i) -> p m i t", t=4, i=4)
-            per = P // len(raws[key])
+        def round_weight(key, shares, t0, t1, where):
+            tile = place([P, (t1 - t0) * W], BF16, f"rounded_{key}{t0}", where)
+            out = tile[:].rearrange("p (t m i) -> p m i t", t=t1 - t0, i=4)
+            in_ = raws[key][:].rearrange("p i (m t) -> p m i t", t=4)[:, :, :, t0:t1]
             for eng, m0, m1 in shares:
-                i = raws[key][m0 // per][:].rearrange("p i (m t) -> p m i t", t=4)
-                copy_on(eng, o[:, m0:m1], i[:, m0 % per : m0 % per + m1 - m0])
-            grouped[key] = g
-
-        def cast_slices(key, t0, t1, eng, tag):
-            g = keep.tile([P, (t1 - t0) * W], BF16, name=f"grp_{key}{t0}", tag=tag, align_bytes=64)
-            o = g[:].rearrange("p (t m i) -> p m i t", t=t1 - t0, i=4)
-            i = raws[key][0][:].rearrange("p i (m t) -> p m i t", t=4)[:, :, :, t0:t1]
-            copy_on(eng, o, i)
+                copy_on(eng, out[:, m0:m1], in_[:, m0:m1])
             for t in range(t0, t1):
-                sliced[(key, t)] = (g, t0)
+                rounded[(key, t)] = (tile, t0)
 
-        def quant_w(key, t0=0, t1=4, tag=None):
-            codes = place([P, (t1 - t0) * P], U32, f"q_{key}{t0}_c", f"q_{key}_{t0}" if tag is None else tag)
-            scales = keep.tile([P, (t1 - t0) * P], U8, name=f"q_{key}{t0}_s", align_bytes=64)
-            g, first = sliced[(key, t0)] if (key, t0) in sliced else (grouped[key], 0)
-            nc.vector.quantize_mx(out=codes[:].bitcast(FP8X4), scales=scales[:], in_=g[:, (t0 - first) * W : (t1 - first) * W])
+        def quantise_weight(key, t0, t1, where=None):
+            codes = place([P, (t1 - t0) * P], U32, f"codes_{key}{t0}", where)
+            plane = place([P, (t1 - t0) * P], U8, f"plane_{key}{t0}")
+            tile, first = rounded[(key, t0)]
+            nc.vector.quantize_mx(
+                out=codes[:].bitcast(FP8X4), scales=plane[:], in_=tile[:, (t0 - first) * W : (t1 - first) * W]
+            )
             for t in range(t0, t1):
                 cols = slice((t - t0) * P, (t - t0 + 1) * P)
-                wq[(key, t)] = (codes[:, cols].bitcast(FP8X4), scales[:, cols])
+                weights[(key, t)] = (codes[:, cols].bitcast(FP8X4), plane[:, cols])
 
-        def gather_w(a, j, c0, n, tag=None):
-            g = keep.tile([P, n], U32, name=f"gw{a}{j}{c0}", tag=tag or f"gw{a}{j}{c0}", align_bytes=64)
-            first = (j * W + c0) // 16
-            nc.vector.tensor_copy(g[:], tabw[a][:].bitcast(U32).indirect(idx[:, first : first + n // 16]))
-            for c in range(c0, c0 + n, 256):
-                gw[(a, j, c)] = (g, c - c0)
+        def gather_words(a, j0, n):
+            tile = place([P, n], U32, f"picked{a}_{j0}")
+            nc.vector.tensor_copy(tile[:], tables[a][:].bitcast(U32).indirect(idx[:, j0 // 16 : (j0 + n) // 16]))
+            for c in range(0, n, Q):
+                picked[(a, j0 + c)] = (tile, c)
 
-        def gather_s(j):
-            g = keep.tile([P, W], U8, name=f"gs{j}", align_bytes=64)
-            nc.vector.tensor_copy(g[:], tabs[:].indirect(idx[:, 32 * j : 32 * j + 32]))
-            gs[j] = g
+        def gather_planes(j):
+            picked_planes[j] = place([P, W], U8, f"picked_planes{j}")
+            nc.vector.tensor_copy(picked_planes[j][:], tab_planes[:].indirect(idx[:, j * W // 16 : (j + 1) * W // 16]))
 
-        def lin(h, j, c0, n, passes, bank, opens=0):
-            for t, a in passes:
-                c, s = wq[(f"w{a}{h}", t)]
-                g, g0 = gw[(a, j, c0)]
-                if a == opens:
-                    accs[(h, j, c0, t)] = psum.tile([P, n], F32, name=f"lin{h}{j}{c0}{t}", tag=bank[t])
-                nc.tensor.matmul_mx(
-                    out=accs[(h, j, c0, t)][:],
-                    lhsT=c,
-                    lhsT_scale=s,
-                    rhs=g[:, g0 : g0 + n].bitcast(FP8X4),
-                    rhs_scale=gs[j][4 * a : P, c0 : c0 + n],
-                    start=(a == opens),
-                    stop=(a != opens),
-                )
+        def lin(h, j0, n, slices, passes, banks, opens=0):
+            j, c0 = divmod(j0, W)
+            for t in slices:
+                for a in passes:
+                    codes, plane = weights[(f"w{a}{h}", t)]
+                    words, col = picked[(a, j0)]
+                    if a == opens:
+                        lins[(h, j0, t)] = psum.tile([P, n], F32, name=f"lin{h}_{j0}_{t}", tag=banks[t])
+                    nc.tensor.matmul_mx(
+                        out=lins[(h, j0, t)][:],
+                        lhsT=codes,
+                        lhsT_scale=plane,
+                        rhs=words[:, col : col + n].bitcast(FP8X4),
+                        rhs_scale=picked_planes[j][4 * a : P, c0 : c0 + n],
+                        start=(a == opens),
+                        stop=(a != opens),
+                    )
 
-        def square(h, j, c0, c1, tag, t0=0, t1=4):
-            if t0 == 0:
-                est[(h, j, c0)] = place([P, 4, c1 - c0], BF16, f"est{h}{j}{c0}", tag)
-            for t in range(t0, t1):
-                nc.scalar.activation(est[(h, j, c0)][:, t, :], accs[(h, j, c0, t)][:], ACT.Square, scale=sg[:, h, t : t + 1])
+        def square(h, j0, n, slices, where=None):
+            if (h, j0) not in squares:
+                squares[(h, j0)] = place([P, 4, n], BF16, f"squares{h}_{j0}", where)
+            for t in slices:
+                nc.scalar.activation(squares[(h, j0)][:, t, :], lins[(h, j0, t)][:], ACT.Square, scale=roots[:, h, t : t + 1])
 
-        def weave_e(h, j, c0, c1, eng, tag, base=None):
-            if base is None:
-                eil[(h, j, c0)] = place([P, 4 * W], BF16, f"eil{h}{j}{c0}", tag)
-                base = c0
-            il = eil[(h, j, base)][:, 4 * (c0 - base) : 4 * (c1 - base)]
+        def weave_e(h, j0, n, eng, where=None):
+            woven[(h, j0)] = place([P, 4 * n], BF16, f"woven{h}_{j0}", where)
             copy_on(
                 eng,
-                il.rearrange("p (c i t) -> p c t i", i=4, t=4),
-                est[(h, j, c0)][:].rearrange("p t (c i) -> p c t i", i=4),
+                woven[(h, j0)][:].rearrange("p (c i t) -> p c t i", i=4, t=4),
+                squares[(h, j0)][:].rearrange("p t (c i) -> p c t i", i=4),
             )
 
-        def quant_e(h, j, c0, c1, tag=None):
-            if (h, j) not in eq:
-                codes = place([P, W], U32, f"q_e{h}{j}_c", f"q_e{h}{j}" if tag is None else tag)
-                scales = keep.tile([P, W], U8, name=f"q_e{h}{j}_s", align_bytes=64)
-                eq[(h, j)] = (codes, scales)
-            codes, scales = eq[(h, j)]
-            nc.vector.quantize_mx(out=codes[:, c0:c1].bitcast(FP8X4), scales=scales[:, c0:c1], in_=eil[(h, j, c0)][:, : 4 * (c1 - c0)])
+        def quantise_e(h, j0, n, where=None):
+            j, c0 = divmod(j0, W)
+            if (h, j) not in e_mx:
+                e_mx[(h, j)] = (place([P, W], U32, f"e_codes{h}{j}", where), place([P, W], U8, f"e_plane{h}{j}"))
+            codes, plane = e_mx[(h, j)]
+            nc.vector.quantize_mx(out=codes[:, c0 : c0 + n].bitcast(FP8X4), scales=plane[:, c0 : c0 + n], in_=woven[(h, j0)][:])
 
-        def deal_wpw():
-            for a in range(2):
-                nc.vector.tensor_copy(
-                    out=wpw[:, a, :].rearrange("p (t m b) -> p t m b", t=4, b=2),
-                    in_=wpw_raw[:, a, :].rearrange("p (m t b) -> p t m b", t=4, b=2),
-                )
-
-        def deal_wps():
-            nc.vector.tensor_copy(
-                out=wps[:].rearrange("p a (t m) -> p a t m", t=4),
-                in_=wps_raw[:].rearrange("p a (m t) -> p a t m", t=4),
-            )
-
-        def pool_part(t, j, bank, tag, tag2, parts=1):
-            acc = psum.tile([P, W], F32, name=f"pool{t}{j}", tag=bank)
-            order = (0, 1) if t + j == 1 else (1, 0)
+        def second_sum(acc, key, t, j0, n, order):
+            j, c0 = divmod(j0, W)
             for h in order:
-                c, s = eq[(h, j)]
+                codes, plane = weights[(f"{key}{h}", t)]
+                e_codes, e_plane = e_mx[(h, j)]
                 nc.tensor.matmul_mx(
-                    out=acc[:],
-                    lhsT=wpw[:, h, 2 * t * P : 2 * (t + 1) * P].bitcast(FP4X4),
-                    lhsT_scale=wps[:, h, t * P : (t + 1) * P],
-                    rhs=c[:].bitcast(FP8X4),
-                    rhs_scale=s[:],
+                    out=acc,
+                    lhsT=codes,
+                    lhsT_scale=plane,
+                    rhs=e_codes[:, c0 : c0 + n].bitcast(FP8X4),
+                    rhs_scale=e_plane[:, c0 : c0 + n],
                     start=(h == order[0]),
                     stop=(h == order[1]),
                 )
-            r = keep.tile([P, W], F32, name=f"r{t}{j}", tag=tag, align_bytes=64)
-            r2 = keep.tile([P, W], F32, name=f"rr{t}{j}", tag=tag2, align_bytes=64)
-            n = W // parts
-            for c0 in range(0, W, n):
-                nc.scalar.activation(r[:, c0 : c0 + n], acc[:, c0 : c0 + n], ACT.Abs_reciprocal_sqrt, bias=1.0)
-                nc.scalar.activation(r2[:, c0 : c0 + n], r[:, c0 : c0 + n], ACT.Square)
-            rec[(t, j)] = r2
 
-        def first_quarter(c0, banks):
-            n = W // 2
-            acc = psum.tile([P, n], F32, name=f"pool_q{c0}", tag=banks[0])
-            for m0 in range(0, n, P):
-                for h in range(2):
-                    c, s = eq[(h, 0)]
-                    nc.tensor.matmul_mx(
-                        out=acc[:, m0 : m0 + P],
-                        lhsT=wpw[:, h, : 2 * P].bitcast(FP4X4),
-                        lhsT_scale=wps[:, h, :P],
-                        rhs=c[:, c0 + m0 : c0 + m0 + P].bitcast(FP8X4),
-                        rhs_scale=s[:, c0 + m0 : c0 + m0 + P],
-                        start=(h == 0),
-                        stop=(h == 1),
-                    )
-            r = keep.tile([P, n], F32, name=f"r_q{c0}", tag="rA" if c0 == 0 else "rE", align_bytes=64)
-            rec[c0] = keep.tile([P, n], F32, name=f"rr_q{c0}", tag="q0" if c0 == 0 else "qE", align_bytes=64)
-            nc.scalar.activation(r[:], acc[:], ACT.Abs_reciprocal_sqrt, bias=1.0)
-            nc.scalar.activation(rec[c0][:], r[:], ACT.Square)
-            acc = psum.tile([P, n], F32, name=f"drive_q{c0}", tag=banks[1])
-            for h in range(2):
-                c, s = eq[(h, 0)]
-                wc, ws = wq[(f"d{h}", 0)]
-                nc.tensor.matmul_mx(
-                    out=acc[:],
-                    lhsT=wc,
-                    lhsT_scale=ws,
-                    rhs=c[:, c0 : c0 + n].bitcast(FP8X4),
-                    rhs_scale=s[:, c0 : c0 + n],
-                    start=(h == 0),
-                    stop=(h == 1),
-                )
-            drives[c0] = acc
+        def pool_recip(t, j0, n, bank, order, where_root, where_recip):
+            acc = psum.tile([P, n], F32, name=f"pool{t}_{j0}", tag=bank)
+            step = W if n == W else P
+            for c in range(0, n, step):
+                second_sum(acc[:, c : c + step], "p", t, j0 + c, step, order)
+            root = place([P, n], F32, f"root{t}_{j0}", where_root)
+            recips[(t, j0)] = place([P, n], F32, f"recip{t}_{j0}", where_recip)
+            nc.scalar.activation(root[:], acc[:], ACT.Abs_reciprocal_sqrt, bias=1.0)
+            nc.scalar.activation(recips[(t, j0)][:], root[:], ACT.Square)
 
-        def first_divide(c0):
-            n = W // 2
-            ys[c0] = keep.tile([P, n], F32, name=f"y_q{c0}", tag="yC" if c0 == 0 else "rB", align_bytes=64)
-            nc.vector.tensor_tensor(ys[c0][:], drives[c0][:], rec[c0][:], ALU.mult)
+        def drive(t, j0, n, bank, order):
+            drives[(t, j0)] = psum.tile([P, n], F32, name=f"drive{t}_{j0}", tag=bank)
+            second_sum(drives[(t, j0)][:], "d", t, j0, n, order)
 
-        def drive_part(t, j, bank):
-            acc = psum.tile([P, W], F32, name=f"drive{t}{j}", tag=bank)
-            order = (0, 1) if (t, j) == (0, 0) else (1, 0)
-            for h in order:
-                c, s = eq[(h, j)]
-                wc, ws = wq[(f"d{h}", t)]
-                nc.tensor.matmul_mx(
-                    out=acc[:],
-                    lhsT=wc,
-                    lhsT_scale=ws,
-                    rhs=c[:].bitcast(FP8X4),
-                    rhs_scale=s[:],
-                    start=(h == order[0]),
-                    stop=(h == order[1]),
-                )
-            drives[(t, j)] = acc
+        def divide(t, j0, n, where=None):
+            values[(t, j0)] = place([P, n], F32, f"y{t}_{j0}", where)
+            nc.vector.tensor_tensor(values[(t, j0)][:], drives[(t, j0)][:], recips[(t, j0)][:], ALU.mult)
 
-        def divide(t, j, tag, c0=0, n=W):
-            if c0 == 0:
-                ys[(t, j)] = place([P, W], F32, f"y{t}{j}", tag)
-            nc.vector.tensor_tensor(ys[(t, j)][:, c0 : c0 + n], drives[(t, j)][:, c0 : c0 + n], rec[(t, j)][:, c0 : c0 + n], ALU.mult)
+        def scatter_times_readout(t, j0, n):
+            j, c0 = divmod(j0, W)
+            window = pages[t][:].indirect(idx2[:, j0 // 16 : (j0 + n) // 16])
+            nc.vector.tensor_tensor(window, values[(t, j0)][:], readout[(t, j)][:, c0 : c0 + n], ALU.mult)
 
-        def products(t, j, tag, utag="yE", dtag=None):
-            tile, row = wg[(t, j)]
-            d = keep.tile([P, W], F32, name=f"d{t}{j}", tag=dtag or f"d{t}", align_bytes=64)
-            u = keep.tile([P, W], F32, name=f"u{t}{j}", tag=utag, align_bytes=64)
-            ys[(t, j)] = keep.tile([P, W], F32, name=f"z{t}{j}", tag=tag, align_bytes=64)
-            nc.scalar.copy(out=d[:], in_=drives[(t, j)][:])
-            nc.gpsimd.tensor_tensor(u[:], rec[(t, j)][:], tile[:, row, :], ALU.mult)
-            nc.gpsimd.tensor_tensor(ys[(t, j)][:], d[:], u[:], ALU.mult)
+        def products_on_gpsimd(t, where_drive, where_values):
+            sums = place([P, W], F32, f"sums{t}", where_drive)
+            factor = place([P, W], F32, f"factor{t}", "factor")
+            values[(t, W)] = place([P, W], F32, f"y{t}_{W}", where_values)
+            nc.scalar.copy(out=sums[:], in_=drives[(t, W)][:])
+            nc.gpsimd.tensor_tensor(factor[:], recips[(t, W)][:], readout[(t, 1)], ALU.mult)
+            nc.gpsimd.tensor_tensor(values[(t, W)][:], sums[:], factor[:], ALU.mult)
 
-        def put(t, j):
-            nc.vector.tensor_copy(pages[t][:].indirect(idx2[:, j * W // 16 : (j + 1) * W // 16]), ys[(t, j)][:])
+        def scatter_copy(t):
+            nc.vector.tensor_copy(pages[t][:].indirect(idx2[:, W // 16 :]), values[(t, W)][:])
 
-        def scatter(t, j, c0=0, n=W):
-            tile, row = wg[(t, j)]
-            nc.vector.tensor_tensor(
-                pages[t][:].indirect(idx2[:, (j * W + c0) // 16 : (j * W + c0 + n) // 16]),
-                ys[(t, j)][:] if n == W else ys[c0][:],
-                tile[:, row, c0 : c0 + n],
-                ALU.mult,
-            )
-
-        pairs = [keep.tile([P, 2, CUTS[c + 1] - CUTS[c], 2], BF16, name=f"pairs{c}") for c in range(NC - 2)]
-
-        def round_page(t, c, eng, m0=0, m1=None):
-            m1 = m1 or CUTS[c + 1] - CUTS[c]
+        def round_page(t, c, eng, m0, m1):
             copy_on(eng, pairs[c][:, t // 2, m0:m1, t % 2], pages[t][:, CUTS[c] + m0 : CUTS[c] + m1])
 
-        def finish_page(t):
+        def store_and_round(t):
             nc.sync.dma_start(out=out_rows[:, t, :], in_=pages[t][:])
-            for c in range(NC - 2 if t == 2 else NC):
-                round_page(t, c, "g" if t < 2 and c >= NC - 2 else "s", OWN if t >= 2 and c == 0 else 0)
+            for c in range(PARTS):
+                eng = "gpsimd" if t < 2 and c >= WIDE else "scalar"
+                round_page(t, c, eng, OWN if t >= 2 and c == 0 else 0, CUTS[c + 1] - CUTS[c])
 
-        def weave_y(c, eng):
-            il = keep.tile([P, 4 * (CUTS[c + 1] - CUTS[c])], BF16, name=f"yil{c}", align_bytes=64)
-            word = I32 if eng == "v" else U32
+        def weave_y(c):
+            eng, word = ("vector", I32) if c < WIDE else ("scalar", U32)
+            y_woven[c] = place([P, 4 * (CUTS[c + 1] - CUTS[c])], BF16, f"y_woven{c}")
             copy_on(
                 eng,
-                il[:].bitcast(word).rearrange("p (m u) -> p m u", u=2),
+                y_woven[c][:].bitcast(word).rearrange("p (m u) -> p m u", u=2),
                 pairs[c][:].rearrange("p u m b -> p u (m b)").bitcast(word).rearrange("p u m -> p m u"),
             )
-            yil[c] = il
 
-        def quant_y(c):
-            codes = ycodes[:, CUTS[c] : CUTS[c + 1]]
-            step = W if c == 0 else W // 2
-            for m0 in range(0, CUTS[c + 1] - CUTS[c], step):
-                g, c0 = divmod(CUTS[c] + m0, W)
+        def quantise_y(c):
+            step = W if c == 0 else Q
+            for m in range(CUTS[c], CUTS[c + 1], step):
+                g, c0 = divmod(m, W)
                 nc.vector.quantize_mx(
-                    out=codes[:, m0 : m0 + step].bitcast(FP8X4),
-                    scales=yscales[4 * g : P, c0 : c0 + step],
-                    in_=yil[c][:, 4 * m0 : 4 * (m0 + step)],
+                    out=y_codes[:, m : m + step].bitcast(FP8X4),
+                    scales=y_planes[4 * g : P, c0 : c0 + step],
+                    in_=y_woven[c][:, 4 * (m - CUTS[c]) : 4 * (m - CUTS[c] + step)],
                 )
-            if c != NC - 2:
-                first = CUTS[min(c, NC - 2)]
-                nc.sync.dma_start(out=words_out[:, first : CUTS[c + 1]], in_=ycodes[:, first : CUTS[c + 1]].bitcast(I32))
 
-        nc.vector.memset(tabs[:].bitcast(I32), 0)
-        nc.vector.memset(wps_raw[:].rearrange("p a c -> p (a c)").bitcast(I32), 0)
+        def store_codes(m0, m1):
+            nc.sync.dma_start(out=words_out[:, m0:m1], in_=y_codes[:, m0:m1].bitcast(I32))
+
+        halves = [("scalar", 0, P // 2), ("vector", P // 2, P)]
+        on_vector = [("vector", 0, P)]
+        for h in range(2):
+            for t in range(4):
+                codes = wp_codes[:, h, 2 * t * P : 2 * (t + 1) * P].bitcast(FP4X4)
+                weights[(f"p{h}", t)] = (codes, wp_planes[:, h, t * P : (t + 1) * P])
+        for c in range(WIDE):
+            pairs[c] = keep.tile([P, 2, W, 2], BF16, name=f"pairs{c}")
+
+        nc.vector.memset(tab_planes[:].bitcast(I32), 0)
+        nc.vector.memset(wp_planes_raw[:].rearrange("p a c -> p (a c)").bitcast(I32), 0)
         nc.vector.memset(tiny[:], 2.0**-100)
-        nc.sync.dma_start(out=g_sb[:], in_=gain.rearrange("(a p t) -> p a t", a=2, t=4))
-        nc.sync.dma_start(out=wpw_raw[:].bitcast(I32), in_=wp_words.rearrange("a p c -> p a c").bitcast(I32))
-        load_tabs()
+        nc.sync.dma_start(out=gains[:], in_=gain.rearrange("(a p t) -> p a t", a=2, t=4))
+        nc.sync.dma_start(out=wp_codes_raw[:].bitcast(I32), in_=wp_words.rearrange("a p c -> p a c").bitcast(I32))
+        for q in range(4):
+            nc.sync.dma_start(
+                out=tab_planes[32 * q : 32 * q + 8, :].bitcast(I32), in_=tab_scales[:, 4 * q : 4 * q + 4, :].bitcast(I32)
+            )
         nc.sync.dma_start(idx[:], offs)
-        load_w("w00", w1, 0, 0, ["R0"])
-        load_tab(0, "T0")
-        load_wps()
-        load_w("w10", w1, 1, 0, [0])
-        load_tab(1, "T1")
-        root_gain()
-        clear_page(0, "page0")
-        deal_wpw()
-        cast_w("w00", [("s", 0, 64), ("v", 64, 128)], "G0")
-        load_w("w01", w1, 0, 1, ["R0"])
-        load_w("w11", w1, 1, 1, ["R2"])
-        gather_s(0)
-        gather_s(1)
-        quant_w("w00")
-        gather_w(0, 0, 0, 512)
-        gather_w(0, 1, 0, 512)
-        deal_wps()
-        cast_w("w10", [("s", 0, 64), ("v", 64, 128)], "G1")
-        load_w("d0", wd, 0, 0, [0])
-        load_w("d1", wd, 1, 0, ["T0"])
+        load_weight("w00", w1, 0, 0, "raw_first")
+        load_table(0)
+        for q in range(4):
+            nc.sync.dma_start(
+                out=wp_planes_raw[32 * q : 32 * q + 4, :, :].bitcast(I32),
+                in_=wp_scales[:, 4 * q : 4 * q + 4, :].rearrange("a r c -> r a c").bitcast(I32),
+            )
+        load_weight("w10", w1, 1, 0, 0)
+        load_table(1)
+        root_of_gain()
+        clear_page(0, nc.vector)
+        for a in range(2):
+            nc.vector.tensor_copy(
+                out=wp_codes[:, a, :].rearrange("p (t m b) -> p t m b", t=4, b=2),
+                in_=wp_codes_raw[:, a, :].rearrange("p (m t b) -> p t m b", t=4, b=2),
+            )
+
+        round_weight("w00", halves, 0, 4, "rounded_a")
+        load_weight("w01", w1, 0, 1, "raw_first")
+        load_weight("w11", w1, 1, 1, None)
+        gather_planes(0)
+        gather_planes(1)
+        quantise_weight("w00", 0, 4, "tab_planes")
+        gather_words(0, 0, W)
+        gather_words(0, W, W)
+        nc.vector.tensor_copy(
+            out=wp_planes[:].rearrange("p a (t m) -> p a t m", t=4),
+            in_=wp_planes_raw[:].rearrange("p a (m t) -> p a t m", t=4),
+        )
+        round_weight("w10", halves, 0, 4, "rounded_b")
+        load_weight("d0", wd, 0, 0, 0)
+        load_weight("d1", wd, 1, 0, "table0")
         nc.sync.dma_start(idx2[:], offs2)
-        lin(0, 0, 0, 256, FIRST, BANKS_A)
-        lin(0, 0, 256, 256, FIRST, BANKS_B)
-        quant_w("w10")
-        gather_w(1, 0, 0, 256)
-        lin(0, 0, 0, 256, SECOND, BANKS_A)
-        gather_w(1, 0, 256, 256)
-        lin(0, 0, 256, 256, SECOND, BANKS_B)
-        gather_w(1, 1, 0, 512)
-        load_wg([(0, 0)], "T1")
-        square(0, 0, 0, 256, "E0", 0, 3)
-        square(0, 0, 256, 512, "E2", 0, 2)
-        square(0, 0, 0, 256, "E0", 3, 4)
-        square(0, 0, 256, 512, "E2", 2, 4)
-        lin(0, 1, 0, 512, BOTH[:6], BANKS_A)
-        square(0, 1, 0, 512, "E5", 0, 1)
-        weave_e(0, 0, 256, 512, "s", "L6")
-        square(0, 1, 0, 512, None, 1, 3)
-        cast_w("w01", [("v", 0, 128)], "G0")
-        weave_e(0, 0, 0, 256, "v", "L5")
-        quant_w("w01")
-        lin(1, 0, 0, 256, FIRST, BANKS_B)
-        cast_slices("w11", 0, 2, "v", "G1")
-        cast_slices("w11", 2, 4, "v", "G4")
-        quant_w("w11", 0, 2)
-        quant_w("w11", 2, 4)
-        lin(1, 0, 0, 256, SECOND, BANKS_B)
-        lin(1, 0, 256, 256, LATE, BANKS_A, 1)
-        square(1, 0, 0, 256, "E1")
-        square(1, 0, 256, 512, "E3")
-        cast_slices("d0", 0, 2, "v", "G0")
-        cast_slices("d0", 2, 4, "v", "G3")
-        quant_w("d0", 0, 2)
-        quant_e(0, 0, 0, 256, 0)
-        quant_e(0, 0, 256, 512)
-        weave_e(1, 0, 0, 256, "v", 2048)
-        quant_w("d0", 2, 4)
-        quant_e(1, 0, 0, 256)
-        weave_e(1, 0, 256, 512, "v", "L3")
-        cast_slices("d1", 0, 2, "s", "G2")
-        quant_w("d1", 0, 2)
-        quant_e(1, 0, 256, 512)
-        first_quarter(0, ["B0", "B1"])
-        first_quarter(256, ["B2", "B3"])
-        cast_slices("d1", 2, 4, "v", "G5")
-        first_divide(0)
-        quant_w("d1", 2, 4, "rA")
-        scatter(0, 0, 0, 256)
-        clear_page(1, "G5")
-        pool_part(1, 0, "A0", "rB", "q1")
-        drive_part(1, 0, "A1")
-        first_divide(256)
-        load_wg([(1, 0), (2, 0)], "q0")
-        divide(1, 0, "yB")
-        scatter(0, 0, 256, 256)
-        clear_page(2, "q1")
-        lin(0, 1, 0, 512, BOTH[6:], ["A0", "A1", "A2", "B2"])
-        pool_part(2, 0, "A2", "rC", "q2")
-        drive_part(2, 0, "A3")
-        divide(2, 0, "yA")
-        clear_page(3, "q2")
-        square(0, 1, 0, 512, None, 3, 4)
-        pool_part(3, 0, "A0", "rD", "q3")
-        lin(1, 1, 0, 512, BOTH, LATER)
-        square(1, 1, 0, 512, "E2")
-        weave_e(0, 1, 0, 512, "s", "rD")
-        load_wg([(3, 0), (0, 1), (1, 1), (2, 1), (3, 1)], "E5")
-        weave_e(1, 1, 0, 512, "s", "L4")
-        scatter(1, 0)
-        scatter(2, 0)
-        drive_part(3, 0, "B0")
-        divide(3, 0, "yF")
-        quant_e(0, 1, 0, 512)
-        quant_e(1, 1, 0, 512)
-        pool_part(0, 1, "B3", "rB", "q4")
-        scatter(3, 0)
-        pool_part(1, 1, "B0", "rB", "q5")
-        drive_part(0, 1, "A1")
-        drive_part(1, 1, "A3")
-        pool_part(2, 1, "B2", "rE", "q6")
-        pool_part(3, 1, "A2", "rC", "q3")
-        drive_part(2, 1, "A0")
-        drive_part(3, 1, "B1")
-        u = keep.tile([P, W], F32, name="u01", tag="yE", align_bytes=64)
-        ys[(0, 1)] = keep.tile([P, W], F32, name="z01", tag="yA", align_bytes=64)
-        for c0 in (0, 256):
-            nc.vector.tensor_tensor(u[:, c0 : c0 + 256], rec[(0, 1)][:, c0 : c0 + 256], wg[(0, 1)][0][:, 1, c0 : c0 + 256], ALU.mult)
-        for c0 in (0, 256):
-            nc.vector.tensor_tensor(ys[(0, 1)][:, c0 : c0 + 256], drives[(0, 1)][:, c0 : c0 + 256], u[:, c0 : c0 + 256], ALU.mult)
-        products(1, 1, "yD")
-        products(2, 1, "yB")
-        products(3, 1, "yC")
-        pairs.append(keep.tile([P, 2, 256, 2], BF16, name="pairs3", tag="d3", align_bytes=64))
-        pairs.append(keep.tile([P, 2, 256, 2], BF16, name="pairs4", tag="yE", align_bytes=64))
-        put(0, 1)
-        finish_page(0)
-        put(1, 1)
-        finish_page(1)
-        put(2, 1)
-        nc.scalar.copy(out=pairs[0][:, 1, 0:OWN, :], in_=pages[2][:, 0:OWN].unsqueeze(2).to_broadcast([P, OWN, 2]))
-        for c in (3, 4):
-            nc.gpsimd.tensor_copy(out=pairs[c][:, 1, :, :], in_=pages[2][:, CUTS[c] : CUTS[c + 1]].unsqueeze(2).to_broadcast([P, 256, 2]))
-        finish_page(2)
-        put(3, 1)
-        round_page(3, 0, "v", 0, OWN)
-        finish_page(3)
-        weave_y(0, "v")
-        weave_y(1, "v")
-        quant_y(0)
-        weave_y(2, "v")
-        quant_y(1)
-        weave_y(3, "s")
-        weave_y(4, "s")
-        quant_y(2)
-        quant_y(3)
-        quant_y(4)
+        lin(0, 0, Q, range(4), (0,), BANKS_A)
+        lin(0, Q, Q, range(4), (0,), BANKS_B)
+        quantise_weight("w10", 0, 4, "wp_planes_raw")
+        gather_words(1, 0, Q)
+        lin(0, 0, Q, range(4), (1,), BANKS_A)
+        gather_words(1, Q, Q)
+        lin(0, Q, Q, range(4), (1,), BANKS_B)
+        gather_words(1, W, W)
+        load_readout([(0, 1, 0)], "table1")
+        square(0, 0, Q, range(3))
+        square(0, Q, Q, range(2), "squares_late")
+        square(0, 0, Q, (3,))
+        square(0, Q, Q, (2, 3))
+        lin(0, W, W, range(3), (0, 1), BANKS_A)
+        square(0, W, W, (0,), "squares_ahead")
+        weave_e(0, Q, Q, "scalar")
+        square(0, W, W, (1, 2))
+
+        round_weight("w01", on_vector, 0, 4, "rounded_a")
+        weave_e(0, 0, Q, "vector")
+        quantise_weight("w01", 0, 4)
+        lin(1, 0, Q, range(4), (0,), BANKS_B)
+        round_weight("w11", on_vector, 0, 2, "rounded_b")
+        round_weight("w11", on_vector, 2, 4, None)
+        quantise_weight("w11", 0, 2)
+        quantise_weight("w11", 2, 4)
+        lin(1, 0, Q, range(4), (1,), BANKS_B)
+        lin(1, Q, Q, range(4), (1, 0), BANKS_A, 1)
+        square(1, 0, Q, range(4))
+        square(1, Q, Q, range(4))
+        round_weight("d0", on_vector, 0, 2, "rounded_a")
+        round_weight("d0", on_vector, 2, 4, None)
+        quantise_weight("d0", 0, 2)
+        quantise_e(0, 0, Q, 0)
+        quantise_e(0, Q, Q)
+        weave_e(1, 0, Q, "vector", 4 * W)
+        quantise_weight("d0", 2, 4)
+        quantise_e(1, 0, Q)
+        weave_e(1, Q, Q, "vector")
+        round_weight("d1", [("scalar", 0, P)], 0, 2, None)
+        quantise_weight("d1", 0, 2)
+        quantise_e(1, Q, Q)
+
+        for j0, banks, roots_at, recips_at in ((0, BANKS_B[:2], "root_a", "recip_a"), (Q, BANKS_B[2:], "root_b", None)):
+            pool_recip(0, j0, Q, banks[0], (0, 1), roots_at, recips_at)
+            drive(0, j0, Q, banks[1], (0, 1))
+        round_weight("d1", on_vector, 2, 4, "rounded_last")
+        divide(0, 0, Q, "values_c")
+        quantise_weight("d1", 2, 4, "root_a")
+        scatter_times_readout(0, 0, Q)
+        clear_page(1, nc.gpsimd, "rounded_last")
+        pool_recip(1, 0, W, "A0", (0, 1), "root_c", "recip_1")
+        drive(1, 0, W, "A1", (1, 0))
+        divide(0, Q, Q, "root_c")
+        load_readout([(1, 1, 0), (2, 1, 0)], "recip_a")
+        divide(1, 0, W, "values_b")
+        scatter_times_readout(0, Q, Q)
+        clear_page(2, nc.gpsimd, "recip_1")
+        lin(0, W, W, (3,), (0, 1), {3: "B2"})
+        pool_recip(2, 0, W, "A2", (1, 0), "root_d", "recip_2")
+        drive(2, 0, W, "A3", (1, 0))
+        divide(2, 0, W, "values_a")
+        clear_page(3, nc.gpsimd, "recip_2")
+        square(0, W, W, (3,))
+        pool_recip(3, 0, W, "A0", (1, 0), "root_e", "recip_3")
+        lin(1, W, W, range(4), (0, 1), ("B3", "B2", "B1", "A2"))
+        square(1, W, W, range(4), "squares_late")
+        weave_e(0, W, W, "scalar", "root_e")
+        load_readout([(3, 1, 0), (2, 2, 1), (0, 2, 1)], "squares_ahead")
+        weave_e(1, W, W, "scalar")
+        scatter_times_readout(1, 0, W)
+        scatter_times_readout(2, 0, W)
+        drive(3, 0, W, "B0", (1, 0))
+        divide(3, 0, W)
+        quantise_e(0, W, W)
+        quantise_e(1, W, W)
+        pool_recip(2, W, W, "B3", (0, 1), "root_c", None)
+        scatter_times_readout(3, 0, W)
+
+        pool_recip(0, W, W, "B0", (1, 0), "root_c", None)
+        drive(2, W, W, "A1", (1, 0))
+        drive(0, W, W, "A3", (1, 0))
+        pool_recip(1, W, W, "B2", (1, 0), "root_b", None)
+        pool_recip(3, W, W, "A2", (1, 0), "root_d", "recip_3")
+        drive(1, W, W, "A0", (1, 0))
+        drive(3, W, W, "B1", (1, 0))
+        factor = place([P, W], F32, "factor2", "factor")
+        values[(2, W)] = place([P, W], F32, f"y2_{W}", "values_a")
+        for c0 in (0, Q):
+            cols = slice(c0, c0 + Q)
+            nc.vector.tensor_tensor(factor[:, cols], recips[(2, W)][:, cols], readout[(2, 1)][:, cols], ALU.mult)
+        for c0 in (0, Q):
+            cols = slice(c0, c0 + Q)
+            nc.vector.tensor_tensor(values[(2, W)][:, cols], drives[(2, W)][:, cols], factor[:, cols], ALU.mult)
+        products_on_gpsimd(0, None, None)
+        products_on_gpsimd(1, None, "values_b")
+        scatter_copy(2)
+        round_page(2, 0, "scalar", 0, OWN)
+        products_on_gpsimd(3, "values_a", "values_c")
+        pairs[3] = place([P, 2, Q, 2], BF16, "pairs3", "values_a")
+        pairs[4] = place([P, 2, Q, 2], BF16, "pairs4", "factor")
+        store_and_round(2)
+        for t in (0, 1):
+            scatter_copy(t)
+            store_and_round(t)
+        scatter_copy(3)
+        round_page(3, 0, "vector", 0, OWN)
+        store_and_round(3)
+
+        weave_y(0)
+        for c in range(WIDE - 1):
+            weave_y(c + 1)
+            quantise_y(c)
+            store_codes(CUTS[c], CUTS[c + 1])
+        for c in range(WIDE, PARTS):
+            weave_y(c)
+        quantise_y(WIDE - 1)
+        store_codes(CUTS[WIDE - 1], CUTS[WIDE])
+        for c in range(WIDE, PARTS):
+            quantise_y(c)
+        store_codes(CUTS[WIDE], T2)
         scales_out = out_2[0].bitcast(I32).rearrange("r (g m) -> g r m", g=4)
         for q in range(4):
-            nc.sync.dma_start(out=scales_out[:, 4 * q : 4 * q + 4, :], in_=yscales[32 * q : 32 * q + 16, :].bitcast(I32))
+            nc.sync.dma_start(out=scales_out[:, 4 * q : 4 * q + 4, :], in_=y_planes[32 * q : 32 * q + 16, :].bitcast(I32))

from contextlib import ExitStack

import concourse.mybir as mybir

K, H, N, T, S, T2 = 1024, 1024, 512, 2048, 1024, 2048
FLOPS = 2 * K * H * S + 2 * 2 * H * N * S

F32 = mybir.dt.float32
BF16 = mybir.dt.bfloat16
I32 = mybir.dt.int32
U32 = mybir.dt.uint32
U16 = mybir.dt.uint16
U8 = mybir.dt.uint8
FP8X4 = mybir.dt.float8_e4m3fn_x4
FP4X4 = mybir.dt.float4_e2m1fn_x4
ACT = mybir.ActivationFunctionType
ALU = mybir.AluOpType

P = 128
W = 512
Q = 256
CUTS = (0, 512, 1024, 1536, 1792, 2048)
PARTS = len(CUTS) - 1
WIDE = 3
OWN = 384
BANKS_A = ("A0", "A1", "A2", "A3")
BANKS_B = ("B0", "B1", "B2", "B3")


def tile_list_contrast_gain_control_kernel(
    tc, tab_words, tab_scales, offs, w1, gain, wp_words, wp_scales, wd, wgo, offs2, out_0, out_1, out_2
):
    nc = tc.nc
    with ExitStack() as ctx:
        keep = ctx.enter_context(tc.tile_pool(name="keep", bufs=1))
        shared = ctx.enter_context(tc.tile_pool(name="shared", bufs=1))
        psum = ctx.enter_context(tc.psum_pool(name="psum", bufs=1))

        def place(shape, dtype, name, where=None):
            if isinstance(where, int):
                return shared.tile(shape, dtype, name=name, align_bytes=64, offset=where)
            return keep.tile(shape, dtype, name=name, tag=where or name, align_bytes=64)

        idx = keep.tile([P, S // 16], U16, name="idx")
        idx2 = keep.tile([P, S // 16], U16, name="idx2")
        tab_planes = place([P, T], U8, "tab_planes")
        wp_planes_raw = place([P, 2, N], U8, "wp_planes_raw")
        wp_codes_raw = place([P, 2, 2 * N], U8, "wp_codes_raw")
        gains = keep.tile([P, 2, 4], F32, name="gains")
        roots = keep.tile([P, 2, 4], F32, name="roots")
        tiny = keep.tile([P, 1], F32, name="tiny")
        wp_codes = place([P, 2, 2 * N], U8, "wp_codes")
        wp_planes = place([P, 2, N], U8, "wp_planes")
        y_planes = place([P, W], U8, "y_planes")
        y_codes = place([P, T2], U32, "y_codes")
        pages = {}
        tables = {}
        raws = {}
        rounded = {}
        weights = {}
        picked = {}
        picked_planes = {}
        lins = {}
        squares = {}
        woven = {}
        e_mx = {}
        recips = {}
        drives = {}
        values = {}
        readout = {}
        pairs = {}
        y_woven = {}
        wgo_rows = wgo.rearrange("(q t) j -> q t j", t=4)
        out_rows = out_0.rearrange("(p t) m -> p t m", t=4)
        words_out = out_1[0].rearrange("p m t -> p (m t)").bitcast(I32)

        def copy_on(eng, out, in_):
            if eng == "vector":
                nc.vector.tensor_copy(out=out, in_=in_)
            elif eng == "gpsimd":
                nc.gpsimd.tensor_copy(out=out, in_=in_)
            else:
                nc.scalar.copy(out=out, in_=in_)

        def clear_page(t, eng, where=None):
            pages[t] = place([P, T2], F32, f"page{t}", where)
            eng.memset(pages[t][:].bitcast(I32), 0)

        def root_of_gain():
            r, s, s2, rest, half, fix = [keep.tile([P, 2, 4], F32, name=f"newton{n}") for n in range(6)]
            nc.scalar.activation(r[:], gains[:], ACT.Abs_reciprocal_sqrt, bias=tiny[:])
            nc.gpsimd.tensor_tensor(s[:], gains[:], r[:], ALU.mult)
            nc.gpsimd.tensor_tensor(s2[:], s[:], s[:], ALU.mult)
            nc.gpsimd.tensor_tensor(rest[:], gains[:], s2[:], ALU.subtract)
            nc.gpsimd.tensor_scalar(half[:], r[:], 0.5, 0.0, ALU.mult, ALU.add)
            nc.gpsimd.tensor_tensor(fix[:], rest[:], half[:], ALU.mult)
            nc.gpsimd.tensor_tensor(roots[:], s[:], fix[:], ALU.add)

        def load_weight(key, src, a, h, where):
            raws[key] = place([P, 4, W], F32, "raw_" + key, where)
            rows = src[a * W : (a + 1) * W, h * W : (h + 1) * W]
            nc.sync.dma_start(out=raws[key][:], in_=rows.rearrange("(p i) c -> p i c", i=4))

        def load_table(a):
            tables[a] = place([P, T], I32, f"table{a}")
            nc.sync.dma_start(out=tables[a][:], in_=tab_words[a].rearrange("p n t -> p (n t)").bitcast(I32))

        def load_readout(runs, where):
            tile = place([P, sum(pages_in for t0, pages_in, j in runs), W], F32, "readout_" + where, where)
            row = 0
            for t0, pages_in, j in runs:
                for q in (0, 2, 1, 3):
                    nc.sync.dma_start(
                        out=tile[32 * q : 32 * q + 32, row : row + pages_in, :],
                        in_=wgo_rows[:, t0 : t0 + pages_in, j * W : (j + 1) * W],
                    )
                for u in range(pages_in):
                    readout[(t0 + u, j)] = tile[:, row + u, :]
                row = row + pages_in

        def round_weight(key, shares, t0, t1, where):
            tile = place([P, (t1 - t0) * W], BF16, f"rounded_{key}{t0}", where)
            out = tile[:].rearrange("p (t m i) -> p m i t", t=t1 - t0, i=4)
            in_ = raws[key][:].rearrange("p i (m t) -> p m i t", t=4)[:, :, :, t0:t1]
            for eng, m0, m1 in shares:
                copy_on(eng, out[:, m0:m1], in_[:, m0:m1])
            for t in range(t0, t1):
                rounded[(key, t)] = (tile, t0)

        def quantise_weight(key, t0, t1, where=None):
            codes = place([P, (t1 - t0) * P], U32, f"codes_{key}{t0}", where)
            plane = place([P, (t1 - t0) * P], U8, f"plane_{key}{t0}")
            tile, first = rounded[(key, t0)]
            nc.vector.quantize_mx(
                out=codes[:].bitcast(FP8X4), scales=plane[:], in_=tile[:, (t0 - first) * W : (t1 - first) * W]
            )
            for t in range(t0, t1):
                cols = slice((t - t0) * P, (t - t0 + 1) * P)
                weights[(key, t)] = (codes[:, cols].bitcast(FP8X4), plane[:, cols])

        def gather_words(a, j0, n):
            tile = place([P, n], U32, f"picked{a}_{j0}")
            nc.vector.tensor_copy(tile[:], tables[a][:].bitcast(U32).indirect(idx[:, j0 // 16 : (j0 + n) // 16]))
            for c in range(0, n, Q):
                picked[(a, j0 + c)] = (tile, c)

        def gather_planes(j):
            picked_planes[j] = place([P, W], U8, f"picked_planes{j}")
            nc.vector.tensor_copy(picked_planes[j][:], tab_planes[:].indirect(idx[:, j * W // 16 : (j + 1) * W // 16]))

        def lin(h, j0, n, slices, passes, banks, opens=0):
            j, c0 = divmod(j0, W)
            for t in slices:
                for a in passes:
                    codes, plane = weights[(f"w{a}{h}", t)]
                    words, col = picked[(a, j0)]
                    if a == opens:
                        lins[(h, j0, t)] = psum.tile([P, n], F32, name=f"lin{h}_{j0}_{t}", tag=banks[t])
                    nc.tensor.matmul_mx(
                        out=lins[(h, j0, t)][:],
                        lhsT=codes,
                        lhsT_scale=plane,
                        rhs=words[:, col : col + n].bitcast(FP8X4),
                        rhs_scale=picked_planes[j][4 * a : P, c0 : c0 + n],
                        start=(a == opens),
                        stop=(a != opens),
                    )

        def square(h, j0, n, slices, where=None):
            if (h, j0) not in squares:
                squares[(h, j0)] = place([P, 4, n], BF16, f"squares{h}_{j0}", where)
            for t in slices:
                nc.scalar.activation(squares[(h, j0)][:, t, :], lins[(h, j0, t)][:], ACT.Square, scale=roots[:, h, t : t + 1])

        def weave_e(h, j0, n, eng, where=None):
            woven[(h, j0)] = place([P, 4 * n], BF16, f"woven{h}_{j0}", where)
            copy_on(
                eng,
                woven[(h, j0)][:].rearrange("p (c i t) -> p c t i", i=4, t=4),
                squares[(h, j0)][:].rearrange("p t (c i) -> p c t i", i=4),
            )

        def quantise_e(h, j0, n, where=None):
            j, c0 = divmod(j0, W)
            if (h, j) not in e_mx:
                e_mx[(h, j)] = (place([P, W], U32, f"e_codes{h}{j}", where), place([P, W], U8, f"e_plane{h}{j}"))
            codes, plane = e_mx[(h, j)]
            nc.vector.quantize_mx(out=codes[:, c0 : c0 + n].bitcast(FP8X4), scales=plane[:, c0 : c0 + n], in_=woven[(h, j0)][:])

        def second_sum(acc, key, t, j0, n, order):
            j, c0 = divmod(j0, W)
            for h in order:
                codes, plane = weights[(f"{key}{h}", t)]
                e_codes, e_plane = e_mx[(h, j)]
                nc.tensor.matmul_mx(
                    out=acc,
                    lhsT=codes,
                    lhsT_scale=plane,
                    rhs=e_codes[:, c0 : c0 + n].bitcast(FP8X4),
                    rhs_scale=e_plane[:, c0 : c0 + n],
                    start=(h == order[0]),
                    stop=(h == order[1]),
                )

        def pool_recip(t, j0, n, bank, order, where_root, where_recip):
            acc = psum.tile([P, n], F32, name=f"pool{t}_{j0}", tag=bank)
            step = W if n == W else P
            for c in range(0, n, step):
                second_sum(acc[:, c : c + step], "p", t, j0 + c, step, order)
            root = place([P, n], F32, f"root{t}_{j0}", where_root)
            recips[(t, j0)] = place([P, n], F32, f"recip{t}_{j0}", where_recip)
            nc.scalar.activation(root[:], acc[:], ACT.Abs_reciprocal_sqrt, bias=1.0)
            nc.scalar.activation(recips[(t, j0)][:], root[:], ACT.Square)

        def drive(t, j0, n, bank, order):
            drives[(t, j0)] = psum.tile([P, n], F32, name=f"drive{t}_{j0}", tag=bank)
            second_sum(drives[(t, j0)][:], "d", t, j0, n, order)

        def divide(t, j0, n, where=None):
            values[(t, j0)] = place([P, n], F32, f"y{t}_{j0}", where)
            nc.vector.tensor_tensor(values[(t, j0)][:], drives[(t, j0)][:], recips[(t, j0)][:], ALU.mult)

        def scatter_times_readout(t, j0, n):
            j, c0 = divmod(j0, W)
            window = pages[t][:].indirect(idx2[:, j0 // 16 : (j0 + n) // 16])
            nc.vector.tensor_tensor(window, values[(t, j0)][:], readout[(t, j)][:, c0 : c0 + n], ALU.mult)

        def products_on_gpsimd(t, where_drive, where_values):
            sums = place([P, W], F32, f"sums{t}", where_drive)
            factor = place([P, W], F32, f"factor{t}", "factor")
            values[(t, W)] = place([P, W], F32, f"y{t}_{W}", where_values)
            nc.scalar.copy(out=sums[:], in_=drives[(t, W)][:])
            nc.gpsimd.tensor_tensor(factor[:], recips[(t, W)][:], readout[(t, 1)], ALU.mult)
            nc.gpsimd.tensor_tensor(values[(t, W)][:], sums[:], factor[:], ALU.mult)

        def scatter_copy(t):
            nc.vector.tensor_copy(pages[t][:].indirect(idx2[:, W // 16 :]), values[(t, W)][:])

        def round_page(t, c, eng, m0, m1):
            copy_on(eng, pairs[c][:, t // 2, m0:m1, t % 2], pages[t][:, CUTS[c] + m0 : CUTS[c] + m1])

        def store_and_round(t):
            nc.sync.dma_start(out=out_rows[:, t, :], in_=pages[t][:])
            for c in range(PARTS):
                eng = "gpsimd" if t < 2 and c >= WIDE else "scalar"
                round_page(t, c, eng, OWN if t >= 2 and c == 0 else 0, CUTS[c + 1] - CUTS[c])

        def weave_y(c):
            eng, word = ("vector", I32) if c < WIDE else ("scalar", U32)
            y_woven[c] = place([P, 4 * (CUTS[c + 1] - CUTS[c])], BF16, f"y_woven{c}")
            copy_on(
                eng,
                y_woven[c][:].bitcast(word).rearrange("p (m u) -> p m u", u=2),
                pairs[c][:].rearrange("p u m b -> p u (m b)").bitcast(word).rearrange("p u m -> p m u"),
            )

        def quantise_y(c):
            step = W if c == 0 else Q
            for m in range(CUTS[c], CUTS[c + 1], step):
                g, c0 = divmod(m, W)
                nc.vector.quantize_mx(
                    out=y_codes[:, m : m + step].bitcast(FP8X4),
                    scales=y_planes[4 * g : P, c0 : c0 + step],
                    in_=y_woven[c][:, 4 * (m - CUTS[c]) : 4 * (m - CUTS[c] + step)],
                )

        def store_codes(m0, m1):
            nc.sync.dma_start(out=words_out[:, m0:m1], in_=y_codes[:, m0:m1].bitcast(I32))

        halves = [("scalar", 0, P // 2), ("vector", P // 2, P)]
        on_vector = [("vector", 0, P)]
        for h in range(2):
            for t in range(4):
                codes = wp_codes[:, h, 2 * t * P : 2 * (t + 1) * P].bitcast(FP4X4)
                weights[(f"p{h}", t)] = (codes, wp_planes[:, h, t * P : (t + 1) * P])
        for c in range(WIDE):
            pairs[c] = keep.tile([P, 2, W, 2], BF16, name=f"pairs{c}")

        nc.vector.memset(tab_planes[:].bitcast(I32), 0)
        nc.vector.memset(wp_planes_raw[:].rearrange("p a c -> p (a c)").bitcast(I32), 0)
        nc.vector.memset(tiny[:], 2.0**-100)
        nc.sync.dma_start(out=gains[:], in_=gain.rearrange("(a p t) -> p a t", a=2, t=4))
        nc.sync.dma_start(out=wp_codes_raw[:].bitcast(I32), in_=wp_words.rearrange("a p c -> p a c").bitcast(I32))
        for q in range(4):
            nc.sync.dma_start(
                out=tab_planes[32 * q : 32 * q + 8, :].bitcast(I32), in_=tab_scales[:, 4 * q : 4 * q + 4, :].bitcast(I32)
            )
        nc.sync.dma_start(idx[:], offs)
        load_weight("w00", w1, 0, 0, "raw_first")
        load_table(0)
        for q in range(4):
            nc.sync.dma_start(
                out=wp_planes_raw[32 * q : 32 * q + 4, :, :].bitcast(I32),
                in_=wp_scales[:, 4 * q : 4 * q + 4, :].rearrange("a r c -> r a c").bitcast(I32),
            )
        load_weight("w10", w1, 1, 0, 0)
        load_table(1)
        root_of_gain()
        clear_page(0, nc.vector)
        for a in range(2):
            nc.vector.tensor_copy(
                out=wp_codes[:, a, :].rearrange("p (t m b) -> p t m b", t=4, b=2),
                in_=wp_codes_raw[:, a, :].rearrange("p (m t b) -> p t m b", t=4, b=2),
            )

        round_weight("w00", halves, 0, 4, "rounded_a")
        load_weight("w01", w1, 0, 1, "raw_first")
        load_weight("w11", w1, 1, 1, None)
        gather_planes(0)
        gather_planes(1)
        quantise_weight("w00", 0, 4, "tab_planes")
        gather_words(0, 0, W)
        gather_words(0, W, W)
        nc.vector.tensor_copy(
            out=wp_planes[:].rearrange("p a (t m) -> p a t m", t=4),
            in_=wp_planes_raw[:].rearrange("p a (m t) -> p a t m", t=4),
        )
        round_weight("w10", halves, 0, 4, "rounded_b")
        load_weight("d0", wd, 0, 0, 0)
        load_weight("d1", wd, 1, 0, "table0")
        nc.sync.dma_start(idx2[:], offs2)
        lin(0, 0, Q, range(4), (0,), BANKS_A)
        lin(0, Q, Q, range(4), (0,), BANKS_B)
        quantise_weight("w10", 0, 4, "wp_planes_raw")
        gather_words(1, 0, Q)
        lin(0, 0, Q, range(4), (1,), BANKS_A)
        gather_words(1, Q, Q)
        lin(0, Q, Q, range(4), (1,), BANKS_B)
        gather_words(1, W, W)
        load_readout([(0, 1, 0)], "table1")
        square(0, 0, Q, range(3))
        square(0, Q, Q, range(2), "squares_late")
        square(0, 0, Q, (3,))
        square(0, Q, Q, (2, 3))
        lin(0, W, W, range(3), (0, 1), BANKS_A)
        square(0, W, W, (0,), "squares_ahead")
        weave_e(0, Q, Q, "scalar")
        square(0, W, W, (1, 2))

        round_weight("w01", on_vector, 0, 4, "rounded_a")
        weave_e(0, 0, Q, "vector")
        quantise_weight("w01", 0, 4)
        lin(1, 0, Q, range(4), (0,), BANKS_B)
        round_weight("w11", on_vector, 0, 2, "rounded_b")
        round_weight("w11", on_vector, 2, 4, None)
        quantise_weight("w11", 0, 2)
        quantise_weight("w11", 2, 4)
        lin(1, 0, Q, range(4), (1,), BANKS_B)
        lin(1, Q, Q, range(4), (1, 0), BANKS_A, 1)
        square(1, 0, Q, range(4))
        square(1, Q, Q, range(4))
        round_weight("d0", on_vector, 0, 2, "rounded_a")
        round_weight("d0", on_vector, 2, 4, None)
        quantise_weight("d0", 0, 2)
        quantise_e(0, 0, Q, 0)
        quantise_e(0, Q, Q)
        weave_e(1, 0, Q, "vector", 4 * W)
        quantise_weight("d0", 2, 4)
        quantise_e(1, 0, Q)
        weave_e(1, Q, Q, "vector")
        round_weight("d1", [("scalar", 0, P)], 0, 2, None)
        quantise_weight("d1", 0, 2)
        quantise_e(1, Q, Q)

        for j0, banks, roots_at, recips_at in ((0, BANKS_B[:2], "root_a", "recip_a"), (Q, BANKS_B[2:], "root_b", None)):
            pool_recip(0, j0, Q, banks[0], (0, 1), roots_at, recips_at)
            drive(0, j0, Q, banks[1], (0, 1))
        round_weight("d1", on_vector, 2, 4, "rounded_last")
        divide(0, 0, Q, "values_c")
        quantise_weight("d1", 2, 4, "root_a")
        scatter_times_readout(0, 0, Q)
        clear_page(1, nc.gpsimd, "rounded_last")
        pool_recip(1, 0, W, "A0", (0, 1), "root_c", "recip_1")
        drive(1, 0, W, "A1", (1, 0))
        divide(0, Q, Q, "root_c")
        load_readout([(1, 1, 0), (2, 1, 0)], "recip_a")
        divide(1, 0, W, "values_b")
        scatter_times_readout(0, Q, Q)
        clear_page(2, nc.gpsimd, "recip_1")
        lin(0, W, W, (3,), (0, 1), {3: "B2"})
        pool_recip(2, 0, W, "A2", (1, 0), "root_d", "recip_2")
        drive(2, 0, W, "A3", (1, 0))
        divide(2, 0, W, "values_a")
        clear_page(3, nc.gpsimd, "recip_2")
        square(0, W, W, (3,))
        pool_recip(3, 0, W, "A0", (1, 0), "root_e", "recip_3")
        lin(1, W, W, range(4), (0, 1), ("B3", "B2", "B1", "A2"))
        square(1, W, W, range(4), "squares_late")
        weave_e(0, W, W, "scalar", "root_e")
        load_readout([(3, 1, 0), (2, 2, 1), (0, 2, 1)], "squares_ahead")
        weave_e(1, W, W, "scalar")
        scatter_times_readout(1, 0, W)
        scatter_times_readout(2, 0, W)
        drive(3, 0, W, "B0", (1, 0))
        divide(3, 0, W)
        quantise_e(0, W, W)
        quantise_e(1, W, W)
        pool_recip(2, W, W, "B3", (0, 1), "root_c", None)
        scatter_times_readout(3, 0, W)

        pool_recip(0, W, W, "B0", (1, 0), "root_c", None)
        drive(2, W, W, "A1", (1, 0))
        drive(0, W, W, "A3", (1, 0))
        pool_recip(1, W, W, "B2", (1, 0), "root_b", None)
        pool_recip(3, W, W, "A2", (1, 0), "root_d", "recip_3")
        drive(1, W, W, "A0", (1, 0))
        drive(3, W, W, "B1", (1, 0))
        factor = place([P, W], F32, "factor2", "factor")
        values[(2, W)] = place([P, W], F32, f"y2_{W}", "values_a")
        for c0 in (0, Q):
            cols = slice(c0, c0 + Q)
            nc.vector.tensor_tensor(factor[:, cols], recips[(2, W)][:, cols], readout[(2, 1)][:, cols], ALU.mult)
        for c0 in (0, Q):
            cols = slice(c0, c0 + Q)
            nc.vector.tensor_tensor(values[(2, W)][:, cols], drives[(2, W)][:, cols], factor[:, cols], ALU.mult)
        products_on_gpsimd(0, None, None)
        products_on_gpsimd(1, None, "values_b")
        scatter_copy(2)
        round_page(2, 0, "scalar", 0, OWN)
        products_on_gpsimd(3, "values_a", "values_c")
        pairs[3] = place([P, 2, Q, 2], BF16, "pairs3", "values_a")
        pairs[4] = place([P, 2, Q, 2], BF16, "pairs4", "factor")
        store_and_round(2)
        for t in (0, 1):
            scatter_copy(t)
            store_and_round(t)
        scatter_copy(3)
        round_page(3, 0, "vector", 0, OWN)
        store_and_round(3)

        weave_y(0)
        for c in range(WIDE - 1):
            weave_y(c + 1)
            quantise_y(c)
            store_codes(CUTS[c], CUTS[c + 1])
        for c in range(WIDE, PARTS):
            weave_y(c)
        quantise_y(WIDE - 1)
        store_codes(CUTS[WIDE - 1], CUTS[WIDE])
        for c in range(WIDE, PARTS):
            quantise_y(c)
        store_codes(CUTS[WIDE], T2)
        scales_out = out_2[0].bitcast(I32).rearrange("r (g m) -> g r m", g=4)
        for q in range(4):
            nc.sync.dma_start(out=scales_out[:, 4 * q : 4 * q + 4, :], in_=y_planes[32 * q : 32 * q + 16, :].bitcast(I32))
